import numpy as np, ml_dtypes
CORES = [36,164,52,180,100,228,116,244]
N = 8
import mx_ref
BF = ml_dtypes.bfloat16
def gentries(a):
    return np.ascontiguousarray(a.reshape(8, 16, -1).transpose(0, 2, 1)).reshape(8, -1)
def gtable(e):
    e = np.asarray(e); return np.ascontiguousarray(e.reshape(8, -1, 16).transpose(0, 2, 1)).reshape(128, -1).astype(np.int32)
def gcols(t, e):
    v = np.concatenate([t.reshape(8, 16, -1, 4), np.zeros((8, 16, 1, 4), BF)], axis=2)
    return np.ascontiguousarray(np.stack([v[g][:, e[g]] for g in range(8)])).reshape(128, -1)
def tile(rs):
    return np.stack(rs, axis=2).reshape(128, -1).astype(BF)
def cut(t, i, w=512):
    return t[:, w * i:w * i + w]
def pick(q, e):
    c = np.concatenate([q[0].reshape(128, -1, 4), np.zeros((128, 1, 4), np.uint8)], axis=1); s = np.concatenate([q[1], np.ones((16, 1), np.uint8)], axis=1)
    return (np.ascontiguousarray(c[:, e].reshape(128, -1)), np.ascontiguousarray(s[:, e]))
def join(*qs):
    return (np.concatenate([q[0] for q in qs], axis=1), np.concatenate([q[1] for q in qs], axis=1))
def put(q, e, v):
    c, s = q[0].reshape(128, -1, 4).copy(), q[1].copy(); c[:, e] = v[0].reshape(128, -1, 4); s[:, e] = v[1]
    return (c.reshape(128, -1), s)
def pk(c, s):
    return (np.ascontiguousarray(c), mx_ref.live(s))
def emit(q):
    return q[0], q[1]
def packed(v, rng):
    q = [mx_ref.quantize(np.ascontiguousarray(v[r])) for r in range(N)]
    return np.stack([a for a, b in q]), np.stack([mx_ref.plane(b, rng) for a, b in q])
def values_of_codes():
    e, c = np.zeros((128, 128, 4), np.float32), np.zeros((128, 2, 4), np.uint8)
    e[np.arange(128), np.arange(128), 0] = 1
    c[:127, :, 0] = np.arange(256).reshape(2, 128).T[:127]
    return mx_ref.matmul(mx_ref.quantize(e.reshape(128, 512).astype(BF)), (c.reshape(128, 8), np.full((16, 2), 127, np.uint8))).T.reshape(-1).astype(np.float64)
CODE_VALUE, SCALE_VALUE = values_of_codes(), 2.0 ** (np.arange(256) - 127.0)
def decode(q):
    return (CODE_VALUE[q[0]].reshape(16, 8, -1, 4) * SCALE_VALUE[q[1]][:, None, :, None] + 0.0).reshape(128, -1).astype(np.float32)
def f(rng, *shape):
    return mx_ref.flush((rng.standard_normal(shape, dtype=np.float32) * np.exp2(rng.integers(-2, 3, shape[:-1] + (1,)))).astype(BF))
def wide(rng, *shape, cols=0):
    v = rng.standard_normal(shape, dtype=np.float32) * np.exp2(rng.integers(-12, 13, shape)).astype(np.float32)
    if cols: v *= np.repeat(np.exp2(rng.integers(-cols, cols + 1, shape[:-2] + (1, shape[-1] // 4))) * (rng.random(shape[:-2] + (1, shape[-1] // 4)) > 0.0625), 4, axis=-1).astype(np.float32)
    return mx_ref.flush(v.astype(BF))
C, A, R = 320, 64, 3
def order(p):
    return np.argsort(-(p + np.float32(0.0)), axis=1, kind="stable")
def means(t, a, x, b):
    return ((gcols(t, a).astype(np.float32) + gcols(x, b).astype(np.float32)) * np.float32(0.5)).astype(BF)
def along(o, e):
    return np.take_along_axis(o, e, axis=1)
def big(v):
    v = v.astype(np.float32)
    v[np.abs(v) < np.float32(2.0 ** -16)] = 0
    return v.astype(BF)
def families(rng):
    return np.stack([big(f(rng, N, 128, 4 * A)) for i in range(2)])
def lists_of(rng):
    return rng.integers(0, A, (2, N, 8, C)), rng.integers(0, C, (2, N, 8, C))
def others(rng):
    k = rng.integers(0, A - 8, (2, N, 8, C))
    return k + k // 7 + 1
def layers(rng, still=()):
    w = big(f(rng, N, 128, 2048)).reshape(N, 8, 16, 4, 8, 16, 4)
    for i in still:
        w[:, :, i] = 0
        w[:, :, :, :, :, i] = 0
    return w
def made(rng, x, s, a, b, w):
    c, p = packed(np.ascontiguousarray(w).reshape(N, 128, 2048), rng)
    x, s = np.ascontiguousarray(x).reshape(N, 128, 4 * C), np.ascontiguousarray(s).reshape(2, N, 128, 4 * A)
    t = [np.stack([gtable(e) for e in k]) for k in (a[0], b[0], a[1], b[1])]
    return {"x": x, "l0": s[0], "r0": s[1], "la": t[0], "lx": t[1], "ra": t[2], "rx": t[3], "wc": c, "ws": p, "v": np.array(f(rng, N, 128, 512))}
def signs(rng):
    return np.stack([rng.permutation(8) % 2 * 2.0 - 1.0 for r in range(N)])
def setup_inputs(rng):
    a, b = lists_of(rng)
    return made(rng, big(f(rng, N, 128, 4 * C)), families(rng), a, b, layers(rng))
def setup_inputs_ties(rng):
    x = big(f(rng, N, 128, 4 * C)).reshape(N, 8, 16, C, 4)
    s = families(rng).reshape(2, N, 8, 16, A, 4)
    keep = s[:, :, :, :8, 0].copy()
    e = rng.permutation(N)
    for r in range(N):
        for t in (x[r], s[0, r], s[1, r]):
            n = t.shape[2]
            k = np.zeros(n, int) if r == e[0] else rng.permutation(n) % 3
            m = t[:, :8, :3].copy()
            m[:, :, 2] = 0
            t[:, :8] = m[:, :, k]
    x[e[1]] = 0
    s[:, :, :, :, ::8] = 0
    for h in range(8): s[:, :, h, :8, 8 * h] = keep[:, :, h]
    a, b = lists_of(rng)
    return made(rng, x, s, a, b, layers(rng, range(8)))
def setup_inputs_near(rng):
    x, s = np.zeros((N, 8, 16, C, 4)), np.zeros((2, N, 8, 16, A, 4))
    a, b = others(rng), np.zeros((2, N, 8, C), int)
    o, c = rng.permutation(N) % 4, signs(rng)
    j = np.arange(C)
    g = ((((j + 1) // 2)[:, None] >> np.arange(8)) & 1) * np.exp2(np.arange(8) - 22.0)
    for r in range(N):
        size = 1.0 if o[r] < 2 else 2.0 ** -4
        if o[r] < 2:
            x[r, :, 0, :, 0] = 2 * c[r][:, None]
            for h in rng.permutation(8)[:4]: x[r, h, 0, C - 1 if c[r, h] > 0 else 0, 0] *= 2.0 ** 29
        if o[r] == 3: x[r, :, 0, :, 0] = (8 + j % 2) * 2.0 ** -29
        x[r, :, 8] = g[:, :4] * size
        x[r, :, 9] = g[:, 4:] * size
        x[r, :, 10:] = rng.integers(4, 8, (8, 6, C, 4)) * 2.0 ** -19 * size
        s[:, r, :, 10:] = rng.integers(4, 8, (2, 8, 6, A, 4)) * 2.0 ** -19 * size
        s[:, r, :, :, ::8] = 0
        k = 1.0 if o[r] == 0 else 2.0 ** -30
        for h in range(8):
            s[:, r, h, 0, 8 * h, 0] = k
            s[:, r, h, 8:10, 8 * h] = k
        m = rng.integers(0, C, (2, 8, 1))
        b[:, r] = (j + m) % (C // 2) * 2 + j // (C // 2) if o[r] == 3 else (j + m) % C
    return made(rng, x.astype(np.float32).astype(BF), s.astype(np.float32).astype(BF), a, b, layers(rng, range(10)))
def setup_inputs_huge(rng):
    one = rng.permutation(N) < N // 2
    n = N - N // 2
    def full(*shape):
        k = 1 - 0.04 * rng.random(shape + (4,))
        k[..., ::8, :, 0] = 1
        return k
    j = np.arange(C)
    c = np.where(one[:, None] | (j >= C // 2), -1.0, 1.0)
    x = 0.6 + 0.2 * rng.random((N, 128, C, 4))
    x[~one] = full(n, 128, C)
    x *= 2.0 ** 30 * c[:, None, :, None]
    s = -(0.6 + 0.2 * rng.random((2, N, 128, A, 4)))
    s[:, ~one] = full(2, n, 128, A) * np.where(np.arange(A) < A // 2, 1.0, -1.0)[:, None]
    q = 1 - 0.25 * rng.random((2, N, 128, 8, 4))
    q[:, ~one] = full(2, n, 128, 8)
    s[:, :, :, ::8] = q * np.stack([signs(rng), signs(rng)])[:, :, None, :, None]
    s *= 2.0 ** 30
    k = (np.argsort(rng.random((2, N, 1, C)), axis=3) >= A // 2).astype(int)
    b = k * (C // 2) + rng.integers(0, C // 2, (2, N, 8, C))
    m = rng.integers(0, A // 2 - 4, (2, N, 8, C))
    a = np.where(one[:, None, None], others(rng), k * (A // 2) + m + m // 7 + 1)
    w = np.zeros((N, 128, 4, 128, 4), np.float32)
    i = np.arange(128)
    for h in range(4): w[:, i, h, i, h] = -16
    return made(rng, x.astype(np.float32).astype(BF), s.astype(np.float32).astype(BF), a, b, w.astype(BF))
def setup_inputs_lists(rng):
    def shapes(n):
        i = np.arange(C)
        k = [np.zeros(C, int), np.full(C, n - 1), i % n, n - 1 - i % n, i * n // C, rng.permutation(C) % n, rng.permutation(n)[i % 2], rng.integers(0, n, C)]
        return np.stack(k)[rng.permutation(8)]
    a, b = [np.stack([np.stack([shapes(n) for r in range(N)]) for i in range(2)]) for n in (A, C)]
    e = int(rng.integers(N))
    a[:, e] = rng.integers(0, A, (2, 8, 1))
    b[:, e] = rng.integers(0, C, (2, 8, 1))
    return made(rng, big(f(rng, N, 128, 4 * C)), families(rng), a, b, layers(rng))
def setup_inputs_spread(rng):
    a, b = lists_of(rng)
    return made(rng, big(wide(rng, N, 128, 4 * C, cols=6)), np.stack([big(wide(rng, N, 128, 4 * A)) for i in range(2)]), a, b, layers(rng))
def check_inputs(d):
    b = []
    for k in ("x", "l0", "r0", "v"):
        a = np.abs(d[k].astype(np.float32))
        if not (np.isfinite(a).all() and ((a == 0) | (a >= 2.0 ** -30) & (a <= 2.0 ** 30)).all()): b.append("a value of " + k)
    for k, n in (("la", A), ("lx", C), ("ra", A), ("rx", C)):
        if not ((d[k] >= 0) & (d[k] < n)).all(): b.append("an entry of " + k)
    if ((d["wc"] & 0x7F) == 0x7F).any(): b.append("a code of wc that is no number")
    z = np.zeros((128, 4, 4), np.float32)
    z[:, 1] = 2.0 ** -30
    z[:, 2] = 2.0 ** 30
    c, s = emit(mx_ref.quantize(z.reshape(128, 16).astype(BF)))
    for r in range(N):
        p = mx_ref.live(d["ws"][r])
        if not ((p == s[0, 0]) | (p >= s[0, 1]) & (p <= s[0, 2])).all(): b.append("a scale of ws")
    return b
def reference(x, l0, r0, la, lx, ra, rx, wc, ws, v):
    lay = [pk(wc[r], ws[r]) for r in range(N)]
    left, right = [l0[r] for r in range(N)], [r0[r] for r in range(N)]
    ol = [np.tile(A * r + np.arange(A), (8, 1)) for r in range(N)]
    og = [k.copy() for k in ol]
    for t in range(R):
        sent, pl, pg = [], [], []
        for r in range(N):
            a, c = gentries(la[r]), gentries(ra[r])
            z, w = means(left[r], a, x[r], gentries(lx[r])), means(right[r], c, x[r], gentries(rx[r]))
            q = mx_ref.quantize(np.concatenate([right[r], left[r]], axis=1))
            e = order(mx_ref.matmul(q, mx_ref.quantize(z))[:A:8])[:, :A]
            h = order(mx_ref.matmul(q, mx_ref.quantize(w))[A::8])[:, :A]
            sent.append(mx_ref.quantize(np.concatenate([gcols(z, e), gcols(w, h)], axis=1)))
            pl.append(along(along(ol[r], a), e))
            pg.append(along(along(og[r], c), h))
        came = decode(join(*sent)).astype(BF)
        for r in range(N):
            i, j = (r - 1) % N, (r + 1) % N
            got = np.concatenate([cut(came, 2 * i, 4 * A), cut(came, 2 * j + 1, 4 * A)], axis=1)
            q = mx_ref.quantize(got)
            new = tile([np.maximum(mx_ref.matmul(pick(lay[r], np.arange(128 * b, 128 * b + 128)), q), np.float32(0.0)) * np.float32(0.03125) + got[:, b::4].astype(np.float32) for b in range(4)])
            left[r], right[r] = new[:, :4 * A], new[:, 4 * A:]
            ol[r], og[r] = pl[i], pg[j]
    y, ot = np.zeros((N, 128, 2 * A), np.float32), np.zeros((N, 8, 2 * A), np.float32)
    oc, osc = np.zeros((N, 128, 8 * A), np.uint8), np.zeros((N, 16, 2 * A), np.uint8)
    for r in range(N):
        q = mx_ref.quantize(np.concatenate([left[r], right[r]], axis=1))
        y[r] = mx_ref.matmul(mx_ref.quantize(v[r]), q)
        ot[r] = np.concatenate([ol[r], og[r]], axis=1)
        oc[r], osc[r] = emit(q)
    return {"y": y, "ot": ot, "oc": oc, "osc": osc}

@@ -1,0 +1,496 @@
+from concourse.bass import DstId, RemoteDMATransfer
+from concourse.mybir import dt, AluOpType, ActivationFunctionType
+
+N, C, A, R = 8, 320, 64, 3
+BIG = 2.0 ** 90
+TILES = [[19, 18, 17], [16, 15, 14, 13], [12, 11, 10, 9], [8, 7, 6, 5], [4, 3, 2, 1], [0]]
+WIDE = [C, 272, 208, 144, 128, 128]
+AT = [sum(WIDE[:j]) for j in range(7)]
+LAST = 2
+ALONE = TILES[0] + TILES[LAST]
+REST = [j for j in range(1, 6) if j != LAST]
+OWN = [c for j in REST for c in TILES[j]]
+WHERE = {c: (j, t) for j in range(6) for t, c in enumerate(TILES[j])}
+
+SCRATCH = {}
+
+
+def sbuf(kind, **names):
+    for k, n in names.items():
+        SCRATCH[k] = ("sbuf", [128, n], kind)
+
+
+BF, F4, I4, U2, Q8, U1 = "bfloat16", "float32", "int32", "uint16", "float8_e4m3fn_x4", "uint8"
+sbuf(I4, li=80, lj=80, lk=80, pki=16, qi=4, qj=4, oi=64, oj=128)
+sbuf(U2, op=40, pk=16, off=320, ou=64 * R, on=64 * R)
+sbuf(BF, xt=4 * C, lr=512, bt=512, vt=512, et=2048, aw=1536, i8=512, zz=512, jk=4 * C, sg=4 * C)
+sbuf(Q8, vq=128, eq=512, aq=384, zc=128, wq=512, sq=128, st=256)
+sbuf(U1, vs=128, es=512, ax=384, zp=128, wp=512, sp=128, ss=256)
+sbuf(F4, rb=512, yo=128, qf=4, r16=C, r4=A, i4=C, m16=C, mb=C, rst=C, h16=C, m4=A, h4=A, olf=128, olo=64, ohi=64, osm=64, of=128, cc=20)
+SCRATCH["pd"] = ("psum", [128, 2048], F4)
+SCRATCH["pw"] = ("psum", [128, 2048], F4)
+for _f in "01":
+    sbuf(BF, **{"xg" + _f: 4 * C, "zt" + _f: 4 * C, "pl" + _f: 512, "ft" + _f: 512, "ut" + _f: 4 * AT[6]})
+    sbuf(F4, **{"ap" + _f: C, "mk" + _f: C, "sc" + _f: C, "nt" + _f: 20, "rk" + _f: 20, "rr" + _f: 20, "rs" + _f: 20, "md" + _f: C, "dd" + _f: C,
+                "inv" + _f: C, "em" + _f: A, "en" + _f: A, "gm" + _f: A, "gn" + _f: A, "oz" + _f: C})
+    sbuf(U2, **{"ro" + _f: 20, "of4" + _f: 16, "eo" + _f: 4})
+    sbuf(Q8, **{"zq" + _f: C, "uq" + _f: AT[6], "fq" + _f: 128, "pc" + _f: 128 * R, "lc" + _f: 256})
+    sbuf(U1, **{"zs" + _f: C, "us" + _f: AT[6], "fs" + _f: 128, "pp" + _f: 128 * R, "lp" + _f: 256})
+SEMAPHORES = ["sV", "sS", "sT", "sG", "ls", "dl", "d0", "dx", "dw", "dv", "dz", "dy", "do", "ao0", "ao1", "ao2"]
+SEMAPHORES += ["ar%d%d" % (_f, _r) for _f in range(2) for _r in range(R)]
+
+
+def rank_program(g, core, T, topo):
+    rank = T.rank_of(core)
+    if rank is None:
+        return
+    OP, AF = AluOpType, ActivationFunctionType
+    Q = {"V": g.vector, "S": g.scalar, "T": g.tensor, "G": g, "Y": g.sync}
+    cnt, seen, snap, lastw, readers, lastx = {"ls": 0}, {e: {} for e in Q}, {}, {}, {}, {}
+
+    def wait(e, k, n):
+        if seen[e].get(k, 0) >= n:
+            return
+        Q[e].wait_ge(T.sem[k], n)
+        seen[e][k] = n
+        for a, b in snap.get((k, n), {}).items():
+            if seen[e].get(a, 0) < b:
+                seen[e][a] = b
+
+    def need(e, rd, wr, ps=()):
+        own, want = "s" + e, {}
+        toks = [lastw[r] for r in list(rd) + list(wr) if r in lastw]
+        for w in wr:
+            toks += readers.get(w, [])
+        toks += [lastx[p] for p in ps if p in lastx and lastx[p][0] != own]
+        for k, n in toks:
+            n = cnt[k] if k[0] == "d" else n
+            want[k] = max(n, want.get(k, 0))
+        for k in sorted(want):
+            wait(e, k, want[k])
+
+    def note(tok, e, rd, wr, ps=()):
+        snap[tok] = dict(seen[e])
+        for r in rd:
+            readers.setdefault(r, []).append(tok)
+        for w in wr:
+            lastw[w], readers[w] = tok, []
+        for p in ps:
+            lastx[p] = tok
+
+    def op(e, f, rd, wr, ps=()):
+        need(e, rd, wr, ps)
+        k = "s" + e
+        cnt[k] = cnt.get(k, 0) + 1
+        f(Q[e]).then_inc(T.sem[k], 1)
+        note((k, cnt[k]), e, rd, wr, ps)
+
+    def tt(o, a, b, how, rd, wr, ps=()):
+        op("V", lambda q: q.tensor_tensor(o, a, b, how), rd, wr, ps)
+
+    def ts(o, a, s1, s2, o1, o2, rd, wr, ps=()):
+        if o2 is None:
+            op("V", lambda q: q.tensor_scalar(o, a, s1, None, o1), rd, wr, ps)
+        else:
+            op("V", lambda q: q.tensor_scalar(o, a, s1, s2, o1, o2), rd, wr, ps)
+
+    def tc(o, a, rd, wr, ps=()):
+        op("V", lambda q: q.tensor_copy(o, a), rd, wr, ps)
+
+    def fill(o, v, wr):
+        op("V", lambda q: q.memset(o, v), [], wr)
+
+    def scan(o, a, b, first, o1, o2, rd, wr):
+        op("V", lambda q: q.tensor_tensor_scan(o, a, b, first, o1, o2), rd, wr)
+
+    def quant(c, s, t, rd, wr):
+        op("V", lambda q: q.quantize_mx(c, s, t), rd, wr)
+
+    def act(o, i, func, rd, wr, ps=(), **kw):
+        op("S", lambda q: q.activation(o, i, func, **kw), rd, wr, ps)
+
+    def mm(bank, o, w, ws, x, xs, rd, start=True, stop=True):
+        op("T", lambda q: q.matmul_mx(o, w, ws, x, xs, start, stop), rd, [], [bank])
+
+    def dma(e, out, in_, rd, wr, k):
+        need(e, rd, wr)
+        cnt[k] = cnt.get(k, 0) + 16
+        Q[e].dma_start(out, in_).then_inc(T.sem[k], 16)
+        note((k, cnt[k]), e, rd, wr)
+
+    def iota(o, pattern, base, mult, wr, **kw):
+        op("G", lambda q: q.iota(o, pattern, base, mult, **kw), [], wr)
+
+    def run(*gens):
+        gens = list(gens)
+        while gens:
+            for x in list(gens):
+                if next(x, 1) is not None:
+                    gens.remove(x)
+
+    def chain(*gens):
+        for x in gens:
+            yield from x
+
+    HALF = [["b%d%d" % (h, b) for b in range(4)] for h in range(2)]
+    LI = ["li0", "li1", "li2", "li3"]
+
+    for i, nm in enumerate(("la", "lx", "ra", "rx")):
+        dma("S", T.li[:, 20 * i:20 * i + 20], T[nm][:, :], [], [LI[i]], "dl")
+    dma("Y", T.lr[:, 0:256], T.l0[:, :], [], ["lr0"], "d0")
+    dma("Y", T.lr[:, 256:512], T.r0[:, :], [], ["lr1"], "d0")
+    dma("Y", T.xt[:, :], T.x[:, :], [], ["xt"], "dx")
+    dma("Y", T.wq[:, :].bitcast(dt.uint8), T.wc[:, :], [], ["wq"], "dw")
+    dma("Y", T.wp[:, :], T.ws[:, :], [], ["wp"], "dw")
+    dma("Y", T.vt[:, :], T.v[:, :], [], ["vt"], "dv")
+
+    big = {"allow_small_or_imprecise_dtypes": True}
+    iota(T.qi[:, 3:4], [[1, 1]], 0, 1, ["qi"])
+    iota(T.pki[:, 0:8], [[8, 8]], 64, 0, ["pki"])
+    iota(T.pki[:, 8:16], [[8, 8]], 0, 0, ["pki2"])
+    iota(T.r16[:, :], [[0, 20], [1, 16]], 0, 0, ["r16"], **big)
+    iota(T.r4[:, :], [[0, 16], [1, 4]], 0, 0, ["r4"], **big)
+    iota(T.i8[:, :], [[1, 8], [0, 64]], 0, 0, ["i8"], **big)
+    val = [2 * (16 * (20 - c) - 1 - 8 * sum(a >= c for a in ALONE)) + (16 * c if c in ALONE else 0) for c in range(20)]
+    runs, c = [], 0
+    while c < 20:
+        d, e = (val[c + 1] - val[c] if c < 19 else 0), c + 1
+        while e < 20 and val[e] - val[e - 1] == d:
+            e += 1
+        runs.append("cc%d" % c)
+        iota(T.cc[:, c:e], [[d, e - c]], val[c], 0, [runs[-1]], **big)
+        c = e
+    iota(T.i4[:, :], [[4, C]], 0, 0, ["i4"], **big)
+    iota(T.olf[:, :], [[32, 2], [0, 2], [1, 32]], 0, 0, ["olf"], **big)
+    fill(T.zz[:, :], 0.0, ["zz"])
+    for b in range(4):
+        e = T.et[:, 512 * b:512 * b + 512]
+        op("G", lambda q: q.affine_select(e, T.zz[:, :], [[1, 512]], OP.not_equal, 0.5, -b, -4), ["zz"], ["et%d" % b])
+    quant(T.zc[:, :], T.zp[:, :], T.zz[:, :], ["zz"], ["zc"])
+    for f in range(2):
+        u = "%d" % f
+        dma("Y", T["lc" + u][:, 0:64].bitcast(dt.uint8), T.zc[:, 0:64].bitcast(dt.uint8), ["zc"], ["pad" + u], "dz")
+        dma("Y", T["lp" + u][:, 0:64], T.zp[:, 0:64], ["zc"], ["pae" + u], "dz")
+    tc(T.pk[:, :], T.pki[:, :], ["pki", "pki2"], ["pk"])
+    for f in range(2):
+        u = "%d" % f
+        for j in range(6):
+            z = T["ut" + u][:, 4 * (AT[j] + (16 * (TILES[j][-1] + 1) if j < 5 else 0)):4 * AT[j + 1]]
+            fill(z, 0.0, ["u%d%d%d" % (f, j, t) for t in range(4)])
+        fill(T["pl" + u][:, 256:512], 0.0, ["pz" + u])
+        fill(T["ft" + u][:, 256:512], 0.0, ["fz" + u])
+        fill(T["rk" + u][:, 0:1], 0.0, ["rk%s0" % u])
+
+    for t in range(4):
+        ts(T.off[:, 80 * t:80 * t + 80], T.li[:, :], 4.0, float(t), OP.mult, OP.add, LI, ["ot%d" % t])
+    act(T.bt[:, 0:256], T.lr[:, 0:256], AF.Copy, ["lr0"], HALF[0], scale=0.5)
+    act(T.bt[:, 256:512], T.lr[:, 256:512], AF.Copy, ["lr1"], HALF[1], scale=0.5)
+
+    def xgather(e, f, t):
+        o = T["xg%d" % f][:, C * t:C * t + C]
+        w = T.xt[:, :].indirect(T.off[:, 80 * t + 40 * f + 20:80 * t + 40 * f + 40])
+        if e == "S":
+            act(o, w, AF.Copy, ["xt", "ot%d" % t], ["xg%d%d" % (f, t)], scale=0.5)
+        else:
+            ts(o, w, 0.5, None, OP.mult, None, ["xt", "ot%d" % t], ["xg%d%d" % (f, t)])
+
+    def constants():
+        ts(T.qj[:, 0:1], T.qi[:, 3:4], 15, None, OP.bitwise_and, None, ["qi"], ["qj0"])
+        ts(T.qj[:, 1:2], T.qi[:, 3:4], 2, 3, OP.logical_shift_right, OP.bitwise_and, ["qi"], ["qj1"])
+        ts(T.qj[:, 2:3], T.qi[:, 3:4], 3, None, OP.bitwise_and, None, ["qi"], ["qj2"])
+        ts(T.qj[:, 3:4], T.qi[:, 3:4], 4, None, OP.logical_shift_right, None, ["qi"], ["qj3"])
+        tc(T.qf[:, :], T.qj[:, :], ["qj0", "qj1", "qj2", "qj3"], ["qf"])
+        ts(T.m16[:, :], T.r16[:, :], T.qf[:, 0:1], None, OP.is_equal, None, ["r16", "qf"], ["m16"])
+        ts(T.h16[:, :], T.r16[:, :], 0.0, None, OP.is_gt, None, ["r16"], ["h16"])
+        ts(T.mb[:, :], T.m16[:, :], 2 * BIG, -BIG, OP.mult, OP.add, ["m16"], ["mb"])
+        ts(T.rst[:, :], T.h16[:, :], 2 * BIG, -BIG, OP.mult, OP.add, ["h16"], ["rst"])
+        ts(T.h4[:, :], T.r4[:, :], 0.0, None, OP.is_gt, None, ["r4"], ["h4"])
+        ts(T.m4[:, :], T.r4[:, :], T.qf[:, 1:2], None, OP.is_equal, None, ["r4", "qf"], ["m4"])
+        ts(T.aw[:, 512:1024], T.i8[:, :], T.qf[:, 3:4], -2.0, OP.is_equal, OP.mult, ["i8", "qf"], ["aw1"])
+
+    def constants2():
+        act(T.aw[:, 0:512], T.aw[:, 512:1024], AF.Copy, ["aw1"], ["aw0"], scale=0.5)
+        act(T.aw[:, 3:512:4], T.aw[:, 515:1024:4], AF.Copy, ["aw1"], ["aw0"], scale=-1.0)
+        act(T.aw[:, 1024:1536], T.aw[:, 512:1024], AF.Copy, ["aw1"], ["aw2"], scale=0.5)
+
+    def constants3():
+        quant(T.aq[:, :], T.ax[:, :], T.aw[:, :], ["aw0", "aw1", "aw2"], ["aq"])
+        yield
+        ts(T.lj[:, :], T.li[:, :], 32.0, 32.0, OP.is_ge, OP.mult, LI, ["lj"])
+        yield
+        tt(T.lk[:, :], T.lj[:, :], T.li[:, :], OP.add, ["lj"] + LI, ["lk"])
+        yield
+        tc(T.op[:, 0:20], T.lk[:, 0:20], ["lk"], ["op0"])
+        ts(T.op[:, 20:40], T.lk[:, 40:60], 32.0, None, OP.add, None, ["lk"], ["op1"])
+
+    def picks(f):
+        s, k = slice(128 * f, 128 * f + 128), T.pk[:, 8 * f:8 * f + 8]
+        tc(T.st[:, s].bitcast(dt.uint32), T.sq[:, 0:128].bitcast(dt.uint32).indirect(k), ["sq", "pk"], ["st%d" % f])
+        act(T.ss[:, s], T.sp[:, 0:128].indirect(k), AF.Copy, ["sq", "pk"], ["ss%d" % f])
+
+    def cand(f, quarters):
+        for t in quarters:
+            w = T.bt[:, 256 * f:256 * f + 256].indirect(T.off[:, 80 * t + 40 * f:80 * t + 40 * f + 20])
+            tt(T["zt%d" % f][:, t:4 * C:4], w, T["xg%d" % f][:, C * t:C * t + C], OP.add, HALF[f] + ["ot%d" % t, "xg%d%d" % (f, t)], ["zt%d%d" % (f, t)])
+            yield
+
+    def zquant(f):
+        u = "%d" % f
+        quant(T["zq" + u][:, :], T["zs" + u][:, :], T["zt" + u][:, :], ["zt" + u + "%d" % t for t in range(4)], ["zq" + u])
+        yield
+
+    def score(f):
+        u = "%d" % f
+        s, k = slice(128 * f, 128 * f + 128), T.pw[:, 512 * f:512 * f + C]
+        mm("pw" + u, k, T.st[:, s], T.ss[:, s], T["zq" + u][:, :], T["zs" + u][:, :], ["st" + u, "ss" + u, "zq" + u])
+
+    def plain(f):
+        act(T["ap%d" % f][:, :], T.pw[:, 512 * f:512 * f + C], AF.Copy, [], ["ap%d" % f], ["pw%d" % f])
+
+    def slot(f, c, a, b):
+        j, t = WHERE[c]
+        return T["ut%d" % f][:, 4 * (AT[j] + a) + t:4 * (AT[j] + b):4], ["u%d%d%d" % (f, j, t)]
+
+    def prep(f):
+        u = "%d" % f
+        k = T.pw[:, 512 * f:512 * f + C]
+        tt(T["mk" + u][:, :], k, T.mb[:, :], OP.min, ["mb"], ["mk" + u], ["pw" + u])
+        yield
+        scan(T["sc" + u][:, :], T.rst[:, :], T["mk" + u][:, :], -BIG, OP.min, OP.max, ["rst", "mk" + u], ["sc" + u])
+        act(T["nt" + u][:, :], T["sc" + u][:, 15:C:16], AF.Copy, ["sc" + u], ["nt" + u], scale=-1.0)
+        yield
+        tt(T["ut" + u][:, 3:4 * C:4], k, T["sc" + u][:, :], OP.is_equal, ["sc" + u], ["u%d03" % f], ["pw" + u])
+        yield
+
+    turn = [0, 0]
+
+    def alone(f, cs):
+        u = "%d" % f
+
+        def second(c, sg):
+            w = 16 * c
+            o, n = slot(f, c, 0, w)
+            act(o, T.sg[:, C * sg:C * sg + w], AF.Sign, ["sg%d" % sg], n + ["rk%s%d" % (u, c)], bias=0.5, accum_out=T["rk" + u][:, c:c + 1])
+            o, n = slot(f, c, w, w + 16)
+            act(o, T.sg[:, C * sg + w:C * sg + w + 16], AF.Sign, ["sg%d" % sg], ["own%s%d" % (u, c)], bias=0.5)
+        last = None
+        for c in cs:
+            sg, turn[0] = turn[0] % 4, turn[0] + 1
+            act(T.sg[:, C * sg:C * sg + 16 * c + 16], T["ap" + u][:, 0:16 * c + 16], AF.Sign, ["ap" + u, "nt" + u], ["sg%d" % sg], bias=T["nt" + u][:, c:c + 1])
+            if last:
+                second(*last)
+            last = (c, sg)
+        second(*last)
+
+    def compare(f, cs):
+        u = "%d" % f
+        for c in cs:
+            o, n = slot(f, c, 0, 16 * c + 16)
+            ts(o, T["ap" + u][:, 0:16 * c + 16], T["sc" + u][:, 16 * c + 15:16 * c + 16], None, OP.is_ge, None, ["ap" + u, "sc" + u], n)
+            yield
+
+    def addup(f):
+        for c in OWN:
+            if c:
+                o, n = slot(f, c, 0, 16 * c)
+                jk, turn[1] = turn[1] % 4, turn[1] + 1
+                act(T.jk[:, C * jk:C * jk + 16 * c], o, AF.Copy, n, ["jk%d" % jk, "rk%d%d" % (f, c)], scale=2.0, accum_out=T["rk%d" % f][:, c:c + 1])
+
+    def down(f, j):
+        u = "%d" % f
+        s = slice(AT[j], AT[j + 1])
+        quant(T["uq" + u][:, s], T["us" + u][:, s], T["ut" + u][:, 4 * AT[j]:4 * AT[j + 1]],
+              ["u%d%d%d" % (f, j, t) for t in range(4)] + ["own%s%d" % (u, c) for c in TILES[j]], ["uq%s%d" % (u, j)])
+        b, w = 2 + f, 0 if j == 0 else 256 if j == LAST else 128
+        mm("pw%d" % b, T.pw[:, 512 * b:512 * b + WIDE[j]], T.aq[:, w:w + 128], T.ax[:, w:w + 128], T["uq" + u][:, s], T["us" + u][:, s],
+           ["aq", "uq%s%d" % (u, j)], j == 0, j == LAST)
+        yield
+
+    def survive(f, r):
+        u = "%d" % f
+        n = "%d%d" % (f, r)
+        b = 2 + f
+        tt(T["md" + u][:, :], T.pw[:, 512 * b:512 * b + C], T.m16[:, :], OP.mult, ["m16"], ["md" + u], ["pw%d" % b])
+        yield
+        scan(T["dd" + u][:, :], T.h16[:, :], T["md" + u][:, :], 0.0, OP.mult, OP.add, ["h16", "md" + u], ["dd" + u])
+        yield
+        tt(T["rr" + u][:, :], T["rk" + u][:, :], T.cc[:, :], OP.add, ["rk%d%d" % (f, c) for c in range(20)] + runs, ["rr" + u])
+        yield
+        tt(T["rs" + u][:, :], T["rr" + u][:, :], T["dd" + u][:, 15:C:16], OP.add, ["rr" + u, "dd" + u], ["rs" + u])
+        yield
+        ts(T["ro" + u][:, :], T["rs" + u][:, :], 0.5, None, OP.mult, None, ["rs" + u], ["ro" + u])
+        yield
+        tc(T["inv" + u][:, :].indirect(T["ro" + u][:, 0:20]), T.i4[:, :], ["ro" + u, "i4"], ["inv" + u])
+        yield
+        tt(T["gm" + u][:, :], T["inv" + u][:, 0:A], T.m4[:, :], OP.mult, ["inv" + u, "m4"], ["gm" + u])
+        yield
+        scan(T["gn" + u][:, :], T.h4[:, :], T["gm" + u][:, :], 0.0, OP.mult, OP.add, ["gm" + u, "h4"], ["gn" + u])
+        yield
+        ts(T["of4" + u][:, :], T["gn" + u][:, 3:A:4], T.qf[:, 2:3], None, OP.add, None, ["gn" + u, "qf"], ["of4" + u])
+        yield
+        tc(T["pl" + u][:, 0:256], T["zt" + u][:, :].indirect(T["of4" + u][:, 0:16]), ["of4" + u] + ["zt" + u + "%d" % t for t in range(4)], ["pl" + u])
+        yield
+        v = slice(128 * r, 128 * r + 128)
+        quant(T["pc" + u][:, v], T["pp" + u][:, v], T["pl" + u][:, :], ["pl" + u, "pz" + u], ["pc" + n])
+        d = T.cores[(rank + 1 - 2 * f) % N]
+        rid, pid = topo.addr(d, core)
+        m, ne = topo.mask(core, d), len(topo.engines(core, d))
+        s, v, k = slice(64 * r + 64, 64 * r + 128), slice(128 * r, 128 * r + 64), "ar" + n
+        need("G", ["pc" + n], [])
+        g.remote_dma(T["lc" + u][:, s].bitcast(dt.uint8), T["pc" + u][:, v].bitcast(dt.uint8), T.sem[k], T.sem.ls, pid, rid, m)
+        g.remote_dma(T["lp" + u][:, s], T["pp" + u][:, v], T.sem[k], T.sem.ls, pid, rid, m)
+        cnt["ls"] += 2 * ne
+        cnt[k] = 2 * ne
+        yield
+
+    def places(f):
+        u = "%d" % f
+        tt(T["em" + u][:, :], T["inv" + u][:, 0:A], T.m16[:, 0:A], OP.mult, ["inv" + u, "m16"], ["em" + u])
+        yield
+        scan(T["en" + u][:, :], T.h16[:, 0:A], T["em" + u][:, :], 0.0, OP.mult, OP.add, ["em" + u, "h16"], ["en" + u])
+        yield
+        ts(T["eo" + u][:, :], T["en" + u][:, 15:A:16], 0.25, None, OP.mult, None, ["en" + u], ["eo" + u])
+        s = slice(32 * f, 32 * f + 32)
+        act(T.olo[:, s], T["oz" + u][:, :].indirect(T["eo" + u][:, 0:2]), AF.Copy, ["oz" + u, "eo" + u], ["olo" + u])
+        act(T.ohi[:, s], T["oz" + u][:, :].indirect(T["eo" + u][:, 2:4]), AF.Copy, ["oz" + u, "eo" + u], ["ohi" + u], scale=64.0)
+        yield
+
+    def origins(f):
+        act(T["oz%d" % f][:, :], T.olf[:, :].indirect(T.op[:, 20 * f:20 * f + 20]), AF.Copy, ["olf", "op%d" % f], ["oz%d" % f])
+
+    def origins_out(r):
+        n = "%d" % r
+        tt(T.osm[:, :], T.olo[:, :], T.ohi[:, :], OP.add, ["olo0", "olo1", "ohi0", "ohi1"], ["osm"])
+        yield
+        tc(T.ou[:, 64 * r:64 * r + 64], T.osm[:, :], ["osm"], ["ou" + n])
+        need("G", ["ou" + n], [])
+        tr = []
+        for f in range(2):
+            d = T.cores[(rank + 1 - 2 * f) % N]
+            rid, pid = topo.addr(d, core)
+            en = topo.engines(core, d)
+            h, s = len(en) // 2, slice(64 * r + 32 * f, 64 * r + 32 * f + 32)
+            tr.append(RemoteDMATransfer(dst_ids=[DstId(rid=rid, pnc=pid)], dma_engine_mask=sum(1 << e for e in en[h * f:h * f + h]),
+                                        remote_sem=T.sem["ao" + n], src=T.ou[:, s], dst=T.on[:, s]))
+            cnt["ls"] += h
+            cnt["ao" + n] = cnt.get("ao" + n, 0) + h
+        g.remote_dma_fused(tr, local_sem=T.sem.ls)
+        yield
+
+    def origins_in(r, last):
+        n = "%d" % r
+        lastw["on" + n] = ("ao" + n, cnt["ao" + n])
+        tc(T.oi[:, :], T.on[:, 64 * r:64 * r + 64], ["on" + n], ["oi"])
+        yield
+        ts(T.oj[:, 0:64], T.oi[:, :], 63, None, OP.bitwise_and, None, ["oi"], ["oj0"])
+        ts(T.oj[:, 64:128], T.oi[:, :], 6, None, OP.logical_shift_right, None, ["oi"], ["oj1"])
+        yield
+        if not last:
+            tc(T.olf[:, :], T.oj[:, :], ["oj0", "oj1"], ["olf"])
+            return
+        for f in range(2):
+            base = float(A * ((rank - R + 2 * R * f) % N))
+            for h in range(2):
+                o, i = 64 * f + 32 * h, 64 * h + 32 * f
+                ts(T.of[:, o:o + 32], T.oj[:, i:i + 32], base, None, OP.add, None, ["oj%d" % h], ["of%d%d" % (f, h)])
+        dma("Y", T.ot[:, :], T.of[0:128:16, :], ["of00", "of01", "of10", "of11"], [], "do")
+
+    def renew(h, r):
+        last, u = r == R - 1, "%d" % h
+        n = "%d%d" % (h, r)
+        lastw["lc" + n] = ("ar" + n, cnt["ar" + n])
+        W = [slice(128 * b, 128 * b + 128) for b in range(4)]
+        P = [slice(512 * b, 512 * b + 128) for b in range(4)]
+        D = [slice(512 * b + 64, 512 * b + 128) for b in range(4)]
+        K = [slice(512 * b, 512 * b + 64) for b in range(4)]
+        B = [slice(64 * b + 256 * h, 64 * b + 256 * h + 64) for b in range(4)]
+        x, ft = slice(64 * r, 64 * r + 128), T["ft" + u]
+        two = 2.0 if last else 1.0
+        for b in range(4):
+            mm("pd%d" % b, T.pd[:, P[b]], T.eq[:, W[b]], T.es[:, W[b]], T["lc" + u][:, x], T["lp" + u][:, x], ["lc" + n, "eq", "pad" + u, "pae" + u])
+        for b in range(4):
+            o, i = ft[:, b:256:4], T.pd[:, D[b]]
+            if b % 2:
+                act(o, i, AF.Copy, [], ["ft%s%d" % (u, b)], ["pd%d" % b], scale=two)
+            else:
+                ts(o, i, two, None, OP.mult, None, [], ["ft%s%d" % (u, b)], ["pd%d" % b])
+                yield
+        quant(T["fq" + u][:, :], T["fs" + u][:, :], ft[:, :], ["ft%s%d" % (u, b) for b in range(4)] + ["fz" + u], ["fq" + u])
+        yield
+        for b in range(4):
+            mm("pw%d" % b, T.pw[:, P[b]], T.wq[:, W[b]], T.wp[:, W[b]], T["fq" + u][:, :], T["fs" + u][:, :], ["wq", "wp", "fq" + u])
+        for b in range(4):
+            act(T.rb[:, B[b]], T.pw[:, K[b]], AF.Relu, [], ["rb%s%d" % (u, b)], ["pw%d" % b], scale=0.03125)
+        for b in range(4):
+            o, i = T.bt[:, 256 * h + b:256 * h + 256:4], T.rb[:, B[b]]
+            if last:
+                tt(o, i, ft[:, b:256:4], OP.add, ["rb%s%d" % (u, b), "ft%s%d" % (u, b)], ["b%s%d" % (u, b)])
+            else:
+                tt(o, i, T.pd[:, D[b]], OP.add, ["rb%s%d" % (u, b)], ["b%s%d" % (u, b)], ["pd%d" % b])
+            yield
+
+    for r in range(R):
+        if r == 0:
+            constants()
+            for t in range(4):
+                xgather("S" if t < 2 else "V", 0, t)
+        quant(T.sq[:, :], T.sp[:, :], T.bt[:, :], HALF[0] + HALF[1], ["sq"])
+        picks(0)
+        if r == 0:
+            constants2()
+            for t in range(4):
+                xgather("S", 1, t)
+            run(cand(0, (2, 3, 0, 1)))
+            run(zquant(0), constants3())
+        score(0)
+        plain(0)
+        picks(1)
+        run(cand(1, (0, 1)))
+        run(prep(0), cand(1, (2, 3)))
+        alone(0, TILES[0])
+        run(zquant(1))
+        score(1)
+        z, p = compare(0, OWN), prep(1)
+        next(z)
+        next(p)
+        plain(1)
+        alone(0, TILES[LAST])
+        next(z)
+        next(p)
+        run(z)
+        run(p)
+        addup(0)
+        alone(1, TILES[0])
+        downs = [down(0, j) for j in [0] + REST]
+        if r:
+            downs.insert(0, origins_in(r - 1, False))
+        run(*downs)
+        run(down(0, LAST))
+        alone(1, TILES[LAST])
+        run(survive(0, r), compare(1, OWN))
+        addup(1)
+        for j in [0] + REST + [LAST]:
+            run(down(1, j))
+        origins(0)
+        origins(1)
+        run(survive(1, r), places(0))
+        if r == 0:
+            quant(T.eq[:, :], T.es[:, :], T.et[:, :], ["et%d" % b for b in range(4)], ["eq"])
+        run(renew(0, r), chain(places(1), origins_out(r)))
+        if r == 0:
+            quant(T.vq[:, :], T.vs[:, :], T.vt[:, :], ["vt"], ["vq"])
+        if r < R - 1:
+            run(cand(0, (0, 1, 2, 3)))
+            run(zquant(0))
+        run(renew(1, r))
+
+    quant(T.sq[:, :], T.sp[:, :], T.bt[:, :], HALF[0] + HALF[1], ["sq"])
+    dma("Y", T.oc[:, :], T.sq[:, :].bitcast(dt.uint8), ["sq"], [], "do")
+    mm("pw0", T.pw[:, 0:128], T.vq[:, :], T.vs[:, :], T.sq[:, :], T.sp[:, :], ["vq", "sq"])
+    act(T.yo[:, :], T.pw[:, 0:128], AF.Copy, [], ["yo"], ["pw0"])
+    dma("S", T.y[:, :], T.yo[:, :], ["yo"], [], "dy")
+    for k in range(4):
+        dma("Y", T.osc[4 * k:4 * k + 4, :], T.sp[32 * k:32 * k + 4, :], ["sq"], [], "do")
+    run(origins_in(R - 1, True))
+    for k in sorted(cnt):
+        wait("G", k, cnt[k])

@@ -3,14 +3,18 @@ from concourse.mybir import dt, AluOpType, ActivationFunctionType
 
 N, C, A, R = 8, 320, 64, 3
 BIG = 2.0 ** 90
+B = 1536
 TILES = [[19, 18, 17], [16, 15, 14, 13], [12, 11, 10, 9], [8, 7, 6, 5], [4, 3, 2, 1], [0]]
 WIDE = [C, 272, 208, 144, 128, 128]
 AT = [sum(WIDE[:j]) for j in range(7)]
-LAST = 2
-ALONE = TILES[0] + TILES[LAST]
-REST = [j for j in range(1, 6) if j != LAST]
-OWN = [c for j in REST for c in TILES[j]]
+ALONE = [[19, 18, 17, 16, 15], [19, 18, 17, 16, 15]]
+QUANT = [[0], [1, 2], [3, 4, 5]]
 WHERE = {c: (j, t) for j in range(6) for t, c in enumerate(TILES[j])}
+BANKS = [[0, 1, 4, 6], [2, 3, 5, 7]]
+FIXED = {"V": 35, "S": 70, "T": 10, "G": 170, "Y": 70}
+GATHER, SCATTER, SIGNAL, LOCAL, REMOTE, HOLD = 1.5, 3.5, 50, 1400, 2200, 60
+
+TURNS = ["sides", "cand0", "score0", "cand1", "score1", "rank0", "tail0", "rank1", "tail1", "renew0", "renew1", "parents"]
 
 SCRATCH = {}
 
@@ -21,23 +25,46 @@ def sbuf(kind, **names):
 
 
 BF, F4, I4, U2, Q8, U1 = "bfloat16", "float32", "int32", "uint16", "float8_e4m3fn_x4", "uint8"
-sbuf(I4, li=80, lj=80, lk=80, pki=16, qi=4, qj=4, oi=64, oj=128)
-sbuf(U2, op=40, pk=16, off=320, ou=64 * R, on=64 * R)
-sbuf(BF, xt=4 * C, lr=512, bt=512, vt=512, et=2048, aw=1536, i8=512, zz=512, jk=4 * C, sg=4 * C)
-sbuf(Q8, vq=128, eq=512, aq=384, zc=128, wq=512, sq=128, st=256)
-sbuf(U1, vs=128, es=512, ax=384, zp=128, wp=512, sp=128, ss=256)
-sbuf(F4, rb=512, yo=128, qf=4, r16=C, r4=A, i4=C, m16=C, mb=C, rst=C, h16=C, m4=A, h4=A, olf=128, olo=64, ohi=64, osm=64, of=128, cc=20)
-SCRATCH["pd"] = ("psum", [128, 2048], F4)
-SCRATCH["pw"] = ("psum", [128, 2048], F4)
+sbuf(I4, li=80, pki=16, qi=4, qj=4, oi=24, oj=24)
+sbuf(U2, pk=16, off=320, ox=24)
+sbuf(BF, xt=4 * C, lr=512, bt=512, vt=512, et=2048, a1=512, aw=512, zz=512, r16=C, mb=C, rs=C)
+sbuf(Q8, vq=128, eq=512, aq=128, zc=128, wq=512, sq=128, st=256)
+sbuf(U1, vs=128, es=512, ax=128, zp=128, wp=512, sp=128, ss=256)
+sbuf(F4, yo=128, cf=8, yy=C, y4=A, i4=C, wj=256, d1=C, d4=A, ou=24, on=24, oa=128, ob=128, of=128)
+SCRATCH["ps"] = ("psum", [128, 4096], F4)
 for _f in "01":
-    sbuf(BF, **{"xg" + _f: 4 * C, "zt" + _f: 4 * C, "pl" + _f: 512, "ft" + _f: 512, "ut" + _f: 4 * AT[6]})
-    sbuf(F4, **{"ap" + _f: C, "mk" + _f: C, "sc" + _f: C, "nt" + _f: 20, "rk" + _f: 20, "rr" + _f: 20, "rs" + _f: 20, "md" + _f: C, "dd" + _f: C,
-                "inv" + _f: C, "em" + _f: A, "en" + _f: A, "gm" + _f: A, "gn" + _f: A, "oz" + _f: C})
-    sbuf(U2, **{"ro" + _f: 20, "of4" + _f: 16, "eo" + _f: 4})
+    sbuf(BF, **{"xg" + _f: 4 * C, "zt" + _f: 4 * C, "pl" + _f: 512, "ft" + _f: 512, "fh" + _f: 256, "ut" + _f: 4 * AT[6], "jk" + _f: 20 * C, "sg" + _f: 10 * C})
+    sbuf(F4, **{"mk" + _f: C, "sc" + _f: C, "rk" + _f: 20, "rr" + _f: 20, "dd" + _f: C, "vv" + _f: C, "inv" + _f: C, "gn" + _f: A, "en" + _f: A})
+    sbuf(U2, **{"ro" + _f: 20, "of4" + _f: 16})
     sbuf(Q8, **{"zq" + _f: C, "uq" + _f: AT[6], "fq" + _f: 128, "pc" + _f: 128 * R, "lc" + _f: 256})
     sbuf(U1, **{"zs" + _f: C, "us" + _f: AT[6], "fs" + _f: 128, "pp" + _f: 128 * R, "lp" + _f: 256})
-SEMAPHORES = ["sV", "sS", "sT", "sG", "ls", "dl", "d0", "dx", "dw", "dv", "dz", "dy", "do", "ao0", "ao1", "ao2"]
+SEMAPHORES = ["sV", "sS", "sT", "sG", "ls", "dl", "d0", "dx", "dw", "dv", "dz", "du", "dy", "do", "ao0", "ao1"]
 SEMAPHORES += ["ar%d%d" % (_f, _r) for _f in range(2) for _r in range(R)]
+
+
+def arrange(calls):
+    after = [[] for _ in calls]
+    for i, c in enumerate(calls):
+        for d in c["deps"] | c["behind"]:
+            after[d].append(i)
+    left = [len(c["deps"] | c["behind"]) for c in calls]
+    ready, free, order = [0.0] * len(calls), {e: 0.0 for e in FIXED}, []
+    todo = {i for i in range(len(calls)) if not left[i]}
+    while todo:
+        first = min(todo, key=lambda i: (max(ready[i], free[calls[i]["e"]]), i))
+        e = calls[first]["e"]
+        now = max(ready[first], free[e])
+        i = min([j for j in todo if calls[j]["e"] == e and ready[j] <= now + HOLD], key=lambda j: (calls[j]["turn"], j))
+        todo.remove(i)
+        order.append(i)
+        start = max(now, ready[i])
+        free[e] = start + calls[i]["busy"]
+        for j in after[i]:
+            ready[j] = max(ready[j], free[e] + calls[i]["late"] + SIGNAL if i in calls[j]["deps"] else start)
+            left[j] -= 1
+            if not left[j]:
+                todo.add(j)
+    return order
 
 
 def rank_program(g, core, T, topo):
@@ -46,7 +73,321 @@ def rank_program(g, core, T, topo):
         return
     OP, AF = AluOpType, ActivationFunctionType
     Q = {"V": g.vector, "S": g.scalar, "T": g.tensor, "G": g, "Y": g.sync}
-    cnt, seen, snap, lastw, readers, lastx = {"ls": 0}, {e: {} for e in Q}, {}, {}, {}, {}
+    calls, lastw, readers, bank, group, turn = [], {}, {}, {}, {}, [0]
+
+    def call(e, f, rd, wr, ps, busy, late=0.0, sem=None):
+        i = len(calls)
+        deps = {lastw[r] for r in list(rd) + list(wr) if r in lastw}
+        for w in wr:
+            deps |= set(readers.get(w, []))
+        behind = set()
+        for p in ps:
+            for j in bank.get(p, []):
+                if calls[j]["e"] != e:
+                    deps.add(j)
+                elif e == "T":
+                    behind.add(j)
+            bank[p] = [i] if e == "T" else bank.get(p, []) + [i]
+        for j in list(deps):
+            if calls[j]["sem"] and calls[j]["sem"] != sem:
+                deps |= set(group[calls[j]["sem"]])
+        if e == "Y" and "Y" in lastw:
+            behind.add(lastw["Y"])
+        lastw[e] = i
+        for r in rd:
+            readers.setdefault(r, []).append(i)
+        for w in wr:
+            lastw[w], readers[w] = i, []
+        if sem:
+            group.setdefault(sem, []).append(i)
+        calls.append({"e": e, "f": f, "deps": deps, "behind": behind - deps, "busy": FIXED[e] + busy, "late": late, "sem": sem, "turn": turn[0]})
+
+    def vec(n, f, rd, wr, ps):
+        call("V", f, rd, wr, ps, max(64, n))
+
+    def tt(n, o, a, b, how, rd, wr, ps=()):
+        vec(n, lambda q: q.tensor_tensor(o, a, b, how), rd, wr, ps)
+
+    def ts(n, o, a, s1, s2, o1, o2, rd, wr, ps=()):
+        if o2 is None:
+            vec(n, lambda q: q.tensor_scalar(o, a, s1, None, o1), rd, wr, ps)
+        else:
+            vec(n, lambda q: q.tensor_scalar(o, a, s1, s2, o1, o2), rd, wr, ps)
+
+    def tc(n, o, a, rd, wr):
+        vec(n, lambda q: q.tensor_copy(o, a), rd, wr, ())
+
+    def fill(n, o, v, wr):
+        vec(n, lambda q: q.memset(o, v), [], wr, ())
+
+    def scan(n, o, a, b, first, o1, o2, rd, wr, ps=()):
+        vec(n, lambda q: q.tensor_tensor_scan(o, a, b, first, o1, o2), rd, wr, ps)
+
+    def quant(n, c, s, t, rd, wr):
+        vec(1.06 * n + 14, lambda q: q.quantize_mx(c, s, t), rd, wr, ())
+
+    def act(n, o, i, func, rd, wr, ps=(), **kw):
+        call("S", lambda q: q.activation(o, i, func, **kw), rd, wr, ps, n + (24 if "accum_out" in kw else 0))
+
+    def mm(b, n, w, ws, x, xs, rd, start=True, stop=True):
+        call("T", lambda q: q.matmul_mx(T.ps[:, 512 * b:512 * b + n], w, ws, x, xs, start, stop), rd, [], [b], 0.7 * n, 30)
+
+    def dma(e, n, out, in_, rd, wr, k):
+        call(e, lambda q: q.dma_start(out, in_), rd, wr, (), 0, LOCAL + n, k)
+
+    def iota(n, o, pattern, base, mult, wr, **kw):
+        call("G", lambda q: q.iota(o, pattern, base, mult, **kw), [], wr, (), 2 * n)
+
+    def select(o, i, pattern, how, other, base, mult, rd, wr):
+        call("G", lambda q: q.affine_select(o, i, pattern, how, other, base, mult), rd, wr, (), 1024)
+
+    def at(r, name):
+        turn[0] = len(TURNS) * (r + 1) + TURNS.index(name)
+
+    def psum(b, lo, hi):
+        return T.ps[:, 512 * b + lo:512 * b + hi]
+
+    HALF = [["b%d%d" % (h, b) for b in range(4)] for h in range(2)]
+    LI = ["li0", "li1", "li2", "li3"]
+    cnt = {"ls": 0}
+
+    for i, nm in enumerate(("la", "lx", "ra", "rx")):
+        dma("S", 80, T.li[:, 20 * i:20 * i + 20], T[nm][:, :], [], [LI[i]], "dl")
+    dma("Y", 2560, T.xt[:, :], T.x[:, :], [], ["xt"], "dx")
+    dma("Y", 512, T.lr[:, 0:256], T.l0[:, :], [], ["lr0"], "d0")
+    dma("Y", 512, T.lr[:, 256:512], T.r0[:, :], [], ["lr1"], "d0")
+
+    big = {"allow_small_or_imprecise_dtypes": True}
+    iota(1, T.qi[:, 3:4], [[1, 1]], 0, 1, ["qi"])
+    iota(8, T.pki[:, 0:8], [[8, 8]], 64, 0, ["pki"])
+    iota(8, T.pki[:, 8:16], [[8, 8]], 0, 0, ["pki2"])
+    iota(C, T.r16[:, :], [[0, 20], [1, 16]], 0, 0, ["r16"], **big)
+    fill(256, T.zz[:, :], 0.0, ["zz"])
+    select(T.a1[:, :], T.zz[:, :], [[-16, 8], [0, 64]], OP.is_ge, 1.0, -16, 1, ["zz"], ["a1"])
+    select(T.aw[:, :], T.a1[:, :], [[-16, 8], [0, 64]], OP.is_ge, 0.0, 0, 1, ["a1"], ["aw"])
+    quant(128, T.aq[:, :], T.ax[:, :], T.aw[:, :], ["aw"], ["aq"])
+    iota(C, T.yy[:, :], [[0, 20], [-2 * B, 16]], -B, 0, ["yy"], **big)
+    iota(A, T.y4[:, :], [[0, 16], [-2 * B, 4]], -B, 0, ["y4"], **big)
+    iota(C, T.i4[:, :], [[4, C]], 0, 0, ["i4"], **big)
+    quant(128, T.zc[:, :], T.zp[:, :], T.zz[:, :], ["zz"], ["zc"])
+    for f in range(2):
+        u = "%d" % f
+        for j in range(6):
+            a = 4 * (AT[j] + (16 * (TILES[j][-1] + 1) if j < 5 else 0))
+            dma("Y", 512, T["ut" + u][:, a:4 * AT[j + 1]], T.zz[:, 0:4 * AT[j + 1] - a], ["zz"], ["u%d%d%d" % (f, j, t) for t in range(4)], "du")
+    dma("Y", 2048, T.wq[:, :].bitcast(dt.uint8), T.wc[:, :], [], ["wq"], "dw")
+    dma("Y", 512, T.wp[:, :], T.ws[:, :], [], ["wp"], "dw")
+    dma("Y", 1024, T.vt[:, :], T.v[:, :], [], ["vt"], "dv")
+    for f in range(2):
+        u = "%d" % f
+        dma("Y", 512, T["pl" + u][:, 256:512], T.zz[:, 0:256], ["zz"], ["pz" + u], "dz")
+        dma("Y", 512, T["ft" + u][:, 0:256], T.zz[:, 0:256], ["zz"], ["fz" + u], "dz")
+        dma("Y", 256, T["lc" + u][:, 0:64].bitcast(dt.uint8), T.zc[:, 0:64].bitcast(dt.uint8), ["zc"], ["pad" + u], "dz")
+        dma("Y", 64, T["lp" + u][:, 0:64], T.zp[:, 0:64], ["zc"], ["pae" + u], "dz")
+        fill(1, T["rk" + u][:, 0:1], 0.0, ["rk%s0" % u])
+    fill(160, T.rs[:, :], 0.0, ["rs"])
+    fill(20, T.rs[:, 0:C:16], -BIG, ["rs"])
+    ts(1, T.qj[:, 0:1], T.qi[:, 3:4], 15, None, OP.bitwise_and, None, ["qi"], ["qj0"])
+    ts(1, T.qj[:, 1:2], T.qi[:, 3:4], 2, 3, OP.logical_shift_right, OP.bitwise_and, ["qi"], ["qj1"])
+    ts(1, T.qj[:, 2:3], T.qi[:, 3:4], 3, None, OP.bitwise_and, None, ["qi"], ["qj2"])
+    tc(16, T.pk[:, :], T.pki[:, :], ["pki", "pki2"], ["pk"])
+    tc(3, T.cf[:, 0:3], T.qj[:, 0:3], ["qj0", "qj1", "qj2"], ["cf0"])
+    ts(2, T.cf[:, 3:5], T.qj[:, 0:2], 2.0 * B, None, OP.mult, None, ["qj0", "qj1"], ["cf3"])
+    ts(2, T.cf[:, 5:7], T.qj[:, 0:2], -1.0 * B, -2.0 * B, OP.mult, OP.add, ["qj0", "qj1"], ["cf5"])
+    ts(1, T.cf[:, 7:8], T.cf[:, 6:7], T.cf[:, 2:3], None, OP.add, None, ["cf0", "cf5"], ["cf7"])
+    ts(160, T.mb[:, :], T.r16[:, :], T.cf[:, 0:1], -BIG, OP.not_equal, OP.mult, ["r16", "cf0"], ["mb"])
+    ts(C, T.d1[:, :], T.yy[:, :], T.cf[:, 3:4], -1.0 * B, OP.add, OP.max, ["yy", "cf3"], ["d1"])
+    iota(20, T.d1[:, 15:C:16], [[16, 20]], 17 * B - 1, 0, ["d1"], **big)
+    ts(A, T.d4[:, :], T.y4[:, :], T.cf[:, 4:5], -1.0 * B, OP.add, OP.max, ["y4", "cf3"], ["d4"])
+    iota(16, T.d4[:, 3:A:4], [[0, 16]], 5 * B, 0, ["d4"], **big)
+    act(256, T.wj[:, :], T.i4[:, 0:256], AF.Copy, ["i4"], ["wj"], scale=2.0 ** -12)
+    for b in range(4):
+        select(T.et[:, 512 * b:512 * b + 512], T.zz[:, :], [[1, 512]], OP.not_equal, 0.5, -b, -4, ["zz"], ["et%d" % b])
+    quant(512, T.eq[:, :], T.es[:, :], T.et[:, :], ["et%d" % b for b in range(4)], ["eq"])
+    quant(128, T.vq[:, :], T.vs[:, :], T.vt[:, :], ["vt"], ["vq"])
+
+    for t in range(4):
+        ts(80, T.off[:, 80 * t:80 * t + 80], T.li[:, :], 4.0, float(t), OP.mult, OP.add, LI, ["ot%d" % t])
+    act(256, T.bt[:, 0:256], T.lr[:, 0:256], AF.Copy, ["lr0"], HALF[0], scale=0.5)
+    act(256, T.bt[:, 256:512], T.lr[:, 256:512], AF.Copy, ["lr1"], HALF[1], scale=0.5)
+    for f in range(2):
+        u = "%d" % f
+        for t in range(4):
+            o = T["xg" + u][:, C * t:C * t + C]
+            w = T.xt[:, :].indirect(T.off[:, 80 * t + 40 * f + 20:80 * t + 40 * f + 40])
+            if f or t:
+                act(GATHER * C, o, w, AF.Copy, ["xt", "ot%d" % t], ["xg%d%d" % (f, t)], scale=0.5)
+            else:
+                ts(GATHER * C, o, w, 0.5, None, OP.mult, None, ["xt", "ot%d" % t], ["xg%d%d" % (f, t)])
+        tt(GATHER * C, T["vv" + u][:, :], T.wj[:, :].indirect(T.off[:, 40 * f:40 * f + 20]), T.i4[:, :], OP.add, ["wj", "ot0", "i4"], ["vv" + u])
+
+    def candidates(f, r):
+        u = "%d" % f
+        at(r, "cand" + u)
+        for t in range(4):
+            w = T.bt[:, 256 * f:256 * f + 256].indirect(T.off[:, 80 * t + 40 * f:80 * t + 40 * f + 20])
+            tt(GATHER * C, T["zt" + u][:, t:4 * C:4], w, T["xg" + u][:, C * t:C * t + C], OP.add, HALF[f] + ["ot%d" % t, "xg%d%d" % (f, t)], ["zt%d%d" % (f, t)])
+        quant(C, T["zq" + u][:, :], T["zs" + u][:, :], T["zt" + u][:, :], ["zt" + u + "%d" % t for t in range(4)], ["zq" + u])
+
+    def slot(f, c, a, b):
+        j, t = WHERE[c]
+        return T["ut%d" % f][:, 4 * (AT[j] + a) + t:4 * (AT[j] + b):4], ["u%d%d%d" % (f, j, t)]
+
+    def order(f, r):
+        u, (kv, ks, kd) = "%d" % f, BANKS[f][:3]
+        at(r, "sides")
+        s, k = slice(128 * f, 128 * f + 128), T.pk[:, 8 * f:8 * f + 8]
+        tc(GATHER * 128, T.st[:, s].bitcast(dt.uint32), T.sq[:, 0:128].bitcast(dt.uint32).indirect(k), ["sq", "pk"], ["st" + u])
+        act(GATHER * 128, T.ss[:, s], T.sp[:, 0:128].indirect(k), AF.Copy, ["sq", "pk"], ["ss" + u])
+        at(r, "score" + u)
+        for b in (kv, ks):
+            mm(b, C, T.st[:, s], T.ss[:, s], T["zq" + u][:, :], T["zs" + u][:, :], ["st" + u, "ss" + u, "zq" + u])
+        sc, sg, rk = T["sc" + u], T["sg" + u], T["rk" + u]
+        tt(C, T["mk" + u][:, :], psum(kv, 0, C), T.mb[:, :], OP.add, ["mb"], ["mk" + u], [kv])
+        scan(C, sc[:, :], T.rs[:, :], T["mk" + u][:, :], -BIG, OP.add, OP.max, ["rs", "mk" + u], ["sc" + u])
+        at(r, "rank" + u)
+        tt(C, T["ut" + u][:, 3:4 * C:4], psum(kv, 0, C), sc[:, :], OP.is_equal, ["sc" + u], ["u%d03" % f], [kv])
+        for i, c in enumerate(ALONE[f]):
+            act(16 * c + 16, sg[:, C * i:C * i + 16 * c + 16], psum(ks, 0, 16 * c + 16), AF.Sign, ["sc" + u], ["sg%s%d" % (u, c)], [ks],
+                bias=sc[:, 16 * c + 15:16 * c + 16], scale=-1.0)
+        for c in range(19, -1, -1):
+            w, own, sums = 16 * c, sc[:, 16 * c + 15:16 * c + 16], "rk%d%d" % (f, c)
+            if c in ALONE[f]:
+                a, sign = C * ALONE[f].index(c), "sg%s%d" % (u, c)
+                o, n = slot(f, c, 0, w)
+                act(w, o, sg[:, a:a + w], AF.Relu, [sign], n + [sums], accum_out=rk[:, c:c + 1])
+                o, n = slot(f, c, w, w + 16)
+                act(16, o, sg[:, a + w:a + w + 16], AF.Relu, [sign], ["own%s%d" % (u, c)])
+            else:
+                o, n = slot(f, c, 0, w + 16)
+                ts(w + 16, o, psum(kv, 0, w + 16), own, None, OP.is_lt, None, ["sc" + u], n, [kv])
+                if c:
+                    o, n = slot(f, c, 0, w)
+                    act(w, T["jk" + u][:, C * c:C * c + w], o, AF.Copy, n, ["jk%d%d" % (f, c), sums], accum_out=rk[:, c:c + 1])
+        for i, js in enumerate(QUANT):
+            s = slice(AT[js[0]], AT[js[-1] + 1])
+            quant(s.stop - s.start, T["uq" + u][:, s], T["us" + u][:, s], T["ut" + u][:, 4 * s.start:4 * s.stop],
+                  ["u%d%d%d" % (f, j, t) for j in js for t in range(4)] + ["own%s%d" % (u, c) for j in js for c in TILES[j]], ["uq%s%d" % (u, i)])
+            for j in js:
+                s = slice(AT[j], AT[j + 1])
+                mm(kd, WIDE[j], T.aq[:, :], T.ax[:, :], T["uq" + u][:, s], T["us" + u][:, s], ["aq", "uq%s%d" % (u, i)], j == 0, j == 5)
+
+    def survive(f, r):
+        u, b = "%d" % f, BANKS[f][2]
+        n = "%d%d" % (f, r)
+        at(r, "tail" + u)
+        scan(C, T["dd" + u][:, :], psum(b, 0, C), T.d1[:, :], 2.0 * B, OP.min, OP.add, ["d1"], ["dd" + u], [b])
+        tt(40, T["rr" + u][:, :], T["dd" + u][:, 15:C:16], T["rk" + u][:, :], OP.subtract, ["rk%d%d" % (f, c) for c in range(20)] + ["dd" + u], ["rr" + u])
+        ts(20, T["ro" + u][:, :], T["rr" + u][:, :], T.cf[:, 5:6], None, OP.add, None, ["rr" + u, "cf5"], ["ro" + u])
+        tc(SCATTER * C, T["inv" + u][:, :].indirect(T["ro" + u][:, 0:20]), T["vv" + u][:, :], ["ro" + u, "vv" + u], ["inv" + u])
+        scan(A, T["gn" + u][:, :], T["inv" + u][:, 0:A], T.d4[:, :], 2.0 * B, OP.min, OP.add, ["inv" + u, "d4"], ["gn" + u])
+        ts(16, T["of4" + u][:, :], T["gn" + u][:, 3:A:4], T.cf[:, 7:8], None, OP.add, None, ["gn" + u, "cf7"], ["of4" + u])
+        act(GATHER * 256, T["pl" + u][:, 0:256], T["zt" + u][:, :].indirect(T["of4" + u][:, 0:16]), AF.Copy,
+            ["of4" + u] + ["zt" + u + "%d" % t for t in range(4)], ["pl" + u])
+        v = slice(128 * r, 128 * r + 128)
+        quant(128, T["pc" + u][:, v], T["pp" + u][:, v], T["pl" + u][:, :], ["pl" + u, "pz" + u], ["pc" + n])
+        d = T.cores[(rank + 1 - 2 * f) % N]
+        rid, pid = topo.addr(d, core)
+        m, ne = topo.mask(core, d), len(topo.engines(core, d))
+        s, v, k = slice(64 * r + 64, 64 * r + 128), slice(128 * r, 128 * r + 64), "ar" + n
+
+        def move(q):
+            q.remote_dma(T["lc" + u][:, s].bitcast(dt.uint8), T["pc" + u][:, v].bitcast(dt.uint8), T.sem[k], T.sem.ls, pid, rid, m)
+            q.remote_dma(T["lp" + u][:, s], T["pp" + u][:, v], T.sem[k], T.sem.ls, pid, rid, m)
+            cnt["ls"] += 2 * ne
+            cnt[k] = 2 * ne
+        call("G", move, ["pc" + n], ["lc" + n], (), FIXED["G"], REMOTE, k)
+        at(r, "parents")
+        s4 = slice(8 * r + 4 * f, 8 * r + 4 * f + 4)
+        scan(A, T["en" + u][:, :], T["inv" + u][:, 0:A], T.d1[:, 0:A], 2.0 * B, OP.min, OP.add, ["inv" + u, "d1"], ["en" + u])
+        act(4, T.ou[:, s4], T["en" + u][:, 15:A:16], AF.Copy, ["en" + u], ["ou" + n], scale=256.0)
+
+    def parents_out(r):
+        k = "ao%d" % (r // (R - 1))
+
+        def move(q):
+            tr = []
+            for f in range(2):
+                d = T.cores[(rank + (R - r) * (1 - 2 * f)) % N]
+                rid, pid = topo.addr(d, core)
+                en = topo.engines(core, d)
+                h, s = len(en) // 2, slice(8 * r + 4 * f, 8 * r + 4 * f + 4)
+                tr.append(RemoteDMATransfer(dst_ids=[DstId(rid=rid, pnc=pid)], dma_engine_mask=sum(1 << e for e in en[h * f:h * f + h]),
+                                            remote_sem=T.sem[k], src=T.ou[:, s], dst=T.on[:, s]))
+                cnt["ls"] += h
+                cnt[k] = cnt.get(k, 0) + h
+            q.remote_dma_fused(tr, local_sem=T.sem.ls)
+        call("G", move, ["ou0%d" % r, "ou1%d" % r, "pc1%d" % r], ["on%d" % r], (), 0, REMOTE, k)
+
+    def parents_in(k):
+        n, s = "%d" % k, slice(16 * k, 16 + 8 * k)
+        tc(16, T.oi[:, s], T.on[:, s], ["on%d" % (k + 1)], ["oi" + n])
+        ts(16, T.oj[:, s], T.oi[:, s], 255, None, OP.bitwise_and, None, ["oi" + n], ["oj" + n])
+        tc(16, T.ox[:, s], T.oj[:, s], ["oj" + n], ["ox" + n])
+        for f in range(2):
+            u, o = "%d" % f, slice(A * f, A * f + A)
+            if k:
+                act(GATHER * A, T.of[:, o], T.ob[:, o].indirect(T.ox[:, 16 + 4 * f:20 + 4 * f]), AF.Copy, ["ox1", "ob" + u], ["of" + u])
+            else:
+                act(GATHER * A, T.oa[:, o], T.i4[:, 0:A].indirect(T.ox[:, 4 * f:4 + 4 * f]), AF.Copy, ["ox0", "i4"], ["oa" + u], scale=0.25)
+                act(GATHER * A, T.ob[:, o], T.oa[:, o].indirect(T.ox[:, 8 + 4 * f:12 + 4 * f]), AF.Identity, ["ox0", "oa" + u], ["ob" + u],
+                    bias=float(A * ((rank - R + 2 * R * f) % N)))
+
+    def renew(h, r):
+        last, u = r == R - 1, "%d" % h
+        n = "%d%d" % (h, r)
+        at(r, "renew" + u)
+        W = [slice(128 * b, 128 * b + 128) for b in range(4)]
+        x, ft = slice(64 * r, 64 * r + 128), T["ft" + u]
+        small = 1.0 / 16 if last else 1.0 / 32
+        FT = ["ft%s%d" % (u, b) for b in range(4)]
+
+        def unpack(b, start, stop):
+            mm(BANKS[h][b], 128, T.eq[:, W[b]], T.es[:, W[b]], T["lc" + u][:, x], T["lp" + u][:, x], ["lc" + n, "eq", "pad" + u, "pae" + u], start, stop)
+        for b in range(4):
+            unpack(b, True, True)
+        for b in range(4):
+            o, i, k = ft[:, 256 + b:512:4], psum(BANKS[h][b], 64, 128), BANKS[h][b]
+            if b % 2 or not h:
+                act(A, o, i, AF.Copy, [], [FT[b]], [k], scale=small)
+            else:
+                ts(A, o, i, small, None, OP.mult, None, [], [FT[b]], [k])
+        quant(128, T["fq" + u][:, :], T["fs" + u][:, :], ft[:, :], FT + ["fz" + u], ["fq" + u])
+        act(256, T["fh" + u][:, :], ft[:, 256:512], AF.Copy, FT, ["fh" + u], scale=32.0)
+        for b in range(4):
+            unpack(b, True, False)
+            if last:
+                unpack(b, False, False)
+        for b in range(4):
+            k = BANKS[h][b]
+            mm(k, 128, T.wq[:, W[b]], T.wp[:, W[b]], T["fq" + u][:, :], T["fs" + u][:, :], ["wq", "wp", "fq" + u], False, True)
+            tt(A, T.bt[:, 256 * h + b:256 * h + 256:4], psum(k, 64, 128), T["fh" + u][:, b:256:4], OP.max, ["fh" + u], ["b%s%d" % (u, b)], [k])
+
+    for r in range(R):
+        at(r, "sides")
+        quant(128, T.sq[:, :], T.sp[:, :], T.bt[:, :], HALF[0] + HALF[1], ["sq"])
+        for f in range(2):
+            candidates(f, r)
+            order(f, r)
+        for f in range(2):
+            survive(f, r)
+        parents_out(r)
+        if r:
+            parents_in(r - 1)
+        for f in range(2):
+            renew(f, r)
+    at(R, "sides")
+
+    quant(128, T.sq[:, :], T.sp[:, :], T.bt[:, :], HALF[0] + HALF[1], ["sq"])
+    dma("Y", 512, T.ot[:, :], T.of[0:128:16, :], ["of0", "of1"], [], "do")
+    dma("Y", 512, T.oc[:, :], T.sq[:, :].bitcast(dt.uint8), ["sq"], [], "do")
+    mm(0, 128, T.vq[:, :], T.vs[:, :], T.sq[:, :], T.sp[:, :], ["vq", "sq"])
+    act(128, T.yo[:, :], psum(0, 0, 128), AF.Copy, [], ["yo"], [0])
+    dma("S", 512, T.y[:, :], T.yo[:, :], ["yo"], [], "dy")
+    for k in range(4):
+        dma("Y", 128, T.osc[4 * k:4 * k + 4, :], T.sp[32 * k:32 * k + 4, :], ["sq"], [], "do")
+
+    seen, snap, token = {e: {} for e in Q}, {}, {}
 
     def wait(e, k, n):
         if seen[e].get(k, 0) >= n:
@@ -57,440 +398,21 @@ def rank_program(g, core, T, topo):
             if seen[e].get(a, 0) < b:
                 seen[e][a] = b
 
-    def need(e, rd, wr, ps=()):
-        own, want = "s" + e, {}
-        toks = [lastw[r] for r in list(rd) + list(wr) if r in lastw]
-        for w in wr:
-            toks += readers.get(w, [])
-        toks += [lastx[p] for p in ps if p in lastx and lastx[p][0] != own]
-        for k, n in toks:
-            n = cnt[k] if k[0] == "d" else n
-            want[k] = max(n, want.get(k, 0))
-        for k in sorted(want):
-            wait(e, k, want[k])
-
-    def note(tok, e, rd, wr, ps=()):
-        snap[tok] = dict(seen[e])
-        for r in rd:
-            readers.setdefault(r, []).append(tok)
-        for w in wr:
-            lastw[w], readers[w] = tok, []
-        for p in ps:
-            lastx[p] = tok
-
-    def op(e, f, rd, wr, ps=()):
-        need(e, rd, wr, ps)
-        k = "s" + e
-        cnt[k] = cnt.get(k, 0) + 1
-        f(Q[e]).then_inc(T.sem[k], 1)
-        note((k, cnt[k]), e, rd, wr, ps)
-
-    def tt(o, a, b, how, rd, wr, ps=()):
-        op("V", lambda q: q.tensor_tensor(o, a, b, how), rd, wr, ps)
-
-    def ts(o, a, s1, s2, o1, o2, rd, wr, ps=()):
-        if o2 is None:
-            op("V", lambda q: q.tensor_scalar(o, a, s1, None, o1), rd, wr, ps)
-        else:
-            op("V", lambda q: q.tensor_scalar(o, a, s1, s2, o1, o2), rd, wr, ps)
-
-    def tc(o, a, rd, wr, ps=()):
-        op("V", lambda q: q.tensor_copy(o, a), rd, wr, ps)
-
-    def fill(o, v, wr):
-        op("V", lambda q: q.memset(o, v), [], wr)
-
-    def scan(o, a, b, first, o1, o2, rd, wr):
-        op("V", lambda q: q.tensor_tensor_scan(o, a, b, first, o1, o2), rd, wr)
-
-    def quant(c, s, t, rd, wr):
-        op("V", lambda q: q.quantize_mx(c, s, t), rd, wr)
-
-    def act(o, i, func, rd, wr, ps=(), **kw):
-        op("S", lambda q: q.activation(o, i, func, **kw), rd, wr, ps)
-
-    def mm(bank, o, w, ws, x, xs, rd, start=True, stop=True):
-        op("T", lambda q: q.matmul_mx(o, w, ws, x, xs, start, stop), rd, [], [bank])
-
-    def dma(e, out, in_, rd, wr, k):
-        need(e, rd, wr)
-        cnt[k] = cnt.get(k, 0) + 16
-        Q[e].dma_start(out, in_).then_inc(T.sem[k], 16)
-        note((k, cnt[k]), e, rd, wr)
-
-    def iota(o, pattern, base, mult, wr, **kw):
-        op("G", lambda q: q.iota(o, pattern, base, mult, **kw), [], wr)
-
-    def run(*gens):
-        gens = list(gens)
-        while gens:
-            for x in list(gens):
-                if next(x, 1) is not None:
-                    gens.remove(x)
-
-    def chain(*gens):
-        for x in gens:
-            yield from x
-
-    HALF = [["b%d%d" % (h, b) for b in range(4)] for h in range(2)]
-    LI = ["li0", "li1", "li2", "li3"]
-
-    for i, nm in enumerate(("la", "lx", "ra", "rx")):
-        dma("S", T.li[:, 20 * i:20 * i + 20], T[nm][:, :], [], [LI[i]], "dl")
-    dma("Y", T.lr[:, 0:256], T.l0[:, :], [], ["lr0"], "d0")
-    dma("Y", T.lr[:, 256:512], T.r0[:, :], [], ["lr1"], "d0")
-    dma("Y", T.xt[:, :], T.x[:, :], [], ["xt"], "dx")
-    dma("Y", T.wq[:, :].bitcast(dt.uint8), T.wc[:, :], [], ["wq"], "dw")
-    dma("Y", T.wp[:, :], T.ws[:, :], [], ["wp"], "dw")
-    dma("Y", T.vt[:, :], T.v[:, :], [], ["vt"], "dv")
-
-    big = {"allow_small_or_imprecise_dtypes": True}
-    iota(T.qi[:, 3:4], [[1, 1]], 0, 1, ["qi"])
-    iota(T.pki[:, 0:8], [[8, 8]], 64, 0, ["pki"])
-    iota(T.pki[:, 8:16], [[8, 8]], 0, 0, ["pki2"])
-    iota(T.r16[:, :], [[0, 20], [1, 16]], 0, 0, ["r16"], **big)
-    iota(T.r4[:, :], [[0, 16], [1, 4]], 0, 0, ["r4"], **big)
-    iota(T.i8[:, :], [[1, 8], [0, 64]], 0, 0, ["i8"], **big)
-    val = [2 * (16 * (20 - c) - 1 - 8 * sum(a >= c for a in ALONE)) + (16 * c if c in ALONE else 0) for c in range(20)]
-    runs, c = [], 0
-    while c < 20:
-        d, e = (val[c + 1] - val[c] if c < 19 else 0), c + 1
-        while e < 20 and val[e] - val[e - 1] == d:
-            e += 1
-        runs.append("cc%d" % c)
-        iota(T.cc[:, c:e], [[d, e - c]], val[c], 0, [runs[-1]], **big)
-        c = e
-    iota(T.i4[:, :], [[4, C]], 0, 0, ["i4"], **big)
-    iota(T.olf[:, :], [[32, 2], [0, 2], [1, 32]], 0, 0, ["olf"], **big)
-    fill(T.zz[:, :], 0.0, ["zz"])
-    for b in range(4):
-        e = T.et[:, 512 * b:512 * b + 512]
-        op("G", lambda q: q.affine_select(e, T.zz[:, :], [[1, 512]], OP.not_equal, 0.5, -b, -4), ["zz"], ["et%d" % b])
-    quant(T.zc[:, :], T.zp[:, :], T.zz[:, :], ["zz"], ["zc"])
-    for f in range(2):
-        u = "%d" % f
-        dma("Y", T["lc" + u][:, 0:64].bitcast(dt.uint8), T.zc[:, 0:64].bitcast(dt.uint8), ["zc"], ["pad" + u], "dz")
-        dma("Y", T["lp" + u][:, 0:64], T.zp[:, 0:64], ["zc"], ["pae" + u], "dz")
-    tc(T.pk[:, :], T.pki[:, :], ["pki", "pki2"], ["pk"])
-    for f in range(2):
-        u = "%d" % f
-        for j in range(6):
-            z = T["ut" + u][:, 4 * (AT[j] + (16 * (TILES[j][-1] + 1) if j < 5 else 0)):4 * AT[j + 1]]
-            fill(z, 0.0, ["u%d%d%d" % (f, j, t) for t in range(4)])
-        fill(T["pl" + u][:, 256:512], 0.0, ["pz" + u])
-        fill(T["ft" + u][:, 256:512], 0.0, ["fz" + u])
-        fill(T["rk" + u][:, 0:1], 0.0, ["rk%s0" % u])
-
-    for t in range(4):
-        ts(T.off[:, 80 * t:80 * t + 80], T.li[:, :], 4.0, float(t), OP.mult, OP.add, LI, ["ot%d" % t])
-    act(T.bt[:, 0:256], T.lr[:, 0:256], AF.Copy, ["lr0"], HALF[0], scale=0.5)
-    act(T.bt[:, 256:512], T.lr[:, 256:512], AF.Copy, ["lr1"], HALF[1], scale=0.5)
-
-    def xgather(e, f, t):
-        o = T["xg%d" % f][:, C * t:C * t + C]
-        w = T.xt[:, :].indirect(T.off[:, 80 * t + 40 * f + 20:80 * t + 40 * f + 40])
-        if e == "S":
-            act(o, w, AF.Copy, ["xt", "ot%d" % t], ["xg%d%d" % (f, t)], scale=0.5)
-        else:
-            ts(o, w, 0.5, None, OP.mult, None, ["xt", "ot%d" % t], ["xg%d%d" % (f, t)])
-
-    def constants():
-        ts(T.qj[:, 0:1], T.qi[:, 3:4], 15, None, OP.bitwise_and, None, ["qi"], ["qj0"])
-        ts(T.qj[:, 1:2], T.qi[:, 3:4], 2, 3, OP.logical_shift_right, OP.bitwise_and, ["qi"], ["qj1"])
-        ts(T.qj[:, 2:3], T.qi[:, 3:4], 3, None, OP.bitwise_and, None, ["qi"], ["qj2"])
-        ts(T.qj[:, 3:4], T.qi[:, 3:4], 4, None, OP.logical_shift_right, None, ["qi"], ["qj3"])
-        tc(T.qf[:, :], T.qj[:, :], ["qj0", "qj1", "qj2", "qj3"], ["qf"])
-        ts(T.m16[:, :], T.r16[:, :], T.qf[:, 0:1], None, OP.is_equal, None, ["r16", "qf"], ["m16"])
-        ts(T.h16[:, :], T.r16[:, :], 0.0, None, OP.is_gt, None, ["r16"], ["h16"])
-        ts(T.mb[:, :], T.m16[:, :], 2 * BIG, -BIG, OP.mult, OP.add, ["m16"], ["mb"])
-        ts(T.rst[:, :], T.h16[:, :], 2 * BIG, -BIG, OP.mult, OP.add, ["h16"], ["rst"])
-        ts(T.h4[:, :], T.r4[:, :], 0.0, None, OP.is_gt, None, ["r4"], ["h4"])
-        ts(T.m4[:, :], T.r4[:, :], T.qf[:, 1:2], None, OP.is_equal, None, ["r4", "qf"], ["m4"])
-        ts(T.aw[:, 512:1024], T.i8[:, :], T.qf[:, 3:4], -2.0, OP.is_equal, OP.mult, ["i8", "qf"], ["aw1"])
-
-    def constants2():
-        act(T.aw[:, 0:512], T.aw[:, 512:1024], AF.Copy, ["aw1"], ["aw0"], scale=0.5)
-        act(T.aw[:, 3:512:4], T.aw[:, 515:1024:4], AF.Copy, ["aw1"], ["aw0"], scale=-1.0)
-        act(T.aw[:, 1024:1536], T.aw[:, 512:1024], AF.Copy, ["aw1"], ["aw2"], scale=0.5)
-
-    def constants3():
-        quant(T.aq[:, :], T.ax[:, :], T.aw[:, :], ["aw0", "aw1", "aw2"], ["aq"])
-        yield
-        ts(T.lj[:, :], T.li[:, :], 32.0, 32.0, OP.is_ge, OP.mult, LI, ["lj"])
-        yield
-        tt(T.lk[:, :], T.lj[:, :], T.li[:, :], OP.add, ["lj"] + LI, ["lk"])
-        yield
-        tc(T.op[:, 0:20], T.lk[:, 0:20], ["lk"], ["op0"])
-        ts(T.op[:, 20:40], T.lk[:, 40:60], 32.0, None, OP.add, None, ["lk"], ["op1"])
-
-    def picks(f):
-        s, k = slice(128 * f, 128 * f + 128), T.pk[:, 8 * f:8 * f + 8]
-        tc(T.st[:, s].bitcast(dt.uint32), T.sq[:, 0:128].bitcast(dt.uint32).indirect(k), ["sq", "pk"], ["st%d" % f])
-        act(T.ss[:, s], T.sp[:, 0:128].indirect(k), AF.Copy, ["sq", "pk"], ["ss%d" % f])
-
-    def cand(f, quarters):
-        for t in quarters:
-            w = T.bt[:, 256 * f:256 * f + 256].indirect(T.off[:, 80 * t + 40 * f:80 * t + 40 * f + 20])
-            tt(T["zt%d" % f][:, t:4 * C:4], w, T["xg%d" % f][:, C * t:C * t + C], OP.add, HALF[f] + ["ot%d" % t, "xg%d%d" % (f, t)], ["zt%d%d" % (f, t)])
-            yield
-
-    def zquant(f):
-        u = "%d" % f
-        quant(T["zq" + u][:, :], T["zs" + u][:, :], T["zt" + u][:, :], ["zt" + u + "%d" % t for t in range(4)], ["zq" + u])
-        yield
-
-    def score(f):
-        u = "%d" % f
-        s, k = slice(128 * f, 128 * f + 128), T.pw[:, 512 * f:512 * f + C]
-        mm("pw" + u, k, T.st[:, s], T.ss[:, s], T["zq" + u][:, :], T["zs" + u][:, :], ["st" + u, "ss" + u, "zq" + u])
-
-    def plain(f):
-        act(T["ap%d" % f][:, :], T.pw[:, 512 * f:512 * f + C], AF.Copy, [], ["ap%d" % f], ["pw%d" % f])
-
-    def slot(f, c, a, b):
-        j, t = WHERE[c]
-        return T["ut%d" % f][:, 4 * (AT[j] + a) + t:4 * (AT[j] + b):4], ["u%d%d%d" % (f, j, t)]
-
-    def prep(f):
-        u = "%d" % f
-        k = T.pw[:, 512 * f:512 * f + C]
-        tt(T["mk" + u][:, :], k, T.mb[:, :], OP.min, ["mb"], ["mk" + u], ["pw" + u])
-        yield
-        scan(T["sc" + u][:, :], T.rst[:, :], T["mk" + u][:, :], -BIG, OP.min, OP.max, ["rst", "mk" + u], ["sc" + u])
-        act(T["nt" + u][:, :], T["sc" + u][:, 15:C:16], AF.Copy, ["sc" + u], ["nt" + u], scale=-1.0)
-        yield
-        tt(T["ut" + u][:, 3:4 * C:4], k, T["sc" + u][:, :], OP.is_equal, ["sc" + u], ["u%d03" % f], ["pw" + u])
-        yield
-
-    turn = [0, 0]
-
-    def alone(f, cs):
-        u = "%d" % f
-
-        def second(c, sg):
-            w = 16 * c
-            o, n = slot(f, c, 0, w)
-            act(o, T.sg[:, C * sg:C * sg + w], AF.Sign, ["sg%d" % sg], n + ["rk%s%d" % (u, c)], bias=0.5, accum_out=T["rk" + u][:, c:c + 1])
-            o, n = slot(f, c, w, w + 16)
-            act(o, T.sg[:, C * sg + w:C * sg + w + 16], AF.Sign, ["sg%d" % sg], ["own%s%d" % (u, c)], bias=0.5)
-        last = None
-        for c in cs:
-            sg, turn[0] = turn[0] % 4, turn[0] + 1
-            act(T.sg[:, C * sg:C * sg + 16 * c + 16], T["ap" + u][:, 0:16 * c + 16], AF.Sign, ["ap" + u, "nt" + u], ["sg%d" % sg], bias=T["nt" + u][:, c:c + 1])
-            if last:
-                second(*last)
-            last = (c, sg)
-        second(*last)
-
-    def compare(f, cs):
-        u = "%d" % f
-        for c in cs:
-            o, n = slot(f, c, 0, 16 * c + 16)
-            ts(o, T["ap" + u][:, 0:16 * c + 16], T["sc" + u][:, 16 * c + 15:16 * c + 16], None, OP.is_ge, None, ["ap" + u, "sc" + u], n)
-            yield
-
-    def addup(f):
-        for c in OWN:
-            if c:
-                o, n = slot(f, c, 0, 16 * c)
-                jk, turn[1] = turn[1] % 4, turn[1] + 1
-                act(T.jk[:, C * jk:C * jk + 16 * c], o, AF.Copy, n, ["jk%d" % jk, "rk%d%d" % (f, c)], scale=2.0, accum_out=T["rk%d" % f][:, c:c + 1])
-
-    def down(f, j):
-        u = "%d" % f
-        s = slice(AT[j], AT[j + 1])
-        quant(T["uq" + u][:, s], T["us" + u][:, s], T["ut" + u][:, 4 * AT[j]:4 * AT[j + 1]],
-              ["u%d%d%d" % (f, j, t) for t in range(4)] + ["own%s%d" % (u, c) for c in TILES[j]], ["uq%s%d" % (u, j)])
-        b, w = 2 + f, 0 if j == 0 else 256 if j == LAST else 128
-        mm("pw%d" % b, T.pw[:, 512 * b:512 * b + WIDE[j]], T.aq[:, w:w + 128], T.ax[:, w:w + 128], T["uq" + u][:, s], T["us" + u][:, s],
-           ["aq", "uq%s%d" % (u, j)], j == 0, j == LAST)
-        yield
-
-    def survive(f, r):
-        u = "%d" % f
-        n = "%d%d" % (f, r)
-        b = 2 + f
-        tt(T["md" + u][:, :], T.pw[:, 512 * b:512 * b + C], T.m16[:, :], OP.mult, ["m16"], ["md" + u], ["pw%d" % b])
-        yield
-        scan(T["dd" + u][:, :], T.h16[:, :], T["md" + u][:, :], 0.0, OP.mult, OP.add, ["h16", "md" + u], ["dd" + u])
-        yield
-        tt(T["rr" + u][:, :], T["rk" + u][:, :], T.cc[:, :], OP.add, ["rk%d%d" % (f, c) for c in range(20)] + runs, ["rr" + u])
-        yield
-        tt(T["rs" + u][:, :], T["rr" + u][:, :], T["dd" + u][:, 15:C:16], OP.add, ["rr" + u, "dd" + u], ["rs" + u])
-        yield
-        ts(T["ro" + u][:, :], T["rs" + u][:, :], 0.5, None, OP.mult, None, ["rs" + u], ["ro" + u])
-        yield
-        tc(T["inv" + u][:, :].indirect(T["ro" + u][:, 0:20]), T.i4[:, :], ["ro" + u, "i4"], ["inv" + u])
-        yield
-        tt(T["gm" + u][:, :], T["inv" + u][:, 0:A], T.m4[:, :], OP.mult, ["inv" + u, "m4"], ["gm" + u])
-        yield
-        scan(T["gn" + u][:, :], T.h4[:, :], T["gm" + u][:, :], 0.0, OP.mult, OP.add, ["gm" + u, "h4"], ["gn" + u])
-        yield
-        ts(T["of4" + u][:, :], T["gn" + u][:, 3:A:4], T.qf[:, 2:3], None, OP.add, None, ["gn" + u, "qf"], ["of4" + u])
-        yield
-        tc(T["pl" + u][:, 0:256], T["zt" + u][:, :].indirect(T["of4" + u][:, 0:16]), ["of4" + u] + ["zt" + u + "%d" % t for t in range(4)], ["pl" + u])
-        yield
-        v = slice(128 * r, 128 * r + 128)
-        quant(T["pc" + u][:, v], T["pp" + u][:, v], T["pl" + u][:, :], ["pl" + u, "pz" + u], ["pc" + n])
-        d = T.cores[(rank + 1 - 2 * f) % N]
-        rid, pid = topo.addr(d, core)
-        m, ne = topo.mask(core, d), len(topo.engines(core, d))
-        s, v, k = slice(64 * r + 64, 64 * r + 128), slice(128 * r, 128 * r + 64), "ar" + n
-        need("G", ["pc" + n], [])
-        g.remote_dma(T["lc" + u][:, s].bitcast(dt.uint8), T["pc" + u][:, v].bitcast(dt.uint8), T.sem[k], T.sem.ls, pid, rid, m)
-        g.remote_dma(T["lp" + u][:, s], T["pp" + u][:, v], T.sem[k], T.sem.ls, pid, rid, m)
-        cnt["ls"] += 2 * ne
-        cnt[k] = 2 * ne
-        yield
-
-    def places(f):
-        u = "%d" % f
-        tt(T["em" + u][:, :], T["inv" + u][:, 0:A], T.m16[:, 0:A], OP.mult, ["inv" + u, "m16"], ["em" + u])
-        yield
-        scan(T["en" + u][:, :], T.h16[:, 0:A], T["em" + u][:, :], 0.0, OP.mult, OP.add, ["em" + u, "h16"], ["en" + u])
-        yield
-        ts(T["eo" + u][:, :], T["en" + u][:, 15:A:16], 0.25, None, OP.mult, None, ["en" + u], ["eo" + u])
-        s = slice(32 * f, 32 * f + 32)
-        act(T.olo[:, s], T["oz" + u][:, :].indirect(T["eo" + u][:, 0:2]), AF.Copy, ["oz" + u, "eo" + u], ["olo" + u])
-        act(T.ohi[:, s], T["oz" + u][:, :].indirect(T["eo" + u][:, 2:4]), AF.Copy, ["oz" + u, "eo" + u], ["ohi" + u], scale=64.0)
-        yield
-
-    def origins(f):
-        act(T["oz%d" % f][:, :], T.olf[:, :].indirect(T.op[:, 20 * f:20 * f + 20]), AF.Copy, ["olf", "op%d" % f], ["oz%d" % f])
-
-    def origins_out(r):
-        n = "%d" % r
-        tt(T.osm[:, :], T.olo[:, :], T.ohi[:, :], OP.add, ["olo0", "olo1", "ohi0", "ohi1"], ["osm"])
-        yield
-        tc(T.ou[:, 64 * r:64 * r + 64], T.osm[:, :], ["osm"], ["ou" + n])
-        need("G", ["ou" + n], [])
-        tr = []
-        for f in range(2):
-            d = T.cores[(rank + 1 - 2 * f) % N]
-            rid, pid = topo.addr(d, core)
-            en = topo.engines(core, d)
-            h, s = len(en) // 2, slice(64 * r + 32 * f, 64 * r + 32 * f + 32)
-            tr.append(RemoteDMATransfer(dst_ids=[DstId(rid=rid, pnc=pid)], dma_engine_mask=sum(1 << e for e in en[h * f:h * f + h]),
-                                        remote_sem=T.sem["ao" + n], src=T.ou[:, s], dst=T.on[:, s]))
-            cnt["ls"] += h
-            cnt["ao" + n] = cnt.get("ao" + n, 0) + h
-        g.remote_dma_fused(tr, local_sem=T.sem.ls)
-        yield
-
-    def origins_in(r, last):
-        n = "%d" % r
-        lastw["on" + n] = ("ao" + n, cnt["ao" + n])
-        tc(T.oi[:, :], T.on[:, 64 * r:64 * r + 64], ["on" + n], ["oi"])
-        yield
-        ts(T.oj[:, 0:64], T.oi[:, :], 63, None, OP.bitwise_and, None, ["oi"], ["oj0"])
-        ts(T.oj[:, 64:128], T.oi[:, :], 6, None, OP.logical_shift_right, None, ["oi"], ["oj1"])
-        yield
-        if not last:
-            tc(T.olf[:, :], T.oj[:, :], ["oj0", "oj1"], ["olf"])
-            return
-        for f in range(2):
-            base = float(A * ((rank - R + 2 * R * f) % N))
-            for h in range(2):
-                o, i = 64 * f + 32 * h, 64 * h + 32 * f
-                ts(T.of[:, o:o + 32], T.oj[:, i:i + 32], base, None, OP.add, None, ["oj%d" % h], ["of%d%d" % (f, h)])
-        dma("Y", T.ot[:, :], T.of[0:128:16, :], ["of00", "of01", "of10", "of11"], [], "do")
-
-    def renew(h, r):
-        last, u = r == R - 1, "%d" % h
-        n = "%d%d" % (h, r)
-        lastw["lc" + n] = ("ar" + n, cnt["ar" + n])
-        W = [slice(128 * b, 128 * b + 128) for b in range(4)]
-        P = [slice(512 * b, 512 * b + 128) for b in range(4)]
-        D = [slice(512 * b + 64, 512 * b + 128) for b in range(4)]
-        K = [slice(512 * b, 512 * b + 64) for b in range(4)]
-        B = [slice(64 * b + 256 * h, 64 * b + 256 * h + 64) for b in range(4)]
-        x, ft = slice(64 * r, 64 * r + 128), T["ft" + u]
-        two = 2.0 if last else 1.0
-        for b in range(4):
-            mm("pd%d" % b, T.pd[:, P[b]], T.eq[:, W[b]], T.es[:, W[b]], T["lc" + u][:, x], T["lp" + u][:, x], ["lc" + n, "eq", "pad" + u, "pae" + u])
-        for b in range(4):
-            o, i = ft[:, b:256:4], T.pd[:, D[b]]
-            if b % 2:
-                act(o, i, AF.Copy, [], ["ft%s%d" % (u, b)], ["pd%d" % b], scale=two)
-            else:
-                ts(o, i, two, None, OP.mult, None, [], ["ft%s%d" % (u, b)], ["pd%d" % b])
-                yield
-        quant(T["fq" + u][:, :], T["fs" + u][:, :], ft[:, :], ["ft%s%d" % (u, b) for b in range(4)] + ["fz" + u], ["fq" + u])
-        yield
-        for b in range(4):
-            mm("pw%d" % b, T.pw[:, P[b]], T.wq[:, W[b]], T.wp[:, W[b]], T["fq" + u][:, :], T["fs" + u][:, :], ["wq", "wp", "fq" + u])
-        for b in range(4):
-            act(T.rb[:, B[b]], T.pw[:, K[b]], AF.Relu, [], ["rb%s%d" % (u, b)], ["pw%d" % b], scale=0.03125)
-        for b in range(4):
-            o, i = T.bt[:, 256 * h + b:256 * h + 256:4], T.rb[:, B[b]]
-            if last:
-                tt(o, i, ft[:, b:256:4], OP.add, ["rb%s%d" % (u, b), "ft%s%d" % (u, b)], ["b%s%d" % (u, b)])
-            else:
-                tt(o, i, T.pd[:, D[b]], OP.add, ["rb%s%d" % (u, b)], ["b%s%d" % (u, b)], ["pd%d" % b])
-            yield
-
-    for r in range(R):
-        if r == 0:
-            constants()
-            for t in range(4):
-                xgather("S" if t < 2 else "V", 0, t)
-        quant(T.sq[:, :], T.sp[:, :], T.bt[:, :], HALF[0] + HALF[1], ["sq"])
-        picks(0)
-        if r == 0:
-            constants2()
-            for t in range(4):
-                xgather("S", 1, t)
-            run(cand(0, (2, 3, 0, 1)))
-            run(zquant(0), constants3())
-        score(0)
-        plain(0)
-        picks(1)
-        run(cand(1, (0, 1)))
-        run(prep(0), cand(1, (2, 3)))
-        alone(0, TILES[0])
-        run(zquant(1))
-        score(1)
-        z, p = compare(0, OWN), prep(1)
-        next(z)
-        next(p)
-        plain(1)
-        alone(0, TILES[LAST])
-        next(z)
-        next(p)
-        run(z)
-        run(p)
-        addup(0)
-        alone(1, TILES[0])
-        downs = [down(0, j) for j in [0] + REST]
-        if r:
-            downs.insert(0, origins_in(r - 1, False))
-        run(*downs)
-        run(down(0, LAST))
-        alone(1, TILES[LAST])
-        run(survive(0, r), compare(1, OWN))
-        addup(1)
-        for j in [0] + REST + [LAST]:
-            run(down(1, j))
-        origins(0)
-        origins(1)
-        run(survive(1, r), places(0))
-        if r == 0:
-            quant(T.eq[:, :], T.es[:, :], T.et[:, :], ["et%d" % b for b in range(4)], ["eq"])
-        run(renew(0, r), chain(places(1), origins_out(r)))
-        if r == 0:
-            quant(T.vq[:, :], T.vs[:, :], T.vt[:, :], ["vt"], ["vq"])
-        if r < R - 1:
-            run(cand(0, (0, 1, 2, 3)))
-            run(zquant(0))
-        run(renew(1, r))
-
-    quant(T.sq[:, :], T.sp[:, :], T.bt[:, :], HALF[0] + HALF[1], ["sq"])
-    dma("Y", T.oc[:, :], T.sq[:, :].bitcast(dt.uint8), ["sq"], [], "do")
-    mm("pw0", T.pw[:, 0:128], T.vq[:, :], T.vs[:, :], T.sq[:, :], T.sp[:, :], ["vq", "sq"])
-    act(T.yo[:, :], T.pw[:, 0:128], AF.Copy, [], ["yo"], ["pw0"])
-    dma("S", T.y[:, :], T.yo[:, :], ["yo"], [], "dy")
-    for k in range(4):
-        dma("Y", T.osc[4 * k:4 * k + 4, :], T.sp[32 * k:32 * k + 4, :], ["sq"], [], "do")
-    run(origins_in(R - 1, True))
+    for i in arrange(calls):
+        c = calls[i]
+        e, k, want = c["e"], c["sem"], {}
+        for j in c["deps"]:
+            a, n = token[j]
+            want[a] = max(cnt[a] if calls[j]["sem"] else n, want.get(a, 0))
+        for a in sorted(want):
+            wait(e, a, want[a])
+        done = c["f"](Q[e])
+        if k is None or k[0] == "d":
+            k, n = k or "s" + e, 16 if k else 1
+            cnt[k] = cnt.get(k, 0) + n
+            done.then_inc(T.sem[k], n)
+        token[i] = (k, cnt[k])
+        if k[0] != "a":
+            snap[token[i]] = dict(seen[e])
     for k in sorted(cnt):
         wait("G", k, cnt[k])

@@ -4,17 +4,18 @@ from concourse.mybir import dt, AluOpType, ActivationFunctionType
 N, C, A, R = 8, 320, 64, 3
 BIG = 2.0 ** 90
 B = 1536
-TILES = [[19, 18, 17], [16, 15, 14, 13], [12, 11, 10, 9], [8, 7, 6, 5], [4, 3, 2, 1], [0]]
-WIDE = [C, 272, 208, 144, 128, 128]
-AT = [sum(WIDE[:j]) for j in range(7)]
-ALONE = [[19, 18, 17, 16, 15], [19, 18, 17, 16, 15]]
-QUANT = [[0], [1, 2], [3, 4, 5]]
-WHERE = {c: (j, t) for j in range(6) for t, c in enumerate(TILES[j])}
+TILES = [[19, 18, 17], [16, 15, 14, 13], [12, 11, 10, 9], [8, 7, 6, 5], [4, 3, 2, 1]]
+WIDE = [C, 256, 192, 128, 128]
+AT = [sum(WIDE[:j]) for j in range(6)]
+ALONE = [range(19, 10, -1), range(19, 12, -1)]
+SCANS = [7, 1]
+QUANT = [[0], [1, 2], [3, 4]]
+WHERE = {c: (j, t) for j in range(5) for t, c in enumerate(TILES[j])}
 BANKS = [[0, 1, 4, 6], [2, 3, 5, 7]]
-FIXED = {"V": 35, "S": 70, "T": 10, "G": 170, "Y": 70}
-GATHER, SCATTER, SIGNAL, LOCAL, REMOTE, HOLD = 1.5, 3.5, 50, 1400, 2200, 60
+FIXED = {"V": 35, "S": 90, "T": 10, "G": 170, "Y": 70}
+GATHER, SCATTER, SIGNAL, LOCAL, LIST, REMOTE, WHOLE, HOLD = 1.5, 3.5, 50, 1400, 1800, 2200, 5000, 60
 
-TURNS = ["sides", "cand0", "score0", "cand1", "score1", "rank0", "tail0", "rank1", "tail1", "renew0", "renew1", "parents"]
+TURNS = ["sides", "cand0", "score0", "cand1", "score1", "rank0", "tail0", "rank1", "tail1", "renew0", "renew1", "unpack", "parents"]
 
 SCRATCH = {}
 
@@ -27,19 +28,24 @@ def sbuf(kind, **names):
 BF, F4, I4, U2, Q8, U1 = "bfloat16", "float32", "int32", "uint16", "float8_e4m3fn_x4", "uint8"
 sbuf(I4, li=80, pki=16, qi=4, qj=4, oi=24, oj=24)
 sbuf(U2, pk=16, off=320, ox=24)
-sbuf(BF, xt=4 * C, lr=512, bt=512, vt=512, et=2048, a1=512, aw=512, zz=512, r16=C, mb=C, rs=C)
-sbuf(Q8, vq=128, eq=512, aq=128, zc=128, wq=512, sq=128, st=256)
-sbuf(U1, vs=128, es=512, ax=128, zp=128, wp=512, sp=128, ss=256)
+sbuf(BF, xt=4 * C, lr=512, bt=512, vt=512, et=2048, a1=512, a2=128, aw=1024, zz=512, r16=C, mb=C, rs=C, h16=C)
+sbuf(Q8, vq=128, eq=512, aq=256, zc=128, wq=512, sq=128, st=256)
+sbuf(U1, vs=128, es=512, ax=256, zp=128, wp=512, sp=128, ss=256)
 sbuf(F4, yo=128, cf=8, yy=C, y4=A, i4=C, wj=256, d1=C, d4=A, ou=24, on=24, oa=128, ob=128, of=128)
 SCRATCH["ps"] = ("psum", [128, 4096], F4)
 for _f in "01":
-    sbuf(BF, **{"xg" + _f: 4 * C, "zt" + _f: 4 * C, "pl" + _f: 512, "ft" + _f: 512, "fh" + _f: 256, "ut" + _f: 4 * AT[6], "jk" + _f: 20 * C, "sg" + _f: 10 * C})
-    sbuf(F4, **{"mk" + _f: C, "sc" + _f: C, "rk" + _f: 20, "rr" + _f: 20, "dd" + _f: C, "vv" + _f: C, "inv" + _f: C, "gn" + _f: A, "en" + _f: A})
-    sbuf(U2, **{"ro" + _f: 20, "of4" + _f: 16})
-    sbuf(Q8, **{"zq" + _f: C, "uq" + _f: AT[6], "fq" + _f: 128, "pc" + _f: 128 * R, "lc" + _f: 256})
-    sbuf(U1, **{"zs" + _f: C, "us" + _f: AT[6], "fs" + _f: 128, "pp" + _f: 128 * R, "lp" + _f: 256})
+    sbuf(BF, **{"xg" + _f: 4 * C, "zt" + _f: 4 * C, "ft" + _f: 512, "ut" + _f: 4 * AT[5], "jk" + _f: 20 * C, "sg" + _f: 12 * C, "de" + _f: C})
+    sbuf(F4, **{"mk" + _f: C, "ap" + _f: C, "sc" + _f: C, "rk" + _f: 20, "ry" + _f: 20, "rr" + _f: 20, "dd" + _f: C, "vv" + _f: C, "inv" + _f: C, "gn" + _f: A, "en" + _f: A})
+    sbuf(U2, **{"ro" + _f: 20, "of4" + _f: 16 * R})
+    sbuf(Q8, **{"zq" + _f: C * R, "uq" + _f: AT[5], "fq" + _f: 128})
+    sbuf(U1, **{"zs" + _f: C * R, "us" + _f: AT[5], "fs" + _f: 128})
+sbuf(BF, pl=512, fh=256, yd=4 * C)
+sbuf(F4, rb=256)
+sbuf(U2, ln=16 * R)
+sbuf(Q8, pc=128 * R, lc=256, yc=C * R)
+sbuf(U1, pp=128 * R, lp=256, yp=C * R)
 SEMAPHORES = ["sV", "sS", "sT", "sG", "ls", "dl", "d0", "dx", "dw", "dv", "dz", "du", "dy", "do", "ao0", "ao1"]
-SEMAPHORES += ["ar%d%d" % (_f, _r) for _f in range(2) for _r in range(R)]
+SEMAPHORES += [_k + "%d" % _r for _k in ("ar0", "ar1", "ay") for _r in range(R)]
 
 
 def arrange(calls):
@@ -103,7 +109,7 @@ def rank_program(g, core, T, topo):
         calls.append({"e": e, "f": f, "deps": deps, "behind": behind - deps, "busy": FIXED[e] + busy, "late": late, "sem": sem, "turn": turn[0]})
 
     def vec(n, f, rd, wr, ps):
-        call("V", f, rd, wr, ps, max(64, n))
+        call("V", f, rd, wr, ps, max(64, n) + (70 if ps else 0))
 
     def tt(n, o, a, b, how, rd, wr, ps=()):
         vec(n, lambda q: q.tensor_tensor(o, a, b, how), rd, wr, ps)
@@ -163,30 +169,36 @@ def rank_program(g, core, T, topo):
     iota(8, T.pki[:, 8:16], [[8, 8]], 0, 0, ["pki2"])
     iota(C, T.r16[:, :], [[0, 20], [1, 16]], 0, 0, ["r16"], **big)
     fill(256, T.zz[:, :], 0.0, ["zz"])
+    at(0, "rank0")
     select(T.a1[:, :], T.zz[:, :], [[-16, 8], [0, 64]], OP.is_ge, 1.0, -16, 1, ["zz"], ["a1"])
-    select(T.aw[:, :], T.a1[:, :], [[-16, 8], [0, 64]], OP.is_ge, 0.0, 0, 1, ["a1"], ["aw"])
-    quant(128, T.aq[:, :], T.ax[:, :], T.aw[:, :], ["aw"], ["aq"])
+    for h in range(2):
+        select(T.aw[:, 512 * h:512 * h + 512], T.a1[:, :], [[-16, 8], [0, 64]], OP.is_ge, 0.0, 0, 1, ["a1"], ["aw%d" % h])
+    select(T.a2[:, :], T.zz[:, 0:128], [[-16, 8], [0, 16]], OP.is_ge, -1.0, -16, 1, ["zz"], ["a2"])
+    select(T.aw[:, 3:512:4], T.a2[:, :], [[-16, 8], [0, 16]], OP.is_ge, 0.0, 0, 1, ["a2"], ["aw0"])
+    quant(256, T.aq[:, :], T.ax[:, :], T.aw[:, :], ["aw0", "aw1"], ["aq"])
+    at(0, "tail0")
     iota(C, T.yy[:, :], [[0, 20], [-2 * B, 16]], -B, 0, ["yy"], **big)
     iota(A, T.y4[:, :], [[0, 16], [-2 * B, 4]], -B, 0, ["y4"], **big)
     iota(C, T.i4[:, :], [[4, C]], 0, 0, ["i4"], **big)
     quant(128, T.zc[:, :], T.zp[:, :], T.zz[:, :], ["zz"], ["zc"])
     for f in range(2):
         u = "%d" % f
-        for j in range(6):
-            a = 4 * (AT[j] + (16 * (TILES[j][-1] + 1) if j < 5 else 0))
+        for j in range(5):
+            a = 4 * (AT[j] + 16 * TILES[j][-1])
             dma("Y", 512, T["ut" + u][:, a:4 * AT[j + 1]], T.zz[:, 0:4 * AT[j + 1] - a], ["zz"], ["u%d%d%d" % (f, j, t) for t in range(4)], "du")
     dma("Y", 2048, T.wq[:, :].bitcast(dt.uint8), T.wc[:, :], [], ["wq"], "dw")
     dma("Y", 512, T.wp[:, :], T.ws[:, :], [], ["wp"], "dw")
     dma("Y", 1024, T.vt[:, :], T.v[:, :], [], ["vt"], "dv")
+    dma("Y", 512, T.pl[:, 256:512], T.zz[:, 0:256], ["zz"], ["pz"], "dz")
+    dma("Y", 256, T.lc[:, 0:64].bitcast(dt.uint8), T.zc[:, 0:64].bitcast(dt.uint8), ["zc"], ["pad"], "dz")
+    dma("Y", 64, T.lp[:, 0:64], T.zp[:, 0:64], ["zc"], ["pae"], "dz")
     for f in range(2):
         u = "%d" % f
-        dma("Y", 512, T["pl" + u][:, 256:512], T.zz[:, 0:256], ["zz"], ["pz" + u], "dz")
         dma("Y", 512, T["ft" + u][:, 0:256], T.zz[:, 0:256], ["zz"], ["fz" + u], "dz")
-        dma("Y", 256, T["lc" + u][:, 0:64].bitcast(dt.uint8), T.zc[:, 0:64].bitcast(dt.uint8), ["zc"], ["pad" + u], "dz")
-        dma("Y", 64, T["lp" + u][:, 0:64], T.zp[:, 0:64], ["zc"], ["pae" + u], "dz")
-        fill(1, T["rk" + u][:, 0:1], 0.0, ["rk%s0" % u])
+        fill(1, T["jk" + u][:, C - 1:C], 0.0, ["rk%s0" % u])
+    turn[0] = 0
     fill(160, T.rs[:, :], 0.0, ["rs"])
-    fill(20, T.rs[:, 0:C:16], -BIG, ["rs"])
+    fill(20, T.rs[:, 0:C:16], BIG, ["rs"])
     ts(1, T.qj[:, 0:1], T.qi[:, 3:4], 15, None, OP.bitwise_and, None, ["qi"], ["qj0"])
     ts(1, T.qj[:, 1:2], T.qi[:, 3:4], 2, 3, OP.logical_shift_right, OP.bitwise_and, ["qi"], ["qj1"])
     ts(1, T.qj[:, 2:3], T.qi[:, 3:4], 3, None, OP.bitwise_and, None, ["qi"], ["qj2"])
@@ -195,23 +207,30 @@ def rank_program(g, core, T, topo):
     ts(2, T.cf[:, 3:5], T.qj[:, 0:2], 2.0 * B, None, OP.mult, None, ["qj0", "qj1"], ["cf3"])
     ts(2, T.cf[:, 5:7], T.qj[:, 0:2], -1.0 * B, -2.0 * B, OP.mult, OP.add, ["qj0", "qj1"], ["cf5"])
     ts(1, T.cf[:, 7:8], T.cf[:, 6:7], T.cf[:, 2:3], None, OP.add, None, ["cf0", "cf5"], ["cf7"])
-    ts(160, T.mb[:, :], T.r16[:, :], T.cf[:, 0:1], -BIG, OP.not_equal, OP.mult, ["r16", "cf0"], ["mb"])
+    ts(1, T.cf[:, 5:6], T.cf[:, 5:6], T.cf[:, 0:1], None, OP.add, None, ["cf0", "cf5"], ["cf5"])
+    ts(160, T.mb[:, :], T.r16[:, :], T.cf[:, 0:1], BIG, OP.not_equal, OP.mult, ["r16", "cf0"], ["mb"])
+    ts(160, T.h16[:, :], T.r16[:, :], 0.0, None, OP.is_gt, None, ["r16"], ["h16"])
+    at(0, "tail0")
     ts(C, T.d1[:, :], T.yy[:, :], T.cf[:, 3:4], -1.0 * B, OP.add, OP.max, ["yy", "cf3"], ["d1"])
-    iota(20, T.d1[:, 15:C:16], [[16, 20]], 17 * B - 1, 0, ["d1"], **big)
+    iota(20, T.d1[:, 15:C:16], [[16, 20]], 17 * B, 0, ["d1"], **big)
     ts(A, T.d4[:, :], T.y4[:, :], T.cf[:, 4:5], -1.0 * B, OP.add, OP.max, ["y4", "cf3"], ["d4"])
     iota(16, T.d4[:, 3:A:4], [[0, 16]], 5 * B, 0, ["d4"], **big)
     act(256, T.wj[:, :], T.i4[:, 0:256], AF.Copy, ["i4"], ["wj"], scale=2.0 ** -12)
+    at(0, "renew0")
     for b in range(4):
         select(T.et[:, 512 * b:512 * b + 512], T.zz[:, :], [[1, 512]], OP.not_equal, 0.5, -b, -4, ["zz"], ["et%d" % b])
     quant(512, T.eq[:, :], T.es[:, :], T.et[:, :], ["et%d" % b for b in range(4)], ["eq"])
+    at(0, "parents")
     quant(128, T.vq[:, :], T.vs[:, :], T.vt[:, :], ["vt"], ["vq"])
 
+    turn[0] = 0
     for t in range(4):
         ts(80, T.off[:, 80 * t:80 * t + 80], T.li[:, :], 4.0, float(t), OP.mult, OP.add, LI, ["ot%d" % t])
     act(256, T.bt[:, 0:256], T.lr[:, 0:256], AF.Copy, ["lr0"], HALF[0], scale=0.5)
     act(256, T.bt[:, 256:512], T.lr[:, 256:512], AF.Copy, ["lr1"], HALF[1], scale=0.5)
     for f in range(2):
         u = "%d" % f
+        at(0, "cand" + u)
         for t in range(4):
             o = T["xg" + u][:, C * t:C * t + C]
             w = T.xt[:, :].indirect(T.off[:, 80 * t + 40 * f + 20:80 * t + 40 * f + 40])
@@ -219,7 +238,20 @@ def rank_program(g, core, T, topo):
                 act(GATHER * C, o, w, AF.Copy, ["xt", "ot%d" % t], ["xg%d%d" % (f, t)], scale=0.5)
             else:
                 ts(GATHER * C, o, w, 0.5, None, OP.mult, None, ["xt", "ot%d" % t], ["xg%d%d" % (f, t)])
+        at(0, "tail" + u)
         tt(GATHER * C, T["vv" + u][:, :], T.wj[:, :].indirect(T.off[:, 40 * f:40 * f + 20]), T.i4[:, :], OP.add, ["wj", "ot0", "i4"], ["vv" + u])
+
+    def move(f, pairs, rd, k, late):
+        d = T.cores[(rank + 1 - 2 * f) % N]
+        rid, pid = topo.addr(d, core)
+        m, ne = topo.mask(core, d), len(topo.engines(core, d))
+
+        def writes(q):
+            for o, i in pairs:
+                q.remote_dma(o, i, T.sem[k], T.sem.ls, pid, rid, m)
+                cnt["ls"] += ne
+                cnt[k] = cnt.get(k, 0) + ne
+        call("G", writes, rd, [k], (), FIXED["G"] * (len(pairs) - 1), late, k)
 
     def candidates(f, r):
         u = "%d" % f
@@ -227,7 +259,10 @@ def rank_program(g, core, T, topo):
         for t in range(4):
             w = T.bt[:, 256 * f:256 * f + 256].indirect(T.off[:, 80 * t + 40 * f:80 * t + 40 * f + 20])
             tt(GATHER * C, T["zt" + u][:, t:4 * C:4], w, T["xg" + u][:, C * t:C * t + C], OP.add, HALF[f] + ["ot%d" % t, "xg%d%d" % (f, t)], ["zt%d%d" % (f, t)])
-        quant(C, T["zq" + u][:, :], T["zs" + u][:, :], T["zt" + u][:, :], ["zt" + u + "%d" % t for t in range(4)], ["zq" + u])
+        s = slice(C * r, C * r + C)
+        quant(C, T["zq" + u][:, s], T["zs" + u][:, s], T["zt" + u][:, :], ["zt" + u + "%d" % t for t in range(4)], ["zq%d%d" % (f, r)])
+        if f:
+            move(f, [(T.yc[:, s].bitcast(dt.uint8), T.zq1[:, s].bitcast(dt.uint8)), (T.yp[:, s], T.zs1[:, s])], ["zq1%d" % r], "ay%d" % r, WHOLE)
 
     def slot(f, c, a, b):
         j, t = WHERE[c]
@@ -241,62 +276,61 @@ def rank_program(g, core, T, topo):
         act(GATHER * 128, T.ss[:, s], T.sp[:, 0:128].indirect(k), AF.Copy, ["sq", "pk"], ["ss" + u])
         at(r, "score" + u)
         for b in (kv, ks):
-            mm(b, C, T.st[:, s], T.ss[:, s], T["zq" + u][:, :], T["zs" + u][:, :], ["st" + u, "ss" + u, "zq" + u])
+            mm(b, C, T.st[:, s], T.ss[:, s], T["zq" + u][:, C * r:C * r + C], T["zs" + u][:, C * r:C * r + C], ["st" + u, "ss" + u, "zq%d%d" % (f, r)])
         sc, sg, rk = T["sc" + u], T["sg" + u], T["rk" + u]
         tt(C, T["mk" + u][:, :], psum(kv, 0, C), T.mb[:, :], OP.add, ["mb"], ["mk" + u], [kv])
-        scan(C, sc[:, :], T.rs[:, :], T["mk" + u][:, :], -BIG, OP.add, OP.max, ["rs", "mk" + u], ["sc" + u])
+        scan(C, sc[:, :], T.rs[:, :], T["mk" + u][:, :], BIG, OP.add, OP.min, ["rs", "mk" + u], ["sc" + u])
+        w = 16 * (min(ALONE[f]) - 1)
+        act(w, T["ap" + u][:, 0:w], psum(ks, 0, w), AF.Copy, [], ["ap" + u], [ks])
         at(r, "rank" + u)
-        tt(C, T["ut" + u][:, 3:4 * C:4], psum(kv, 0, C), sc[:, :], OP.is_equal, ["sc" + u], ["u%d03" % f], [kv])
         for i, c in enumerate(ALONE[f]):
-            act(16 * c + 16, sg[:, C * i:C * i + 16 * c + 16], psum(ks, 0, 16 * c + 16), AF.Sign, ["sc" + u], ["sg%s%d" % (u, c)], [ks],
+            act(16 * c, sg[:, C * i:C * i + 16 * c], psum(ks, 0, 16 * c), AF.Sign, ["sc" + u], ["sg%s%d" % (u, c)], [ks],
                 bias=sc[:, 16 * c + 15:16 * c + 16], scale=-1.0)
-        for c in range(19, -1, -1):
-            w, own, sums = 16 * c, sc[:, 16 * c + 15:16 * c + 16], "rk%d%d" % (f, c)
+        de, jk, a = T["de" + u], T["jk" + u], SCANS[f] + 1
+        tt(C, T["ut" + u][:, 3:4 * C:4], psum(kv, 0, C), sc[:, :], OP.is_gt, ["sc" + u], ["u%d03" % f], [kv])
+        for c in range(19, 0, -1):
+            w, sums = 16 * c, "rk%d%d" % (f, c)
+            o, n = slot(f, c, 0, w)
             if c in ALONE[f]:
-                a, sign = C * ALONE[f].index(c), "sg%s%d" % (u, c)
-                o, n = slot(f, c, 0, w)
-                act(w, o, sg[:, a:a + w], AF.Relu, [sign], n + [sums], accum_out=rk[:, c:c + 1])
-                o, n = slot(f, c, w, w + 16)
-                act(16, o, sg[:, a + w:a + w + 16], AF.Relu, [sign], ["own%s%d" % (u, c)])
-            else:
-                o, n = slot(f, c, 0, w + 16)
-                ts(w + 16, o, psum(kv, 0, w + 16), own, None, OP.is_lt, None, ["sc" + u], n, [kv])
-                if c:
-                    o, n = slot(f, c, 0, w)
-                    act(w, T["jk" + u][:, C * c:C * c + w], o, AF.Copy, n, ["jk%d%d" % (f, c), sums], accum_out=rk[:, c:c + 1])
+                i = C * ALONE[f].index(c)
+                act(w, o, sg[:, i:i + w], AF.Relu, ["sg%s%d" % (u, c)], n + [sums], accum_out=rk[:, c:c + 1])
+                continue
+            ts(w, o, T["ap" + u][:, 0:w], sc[:, w + 15:w + 16], None, OP.is_lt, None, ["sc" + u, "ap" + u], n)
+            if c >= a:
+                act(w, jk[:, C * c:C * c + w], o, AF.Copy, n, ["jk%d%d" % (f, c), sums], accum_out=rk[:, c:c + 1])
+        for c in range(a - 1, 0, -1):
+            o, n = slot(f, c, 0, 16 * c)
+            scan(8 * c, jk[:, C * c + C - 16 * c:C * c + C], o, T.zz[:, 0:16 * c], 0.0, OP.add, OP.add, n + ["zz"], ["rk%d%d" % (f, c)])
+        scan(C / 2, de[:, :], T.h16[:, :], T["ut" + u][:, 3:4 * C:4], 0.0, OP.mult, OP.add, ["h16", "u%d03" % f], ["de" + u])
+        tt(40, T["ry" + u][:, 0:a], jk[:, C - 1:C * a:C], de[:, 15:16 * a:16], OP.subtract, ["rk%d%d" % (f, c) for c in range(a)] + ["de" + u], ["rx" + u])
+        tt(40, T["ry" + u][:, a:20], rk[:, a:20], de[:, 16 * a + 15:C:16], OP.subtract, ["rk%d%d" % (f, c) for c in range(a, 20)] + ["de" + u], ["ry" + u])
         for i, js in enumerate(QUANT):
             s = slice(AT[js[0]], AT[js[-1] + 1])
             quant(s.stop - s.start, T["uq" + u][:, s], T["us" + u][:, s], T["ut" + u][:, 4 * s.start:4 * s.stop],
-                  ["u%d%d%d" % (f, j, t) for j in js for t in range(4)] + ["own%s%d" % (u, c) for j in js for c in TILES[j]], ["uq%s%d" % (u, i)])
+                  ["u%d%d%d" % (f, j, t) for j in js for t in range(4)], ["uq%s%d" % (u, i)])
             for j in js:
                 s = slice(AT[j], AT[j + 1])
-                mm(kd, WIDE[j], T.aq[:, :], T.ax[:, :], T["uq" + u][:, s], T["us" + u][:, s], ["aq", "uq%s%d" % (u, i)], j == 0, j == 5)
+                w = slice(128, 256) if j else slice(0, 128)
+                mm(kd, WIDE[j], T.aq[:, w], T.ax[:, w], T["uq" + u][:, s], T["us" + u][:, s], ["aq", "uq%s%d" % (u, i)], j == 0, j == 4)
 
     def survive(f, r):
         u, b = "%d" % f, BANKS[f][2]
         n = "%d%d" % (f, r)
         at(r, "tail" + u)
         scan(C, T["dd" + u][:, :], psum(b, 0, C), T.d1[:, :], 2.0 * B, OP.min, OP.add, ["d1"], ["dd" + u], [b])
-        tt(40, T["rr" + u][:, :], T["dd" + u][:, 15:C:16], T["rk" + u][:, :], OP.subtract, ["rk%d%d" % (f, c) for c in range(20)] + ["dd" + u], ["rr" + u])
+        tt(40, T["rr" + u][:, :], T["dd" + u][:, 15:C:16], T["ry" + u][:, :], OP.subtract, ["rx" + u, "ry" + u, "dd" + u], ["rr" + u])
         ts(20, T["ro" + u][:, :], T["rr" + u][:, :], T.cf[:, 5:6], None, OP.add, None, ["rr" + u, "cf5"], ["ro" + u])
         tc(SCATTER * C, T["inv" + u][:, :].indirect(T["ro" + u][:, 0:20]), T["vv" + u][:, :], ["ro" + u, "vv" + u], ["inv" + u])
         scan(A, T["gn" + u][:, :], T["inv" + u][:, 0:A], T.d4[:, :], 2.0 * B, OP.min, OP.add, ["inv" + u, "d4"], ["gn" + u])
-        ts(16, T["of4" + u][:, :], T["gn" + u][:, 3:A:4], T.cf[:, 7:8], None, OP.add, None, ["gn" + u, "cf7"], ["of4" + u])
-        act(GATHER * 256, T["pl" + u][:, 0:256], T["zt" + u][:, :].indirect(T["of4" + u][:, 0:16]), AF.Copy,
-            ["of4" + u] + ["zt" + u + "%d" % t for t in range(4)], ["pl" + u])
-        v = slice(128 * r, 128 * r + 128)
-        quant(128, T["pc" + u][:, v], T["pp" + u][:, v], T["pl" + u][:, :], ["pl" + u, "pz" + u], ["pc" + n])
-        d = T.cores[(rank + 1 - 2 * f) % N]
-        rid, pid = topo.addr(d, core)
-        m, ne = topo.mask(core, d), len(topo.engines(core, d))
-        s, v, k = slice(64 * r + 64, 64 * r + 128), slice(128 * r, 128 * r + 64), "ar" + n
-
-        def move(q):
-            q.remote_dma(T["lc" + u][:, s].bitcast(dt.uint8), T["pc" + u][:, v].bitcast(dt.uint8), T.sem[k], T.sem.ls, pid, rid, m)
-            q.remote_dma(T["lp" + u][:, s], T["pp" + u][:, v], T.sem[k], T.sem.ls, pid, rid, m)
-            cnt["ls"] += 2 * ne
-            cnt[k] = 2 * ne
-        call("G", move, ["pc" + n], ["lc" + n], (), FIXED["G"], REMOTE, k)
+        s = slice(16 * r, 16 * r + 16)
+        ts(16, T["of4" + u][:, s], T["gn" + u][:, 3:A:4], T.cf[:, 7:8], None, OP.add, None, ["gn" + u, "cf7"], ["of4" + n])
+        if f:
+            move(f, [(T.ln[:, s], T.of41[:, s])], ["of4" + n], "ar" + n, LIST)
+        else:
+            act(GATHER * 256, T.pl[:, 0:256], T.zt0[:, :].indirect(T.of40[:, s]), AF.Copy, ["of4" + n] + ["zt0%d" % t for t in range(4)], ["pl"])
+            s, v = slice(64 * r + 64, 64 * r + 128), slice(128 * r, 128 * r + 64)
+            quant(128, T.pc[:, 128 * r:128 * r + 128], T.pp[:, 128 * r:128 * r + 128], T.pl[:, :], ["pl", "pz"], ["pc" + n])
+            move(f, [(T.lc[:, s].bitcast(dt.uint8), T.pc[:, v].bitcast(dt.uint8)), (T.lp[:, s], T.pp[:, v])], ["pc" + n], "ar" + n, REMOTE)
         at(r, "parents")
         s4 = slice(8 * r + 4 * f, 8 * r + 4 * f + 4)
         scan(A, T["en" + u][:, :], T["inv" + u][:, 0:A], T.d1[:, 0:A], 2.0 * B, OP.min, OP.add, ["inv" + u, "d1"], ["en" + u])
@@ -317,7 +351,7 @@ def rank_program(g, core, T, topo):
                 cnt["ls"] += h
                 cnt[k] = cnt.get(k, 0) + h
             q.remote_dma_fused(tr, local_sem=T.sem.ls)
-        call("G", move, ["ou0%d" % r, "ou1%d" % r, "pc1%d" % r], ["on%d" % r], (), 0, REMOTE, k)
+        call("G", move, ["ou0%d" % r, "ou1%d" % r, "of41%d" % r], ["on%d" % r], (), 0, REMOTE, k)
 
     def parents_in(k):
         n, s = "%d" % k, slice(16 * k, 16 + 8 * k)
@@ -333,35 +367,42 @@ def rank_program(g, core, T, topo):
                 act(GATHER * A, T.ob[:, o], T.oa[:, o].indirect(T.ox[:, 8 + 4 * f:12 + 4 * f]), AF.Identity, ["ox0", "oa" + u], ["ob" + u],
                     bias=float(A * ((rank - R + 2 * R * f) % N)))
 
-    def renew(h, r):
-        last, u = r == R - 1, "%d" % h
-        n = "%d%d" % (h, r)
-        at(r, "renew" + u)
-        W = [slice(128 * b, 128 * b + 128) for b in range(4)]
-        x, ft = slice(64 * r, 64 * r + 128), T["ft" + u]
-        small = 1.0 / 16 if last else 1.0 / 32
-        FT = ["ft%s%d" % (u, b) for b in range(4)]
+    W = [slice(128 * b, 128 * b + 128) for b in range(4)]
+
+    def renew_left(r):
+        last, x, K = r == R - 1, slice(64 * r, 64 * r + 128), BANKS[0]
+        at(r, "renew0")
+        FT = ["ft0%d" % b for b in range(4)]
 
         def unpack(b, start, stop):
-            mm(BANKS[h][b], 128, T.eq[:, W[b]], T.es[:, W[b]], T["lc" + u][:, x], T["lp" + u][:, x], ["lc" + n, "eq", "pad" + u, "pae" + u], start, stop)
+            mm(K[b], 128, T.eq[:, W[b]], T.es[:, W[b]], T.lc[:, x], T.lp[:, x], ["ar0%d" % r, "eq", "pad", "pae"], start, stop)
         for b in range(4):
             unpack(b, True, True)
         for b in range(4):
-            o, i, k = ft[:, 256 + b:512:4], psum(BANKS[h][b], 64, 128), BANKS[h][b]
-            if b % 2 or not h:
-                act(A, o, i, AF.Copy, [], [FT[b]], [k], scale=small)
-            else:
-                ts(A, o, i, small, None, OP.mult, None, [], [FT[b]], [k])
-        quant(128, T["fq" + u][:, :], T["fs" + u][:, :], ft[:, :], FT + ["fz" + u], ["fq" + u])
-        act(256, T["fh" + u][:, :], ft[:, 256:512], AF.Copy, FT, ["fh" + u], scale=32.0)
+            act(A, T.ft0[:, 256 + b:512:4], psum(K[b], 64, 128), AF.Copy, [], [FT[b]], [K[b]], scale=1.0 / 16 if last else 1.0 / 32)
+        quant(128, T.fq0[:, :], T.fs0[:, :], T.ft0[:, :], FT + ["fz0"], ["fq0"])
+        act(256, T.fh[:, :], T.ft0[:, 256:512], AF.Copy, FT, ["fh"], scale=32.0)
         for b in range(4):
             unpack(b, True, False)
             if last:
                 unpack(b, False, False)
         for b in range(4):
-            k = BANKS[h][b]
-            mm(k, 128, T.wq[:, W[b]], T.wp[:, W[b]], T["fq" + u][:, :], T["fs" + u][:, :], ["wq", "wp", "fq" + u], False, True)
-            tt(A, T.bt[:, 256 * h + b:256 * h + 256:4], psum(k, 64, 128), T["fh" + u][:, b:256:4], OP.max, ["fh" + u], ["b%s%d" % (u, b)], [k])
+            mm(K[b], 128, T.wq[:, W[b]], T.wp[:, W[b]], T.fq0[:, :], T.fs0[:, :], ["wq", "wp", "fq0"], False, True)
+            tt(A, T.bt[:, b:256:4], psum(K[b], 64, 128), T.fh[:, b:256:4], OP.max, ["fh"], ["b0%d" % b], [K[b]])
+
+    def renew_right(r):
+        x, K = slice(C * r, C * r + C), [BANKS[1][b] for b in (3, 1, 0, 2)]
+        at(r, "unpack")
+        for b in range(4):
+            mm(K[b], C, T.eq[:, W[b]], T.es[:, W[b]], T.yc[:, x], T.yp[:, x], ["ay%d" % r, "eq"])
+            act(C, T.yd[:, b:4 * C:4], psum(K[b], 0, C), AF.Copy, [], ["yd%d" % b], [K[b]], scale=2.0 if r == R - 1 else 1.0)
+        at(r, "renew1")
+        act(GATHER * 256, T.ft1[:, 256:512], T.yd[:, :].indirect(T.ln[:, 16 * r:16 * r + 16]), AF.Copy, ["ar1%d" % r] + ["yd%d" % b for b in range(4)], ["ft1"])
+        quant(128, T.fq1[:, :], T.fs1[:, :], T.ft1[:, :], ["ft1", "fz1"], ["fq1"])
+        for b in range(4):
+            mm(K[b], 128, T.wq[:, W[b]], T.wp[:, W[b]], T.fq1[:, :], T.fs1[:, :], ["wq", "wp", "fq1"])
+            act(A, T.rb[:, A * b:A * b + A], psum(K[b], 64, 128), AF.Relu, [], ["rb%d" % b], [K[b]], scale=0.03125)
+            tt(2 * A, T.bt[:, 256 + b:512:4], T.rb[:, A * b:A * b + A], T.ft1[:, 256 + b:512:4], OP.add, ["rb%d" % b, "ft1"], ["b1%d" % b])
 
     for r in range(R):
         at(r, "sides")
@@ -374,8 +415,8 @@ def rank_program(g, core, T, topo):
         parents_out(r)
         if r:
             parents_in(r - 1)
-        for f in range(2):
-            renew(f, r)
+        renew_left(r)
+        renew_right(r)
     at(R, "sides")
 
     quant(128, T.sq[:, :], T.sp[:, :], T.bt[:, :], HALF[0] + HALF[1], ["sq"])

@@ -8,12 +8,12 @@ TILES = [[19, 18, 17], [16, 15, 14, 13], [12, 11, 10, 9], [8, 7, 6, 5], [4, 3, 2
 WIDE = [C, 256, 192, 128, 128]
 AT = [sum(WIDE[:j]) for j in range(6)]
 ALONE = [range(19, 10, -1), range(19, 12, -1)]
-SCANS = [7, 1]
+SCANS = [9, 7]
 QUANT = [[0], [1, 2], [3, 4]]
 WHERE = {c: (j, t) for j in range(5) for t, c in enumerate(TILES[j])}
 BANKS = [[0, 1, 4, 6], [2, 3, 5, 7]]
 FIXED = {"V": 35, "S": 90, "T": 10, "G": 170, "Y": 70}
-GATHER, SCATTER, SIGNAL, LOCAL, LIST, REMOTE, WHOLE, HOLD = 1.5, 3.5, 50, 1400, 1800, 2200, 5000, 60
+GATHER, SCATTER, SIGNAL, LOCAL, LIST, REMOTE, WHOLE, HOLD = 1.5, 3.5, 100, 1400, 1800, 2200, 5000, 60
 
 TURNS = ["sides", "cand0", "score0", "cand1", "score1", "rank0", "tail0", "rank1", "tail1", "renew0", "renew1", "unpack", "parents"]
 
@@ -109,7 +109,7 @@ def rank_program(g, core, T, topo):
         calls.append({"e": e, "f": f, "deps": deps, "behind": behind - deps, "busy": FIXED[e] + busy, "late": late, "sem": sem, "turn": turn[0]})
 
     def vec(n, f, rd, wr, ps):
-        call("V", f, rd, wr, ps, max(64, n) + (70 if ps else 0))
+        call("V", f, rd, wr, ps, max(64, n) + (15 if ps else 0))
 
     def tt(n, o, a, b, how, rd, wr, ps=()):
         vec(n, lambda q: q.tensor_tensor(o, a, b, how), rd, wr, ps)
@@ -136,7 +136,7 @@ def rank_program(g, core, T, topo):
         call("S", lambda q: q.activation(o, i, func, **kw), rd, wr, ps, n + (24 if "accum_out" in kw else 0))
 
     def mm(b, n, w, ws, x, xs, rd, start=True, stop=True):
-        call("T", lambda q: q.matmul_mx(T.ps[:, 512 * b:512 * b + n], w, ws, x, xs, start, stop), rd, [], [b], 0.7 * n, 30)
+        call("T", lambda q: q.matmul_mx(T.ps[:, 512 * b:512 * b + n], w, ws, x, xs, start, stop), rd, [], [b], 1.05 * n, 30)
 
     def dma(e, n, out, in_, rd, wr, k):
         call(e, lambda q: q.dma_start(out, in_), rd, wr, (), 0, LOCAL + n, k)
@@ -278,8 +278,11 @@ def rank_program(g, core, T, topo):
         for b in (kv, ks):
             mm(b, C, T.st[:, s], T.ss[:, s], T["zq" + u][:, C * r:C * r + C], T["zs" + u][:, C * r:C * r + C], ["st" + u, "ss" + u, "zq%d%d" % (f, r)])
         sc, sg, rk = T["sc" + u], T["sg" + u], T["rk" + u]
-        tt(C, T["mk" + u][:, :], psum(kv, 0, C), T.mb[:, :], OP.add, ["mb"], ["mk" + u], [kv])
-        scan(C, sc[:, :], T.rs[:, :], T["mk" + u][:, :], BIG, OP.add, OP.min, ["rs", "mk" + u], ["sc" + u])
+        cut = 0 if f else 16 * min(ALONE[f])
+        for n, lo, hi in (("sc", cut, C), ("sd", 0, cut)):
+            if hi > lo:
+                tt(hi - lo, T["mk" + u][:, lo:hi], psum(kv, lo, hi), T.mb[:, lo:hi], OP.add, ["mb"], ["m" + n + u], [kv])
+                scan(hi - lo, sc[:, lo:hi], T.rs[:, lo:hi], T["mk" + u][:, lo:hi], BIG, OP.add, OP.min, ["rs", "m" + n + u], [n + u])
         w = 16 * (min(ALONE[f]) - 1)
         act(w, T["ap" + u][:, 0:w], psum(ks, 0, w), AF.Copy, [], ["ap" + u], [ks])
         at(r, "rank" + u)
@@ -287,7 +290,7 @@ def rank_program(g, core, T, topo):
             act(16 * c, sg[:, C * i:C * i + 16 * c], psum(ks, 0, 16 * c), AF.Sign, ["sc" + u], ["sg%s%d" % (u, c)], [ks],
                 bias=sc[:, 16 * c + 15:16 * c + 16], scale=-1.0)
         de, jk, a = T["de" + u], T["jk" + u], SCANS[f] + 1
-        tt(C, T["ut" + u][:, 3:4 * C:4], psum(kv, 0, C), sc[:, :], OP.is_gt, ["sc" + u], ["u%d03" % f], [kv])
+        tt(C, T["ut" + u][:, 3:4 * C:4], psum(kv, 0, C), sc[:, :], OP.is_gt, ["sc" + u, "sd" + u], ["u%d03" % f], [kv])
         for c in range(19, 0, -1):
             w, sums = 16 * c, "rk%d%d" % (f, c)
             o, n = slot(f, c, 0, w)
@@ -295,7 +298,7 @@ def rank_program(g, core, T, topo):
                 i = C * ALONE[f].index(c)
                 act(w, o, sg[:, i:i + w], AF.Relu, ["sg%s%d" % (u, c)], n + [sums], accum_out=rk[:, c:c + 1])
                 continue
-            ts(w, o, T["ap" + u][:, 0:w], sc[:, w + 15:w + 16], None, OP.is_lt, None, ["sc" + u, "ap" + u], n)
+            ts(w, o, T["ap" + u][:, 0:w], sc[:, w + 15:w + 16], None, OP.is_lt, None, ["sc" + u, "sd" + u, "ap" + u], n)
             if c >= a:
                 act(w, jk[:, C * c:C * c + w], o, AF.Copy, n, ["jk%d%d" % (f, c), sums], accum_out=rk[:, c:c + 1])
         for c in range(a - 1, 0, -1):

@@ -7,13 +7,14 @@ B = 1536
 TILES = [[19, 18, 17], [16, 15, 14, 13], [12, 11, 10, 9], [8, 7, 6, 5], [4, 3, 2, 1]]
 WIDE = [C, 256, 192, 128, 128]
 AT = [sum(WIDE[:j]) for j in range(6)]
-ALONE = [range(19, 10, -1), range(19, 12, -1)]
-SCANS = [9, 7]
+ALONE = [range(19, 11, -1), range(19, 11, -1)]
+SHARE, ADDING = 10, 2400
+SCANS = [9, 6]
 QUANT = [[0], [1, 2], [3, 4]]
 WHERE = {c: (j, t) for j in range(5) for t, c in enumerate(TILES[j])}
 BANKS = [[0, 1, 4, 6], [2, 3, 5, 7]]
-FIXED = {"V": 35, "S": 90, "T": 10, "G": 170, "Y": 70}
-GATHER, SCATTER, SIGNAL, LOCAL, LIST, REMOTE, WHOLE, HOLD = 1.5, 3.5, 100, 1400, 1800, 2200, 5000, 60
+FIXED = {"V": 25, "S": 45, "T": 10, "G": 170, "Y": 70}
+GATHER, SCATTER, SIGNAL, LOCAL, LIST, REMOTE, WHOLE, HOLD = 1.5, 3.5, 230, 1400, 1500, 2000, 5000, 60
 
 TURNS = ["sides", "cand0", "score0", "cand1", "score1", "rank0", "tail0", "rank1", "tail1", "renew0", "renew1", "unpack", "parents"]
 
@@ -27,24 +28,24 @@ def sbuf(kind, **names):
 
 BF, F4, I4, U2, Q8, U1 = "bfloat16", "float32", "int32", "uint16", "float8_e4m3fn_x4", "uint8"
 sbuf(I4, li=80, pki=16, qi=4, qj=4, oi=24, oj=24)
-sbuf(U2, pk=16, off=320, ox=24)
-sbuf(BF, xt=4 * C, lr=512, bt=512, vt=512, et=2048, a1=512, a2=128, aw=1024, zz=512, r16=C, mb=C, rs=C, h16=C)
+sbuf(U2, pk=16, off=320, ox=24, on=24)
+sbuf(BF, xt=4 * C, lr=512, bt=512, vt=512, et=2048, a1=512, a2=128, aw=1024, zz=512, r16=C, mb=C, rs=C)
 sbuf(Q8, vq=128, eq=512, aq=256, zc=128, wq=512, sq=128, st=256)
 sbuf(U1, vs=128, es=512, ax=256, zp=128, wp=512, sp=128, ss=256)
-sbuf(F4, yo=128, cf=8, yy=C, y4=A, i4=C, wj=256, d1=C, d4=A, ou=24, on=24, oa=128, ob=128, of=128)
+sbuf(F4, yo=128, cf=8, yy=C, y4=A, i4=C, wj=256, kc=C, d4=A, ou=24, oa=128, ob=128, of=128)
 SCRATCH["ps"] = ("psum", [128, 4096], F4)
 for _f in "01":
-    sbuf(BF, **{"xg" + _f: 4 * C, "zt" + _f: 4 * C, "ft" + _f: 512, "ut" + _f: 4 * AT[5], "jk" + _f: 20 * C, "sg" + _f: 12 * C, "de" + _f: C})
-    sbuf(F4, **{"mk" + _f: C, "ap" + _f: C, "sc" + _f: C, "rk" + _f: 20, "ry" + _f: 20, "rr" + _f: 20, "dd" + _f: C, "vv" + _f: C, "inv" + _f: C, "gn" + _f: A, "en" + _f: A})
+    sbuf(BF, **{"xg" + _f: 4 * C, "zt" + _f: 4 * C, "ft" + _f: 512, "ut" + _f: 4 * AT[5], "jk" + _f: 20 * C, "sg" + _f: 12 * C})
+    sbuf(F4, **{"mk" + _f: C, "sc" + _f: C, "rk" + _f: 20, "de" + _f: C, "d1" + _f: C, "dd" + _f: C, "vv" + _f: C, "inv" + _f: C, "gn" + _f: A, "en" + _f: A})
     sbuf(U2, **{"ro" + _f: 20, "of4" + _f: 16 * R})
     sbuf(Q8, **{"zq" + _f: C * R, "uq" + _f: AT[5], "fq" + _f: 128})
     sbuf(U1, **{"zs" + _f: C * R, "us" + _f: AT[5], "fs" + _f: 128})
-sbuf(BF, pl=512, fh=256, yd=4 * C)
+sbuf(BF, zl=4 * C, pl=512, fh=256, yd=4 * C)
 sbuf(F4, rb=256)
 sbuf(U2, ln=16 * R)
 sbuf(Q8, pc=128 * R, lc=256, yc=C * R)
 sbuf(U1, pp=128 * R, lp=256, yp=C * R)
-SEMAPHORES = ["sV", "sS", "sT", "sG", "ls", "dl", "d0", "dx", "dw", "dv", "dz", "du", "dy", "do", "ao0", "ao1"]
+SEMAPHORES = ["sV", "sS", "sT", "sG", "ls", "dl", "d0", "d1", "dx", "dw", "dv", "dz", "du", "dg", "da1", "da2", "dy", "do", "ao0", "ao1"]
 SEMAPHORES += [_k + "%d" % _r for _k in ("ar0", "ar1", "ay") for _r in range(R)]
 
 
@@ -79,7 +80,7 @@ def rank_program(g, core, T, topo):
         return
     OP, AF = AluOpType, ActivationFunctionType
     Q = {"V": g.vector, "S": g.scalar, "T": g.tensor, "G": g, "Y": g.sync}
-    calls, lastw, readers, bank, group, turn = [], {}, {}, {}, {}, [0]
+    calls, lastw, readers, bank, group, turn, moved, gate = [], {}, {}, {}, {}, [0], [0], {}
 
     def call(e, f, rd, wr, ps, busy, late=0.0, sem=None):
         i = len(calls)
@@ -99,6 +100,8 @@ def rank_program(g, core, T, topo):
                 deps |= set(group[calls[j]["sem"]])
         if e == "Y" and "Y" in lastw:
             behind.add(lastw["Y"])
+        if e in gate:
+            behind.add(gate[e])
         lastw[e] = i
         for r in rd:
             readers.setdefault(r, []).append(i)
@@ -109,7 +112,7 @@ def rank_program(g, core, T, topo):
         calls.append({"e": e, "f": f, "deps": deps, "behind": behind - deps, "busy": FIXED[e] + busy, "late": late, "sem": sem, "turn": turn[0]})
 
     def vec(n, f, rd, wr, ps):
-        call("V", f, rd, wr, ps, max(64, n) + (15 if ps else 0))
+        call("V", f, rd, wr, ps, max(64, n))
 
     def tt(n, o, a, b, how, rd, wr, ps=()):
         vec(n, lambda q: q.tensor_tensor(o, a, b, how), rd, wr, ps)
@@ -136,10 +139,11 @@ def rank_program(g, core, T, topo):
         call("S", lambda q: q.activation(o, i, func, **kw), rd, wr, ps, n + (24 if "accum_out" in kw else 0))
 
     def mm(b, n, w, ws, x, xs, rd, start=True, stop=True):
-        call("T", lambda q: q.matmul_mx(T.ps[:, 512 * b:512 * b + n], w, ws, x, xs, start, stop), rd, [], [b], 1.05 * n, 30)
+        call("T", lambda q: q.matmul_mx(T.ps[:, 512 * b:512 * b + n], w, ws, x, xs, start, stop), rd, [], [b], 0.6 * n, 30)
 
     def dma(e, n, out, in_, rd, wr, k):
-        call(e, lambda q: q.dma_start(out, in_), rd, wr, (), 0, LOCAL + n, k)
+        moved[0] = n + (0 if rd else moved[0])
+        call(e, lambda q: q.dma_start(out, in_), rd, wr, (), 0, LOCAL + moved[0], k)
 
     def iota(n, o, pattern, base, mult, wr, **kw):
         call("G", lambda q: q.iota(o, pattern, base, mult, **kw), [], wr, (), 2 * n)
@@ -159,15 +163,17 @@ def rank_program(g, core, T, topo):
 
     for i, nm in enumerate(("la", "lx", "ra", "rx")):
         dma("S", 80, T.li[:, 20 * i:20 * i + 20], T[nm][:, :], [], [LI[i]], "dl")
-    dma("Y", 2560, T.xt[:, :], T.x[:, :], [], ["xt"], "dx")
     dma("Y", 512, T.lr[:, 0:256], T.l0[:, :], [], ["lr0"], "d0")
-    dma("Y", 512, T.lr[:, 256:512], T.r0[:, :], [], ["lr1"], "d0")
+    dma("Y", 2560, T.xt[:, :], T.x[:, :], [], ["xt"], "dx")
+    dma("Y", 512, T.lr[:, 256:512], T.r0[:, :], [], ["lr1"], "d1")
 
     big = {"allow_small_or_imprecise_dtypes": True}
     iota(1, T.qi[:, 3:4], [[1, 1]], 0, 1, ["qi"])
     iota(8, T.pki[:, 0:8], [[8, 8]], 64, 0, ["pki"])
     iota(8, T.pki[:, 8:16], [[8, 8]], 0, 0, ["pki2"])
     iota(C, T.r16[:, :], [[0, 20], [1, 16]], 0, 0, ["r16"], **big)
+    iota(C, T.i4[:, :], [[4, C]], 0, 0, ["i4"], **big)
+    iota(C, T.yy[:, :], [[0, 20], [-2 * B, 16]], 0, 0, ["yy"], **big)
     fill(256, T.zz[:, :], 0.0, ["zz"])
     at(0, "rank0")
     select(T.a1[:, :], T.zz[:, :], [[-16, 8], [0, 64]], OP.is_ge, 1.0, -16, 1, ["zz"], ["a1"])
@@ -177,15 +183,19 @@ def rank_program(g, core, T, topo):
     select(T.aw[:, 3:512:4], T.a2[:, :], [[-16, 8], [0, 16]], OP.is_ge, 0.0, 0, 1, ["a2"], ["aw0"])
     quant(256, T.aq[:, :], T.ax[:, :], T.aw[:, :], ["aw0", "aw1"], ["aq"])
     at(0, "tail0")
-    iota(C, T.yy[:, :], [[0, 20], [-2 * B, 16]], -B, 0, ["yy"], **big)
-    iota(A, T.y4[:, :], [[0, 16], [-2 * B, 4]], -B, 0, ["y4"], **big)
-    iota(C, T.i4[:, :], [[4, C]], 0, 0, ["i4"], **big)
+    iota(C, T.kc[:, :], [[16, 20], [0, 16]], 17 * B, 0, ["kc"], **big)
+    iota(A, T.y4[:, :], [[0, 16], [-2 * B, 4]], 0, 0, ["y4"], **big)
     quant(128, T.zc[:, :], T.zp[:, :], T.zz[:, :], ["zz"], ["zc"])
     for f in range(2):
         u = "%d" % f
         for j in range(5):
             a = 4 * (AT[j] + 16 * TILES[j][-1])
-            dma("Y", 512, T["ut" + u][:, a:4 * AT[j + 1]], T.zz[:, 0:4 * AT[j + 1] - a], ["zz"], ["u%d%d%d" % (f, j, t) for t in range(4)], "du")
+            o, wr = T["ut" + u][:, a:4 * AT[j + 1]], ["u%d%d%d" % (f, j, t) for t in range(4)]
+            at(0, "rank" + u)
+            if f:
+                dma("Y", 512, o, T.zz[:, 0:4 * AT[j + 1] - a], ["zz"], wr, "du")
+            else:
+                fill(2 * AT[j + 1] - a / 2, o, 0.0, wr)
     dma("Y", 2048, T.wq[:, :].bitcast(dt.uint8), T.wc[:, :], [], ["wq"], "dw")
     dma("Y", 512, T.wp[:, :], T.ws[:, :], [], ["wp"], "dw")
     dma("Y", 1024, T.vt[:, :], T.v[:, :], [], ["vt"], "dv")
@@ -209,12 +219,14 @@ def rank_program(g, core, T, topo):
     ts(1, T.cf[:, 7:8], T.cf[:, 6:7], T.cf[:, 2:3], None, OP.add, None, ["cf0", "cf5"], ["cf7"])
     ts(1, T.cf[:, 5:6], T.cf[:, 5:6], T.cf[:, 0:1], None, OP.add, None, ["cf0", "cf5"], ["cf5"])
     ts(160, T.mb[:, :], T.r16[:, :], T.cf[:, 0:1], BIG, OP.not_equal, OP.mult, ["r16", "cf0"], ["mb"])
-    ts(160, T.h16[:, :], T.r16[:, :], 0.0, None, OP.is_gt, None, ["r16"], ["h16"])
     at(0, "tail0")
-    ts(C, T.d1[:, :], T.yy[:, :], T.cf[:, 3:4], -1.0 * B, OP.add, OP.max, ["yy", "cf3"], ["d1"])
-    iota(20, T.d1[:, 15:C:16], [[16, 20]], 17 * B, 0, ["d1"], **big)
-    ts(A, T.d4[:, :], T.y4[:, :], T.cf[:, 4:5], -1.0 * B, OP.add, OP.max, ["y4", "cf3"], ["d4"])
+    act(C, T.yy[:, :], T.yy[:, :], AF.Relu, ["cf3"], ["yy"], bias=T.cf[:, 3:4])
+    for f in range(2):
+        act(C, T["d1%d" % f][:, :], T.yy[:, :], AF.Identity, ["yy"], ["rx%d" % f, "ry%d" % f], bias=-1.0 * B)
+    act(A, T.y4[:, :], T.y4[:, :], AF.Relu, ["cf3"], ["y4"], bias=T.cf[:, 4:5])
+    act(A, T.d4[:, :], T.y4[:, :], AF.Identity, ["y4"], ["d4"], bias=-1.0 * B)
     iota(16, T.d4[:, 3:A:4], [[0, 16]], 5 * B, 0, ["d4"], **big)
+    at(0, "score1")
     act(256, T.wj[:, :], T.i4[:, 0:256], AF.Copy, ["i4"], ["wj"], scale=2.0 ** -12)
     at(0, "renew0")
     for b in range(4):
@@ -226,20 +238,21 @@ def rank_program(g, core, T, topo):
     turn[0] = 0
     for t in range(4):
         ts(80, T.off[:, 80 * t:80 * t + 80], T.li[:, :], 4.0, float(t), OP.mult, OP.add, LI, ["ot%d" % t])
-    act(256, T.bt[:, 0:256], T.lr[:, 0:256], AF.Copy, ["lr0"], HALF[0], scale=0.5)
     act(256, T.bt[:, 256:512], T.lr[:, 256:512], AF.Copy, ["lr1"], HALF[1], scale=0.5)
-    for f in range(2):
-        u = "%d" % f
-        at(0, "cand" + u)
+    for t in range(4):
+        act(GATHER * C, T.zl[:, C * t:C * t + C], T.lr[:, 0:256].indirect(T.off[:, 80 * t:80 * t + 20]), AF.Copy, ["lr0", "ot%d" % t], ["zl%d" % t])
+
+    def halves(f, rd):
         for t in range(4):
-            o = T["xg" + u][:, C * t:C * t + C]
-            w = T.xt[:, :].indirect(T.off[:, 80 * t + 40 * f + 20:80 * t + 40 * f + 40])
-            if f or t:
-                act(GATHER * C, o, w, AF.Copy, ["xt", "ot%d" % t], ["xg%d%d" % (f, t)], scale=0.5)
-            else:
-                ts(GATHER * C, o, w, 0.5, None, OP.mult, None, ["xt", "ot%d" % t], ["xg%d%d" % (f, t)])
-        at(0, "tail" + u)
-        tt(GATHER * C, T["vv" + u][:, :], T.wj[:, :].indirect(T.off[:, 40 * f:40 * f + 20]), T.i4[:, :], OP.add, ["wj", "ot0", "i4"], ["vv" + u])
+            act(GATHER * C, T["xg%d" % f][:, t:4 * C:4], T.xt[:, :].indirect(T.off[:, 80 * t + 40 * f + 20:80 * t + 40 * f + 40]), AF.Copy,
+                ["xt", "ot%d" % t] + rd, ["xg%d%d" % (f, t)], scale=0.5)
+    at(0, "cand1")
+    halves(1, [])
+    at(0, "score1")
+    for f in range(2):
+        act(GATHER * C, T["vv%d" % f][:, :], T.wj[:, :].indirect(T.off[:, 40 * f:40 * f + 20]), AF.Copy, ["wj", "ot0"], ["vv%d" % f])
+    for f in range(2):
+        call("G", lambda q, f=f: q.dma_start(T["vv%d" % f][:, :], T.i4[:, :], accum_op=OP.add), ["i4"], ["vv%d" % f], (), 400, 3000, "dg")
 
     def move(f, pairs, rd, k, late):
         d = T.cores[(rank + 1 - 2 * f) % N]
@@ -256,11 +269,20 @@ def rank_program(g, core, T, topo):
     def candidates(f, r):
         u = "%d" % f
         at(r, "cand" + u)
+        k = SHARE if r and f else 0
+        zt, xg, fam, ZU = T["zt" + u], T["xg" + u], T.bt[:, 256 * f:256 * f + 256], ["zu%d" % t for t in range(4)] if f else []
         for t in range(4):
-            w = T.bt[:, 256 * f:256 * f + 256].indirect(T.off[:, 80 * t + 40 * f:80 * t + 40 * f + 20])
-            tt(GATHER * C, T["zt" + u][:, t:4 * C:4], w, T["xg" + u][:, C * t:C * t + C], OP.add, HALF[f] + ["ot%d" % t, "xg%d%d" % (f, t)], ["zt%d%d" % (f, t)])
+            o, z = 80 * t + 40 * f, slice(64 * k + t, 4 * C, 4)
+            if k:
+                act(GATHER * 16 * k, zt[:, t:64 * k:4], fam.indirect(T.off[:, o:o + k]), AF.Copy, HALF[f] + ["ot%d" % t], [ZU[t]])
+            if r or f:
+                tt(GATHER * (C - 16 * k) + 30, zt[:, z], fam.indirect(T.off[:, o + k:o + 20]), xg[:, z], OP.add, HALF[f] + ["ot%d" % t, "xg%d%d" % (f, t)], ["zt%d%d" % (f, t)])
+            else:
+                tt(GATHER * C + 30, zt[:, z], T.xt[:, :].indirect(T.off[:, o + 20:o + 40]), T.zl[:, C * t:C * t + C], OP.add, ["xt", "zl%d" % t], ["zt0%d" % t])
+        if k:
+            call("G", lambda q: q.dma_start(zt[:, 0:64 * k], xg[:, 0:64 * k], accum_op=OP.add), ["xg1%d" % t for t in range(4)], ZU, (), 400, ADDING, "da%d" % r)
         s = slice(C * r, C * r + C)
-        quant(C, T["zq" + u][:, s], T["zs" + u][:, s], T["zt" + u][:, :], ["zt" + u + "%d" % t for t in range(4)], ["zq%d%d" % (f, r)])
+        quant(C, T["zq" + u][:, s], T["zs" + u][:, s], zt[:, :], ["zt" + u + "%d" % t for t in range(4)] + ZU, ["zq%d%d" % (f, r)])
         if f:
             move(f, [(T.yc[:, s].bitcast(dt.uint8), T.zq1[:, s].bitcast(dt.uint8)), (T.yp[:, s], T.zs1[:, s])], ["zq1%d" % r], "ay%d" % r, WHOLE)
 
@@ -283,8 +305,6 @@ def rank_program(g, core, T, topo):
             if hi > lo:
                 tt(hi - lo, T["mk" + u][:, lo:hi], psum(kv, lo, hi), T.mb[:, lo:hi], OP.add, ["mb"], ["m" + n + u], [kv])
                 scan(hi - lo, sc[:, lo:hi], T.rs[:, lo:hi], T["mk" + u][:, lo:hi], BIG, OP.add, OP.min, ["rs", "m" + n + u], [n + u])
-        w = 16 * (min(ALONE[f]) - 1)
-        act(w, T["ap" + u][:, 0:w], psum(ks, 0, w), AF.Copy, [], ["ap" + u], [ks])
         at(r, "rank" + u)
         for i, c in enumerate(ALONE[f]):
             act(16 * c, sg[:, C * i:C * i + 16 * c], psum(ks, 0, 16 * c), AF.Sign, ["sc" + u], ["sg%s%d" % (u, c)], [ks],
@@ -298,15 +318,15 @@ def rank_program(g, core, T, topo):
                 i = C * ALONE[f].index(c)
                 act(w, o, sg[:, i:i + w], AF.Relu, ["sg%s%d" % (u, c)], n + [sums], accum_out=rk[:, c:c + 1])
                 continue
-            ts(w, o, T["ap" + u][:, 0:w], sc[:, w + 15:w + 16], None, OP.is_lt, None, ["sc" + u, "sd" + u, "ap" + u], n)
+            ts(w, o, psum(kv, 0, w), sc[:, w + 15:w + 16], None, OP.is_lt, None, ["sc" + u, "sd" + u], n, [kv])
             if c >= a:
                 act(w, jk[:, C * c:C * c + w], o, AF.Copy, n, ["jk%d%d" % (f, c), sums], accum_out=rk[:, c:c + 1])
         for c in range(a - 1, 0, -1):
             o, n = slot(f, c, 0, 16 * c)
             scan(8 * c, jk[:, C * c + C - 16 * c:C * c + C], o, T.zz[:, 0:16 * c], 0.0, OP.add, OP.add, n + ["zz"], ["rk%d%d" % (f, c)])
-        scan(C / 2, de[:, :], T.h16[:, :], T["ut" + u][:, 3:4 * C:4], 0.0, OP.mult, OP.add, ["h16", "u%d03" % f], ["de" + u])
-        tt(40, T["ry" + u][:, 0:a], jk[:, C - 1:C * a:C], de[:, 15:16 * a:16], OP.subtract, ["rk%d%d" % (f, c) for c in range(a)] + ["de" + u], ["rx" + u])
-        tt(40, T["ry" + u][:, a:20], rk[:, a:20], de[:, 16 * a + 15:C:16], OP.subtract, ["rk%d%d" % (f, c) for c in range(a, 20)] + ["de" + u], ["ry" + u])
+        scan(C, de[:, :], T.kc[:, :], T["ut" + u][:, 3:4 * C:4], 0.0, OP.max, OP.add, ["kc", "u%d03" % f], ["de" + u])
+        tt(40, T["d1" + u][:, 15:16 * a:16], de[:, 15:16 * a:16], jk[:, C - 1:C * a:C], OP.subtract, ["rk%d%d" % (f, c) for c in range(a)] + ["de" + u], ["rx" + u])
+        tt(40, T["d1" + u][:, 16 * a + 15:C:16], de[:, 16 * a + 15:C:16], rk[:, a:20], OP.subtract, ["rk%d%d" % (f, c) for c in range(a, 20)] + ["de" + u], ["ry" + u])
         for i, js in enumerate(QUANT):
             s = slice(AT[js[0]], AT[js[-1] + 1])
             quant(s.stop - s.start, T["uq" + u][:, s], T["us" + u][:, s], T["ut" + u][:, 4 * s.start:4 * s.stop],
@@ -320,9 +340,8 @@ def rank_program(g, core, T, topo):
         u, b = "%d" % f, BANKS[f][2]
         n = "%d%d" % (f, r)
         at(r, "tail" + u)
-        scan(C, T["dd" + u][:, :], psum(b, 0, C), T.d1[:, :], 2.0 * B, OP.min, OP.add, ["d1"], ["dd" + u], [b])
-        tt(40, T["rr" + u][:, :], T["dd" + u][:, 15:C:16], T["ry" + u][:, :], OP.subtract, ["rx" + u, "ry" + u, "dd" + u], ["rr" + u])
-        ts(20, T["ro" + u][:, :], T["rr" + u][:, :], T.cf[:, 5:6], None, OP.add, None, ["rr" + u, "cf5"], ["ro" + u])
+        scan(C, T["dd" + u][:, :], psum(b, 0, C), T["d1" + u][:, :], 2.0 * B, OP.min, OP.add, ["rx" + u, "ry" + u], ["dd" + u], [b])
+        ts(20, T["ro" + u][:, :], T["dd" + u][:, 15:C:16], T.cf[:, 5:6], None, OP.add, None, ["dd" + u, "cf5"], ["ro" + u])
         tc(SCATTER * C, T["inv" + u][:, :].indirect(T["ro" + u][:, 0:20]), T["vv" + u][:, :], ["ro" + u, "vv" + u], ["inv" + u])
         scan(A, T["gn" + u][:, :], T["inv" + u][:, 0:A], T.d4[:, :], 2.0 * B, OP.min, OP.add, ["inv" + u, "d4"], ["gn" + u])
         s = slice(16 * r, 16 * r + 16)
@@ -330,17 +349,21 @@ def rank_program(g, core, T, topo):
         if f:
             move(f, [(T.ln[:, s], T.of41[:, s])], ["of4" + n], "ar" + n, LIST)
         else:
-            act(GATHER * 256, T.pl[:, 0:256], T.zt0[:, :].indirect(T.of40[:, s]), AF.Copy, ["of4" + n] + ["zt0%d" % t for t in range(4)], ["pl"])
+            act(GATHER * 256, T.pl[:, 0:256], T.zt0[:, :].indirect(T.of40[:, s]), AF.Copy, ["of4" + n] + ["zt0%d" % t for t in range(4)], ["pl"],
+                scale=1.0 if r else 0.5)
             s, v = slice(64 * r + 64, 64 * r + 128), slice(128 * r, 128 * r + 64)
             quant(128, T.pc[:, 128 * r:128 * r + 128], T.pp[:, 128 * r:128 * r + 128], T.pl[:, :], ["pl", "pz"], ["pc" + n])
             move(f, [(T.lc[:, s].bitcast(dt.uint8), T.pc[:, v].bitcast(dt.uint8)), (T.lp[:, s], T.pp[:, v])], ["pc" + n], "ar" + n, REMOTE)
-        at(r, "parents")
+        at(r, "parents" if r < R - 1 else "tail1")
         s4 = slice(8 * r + 4 * f, 8 * r + 4 * f + 4)
-        scan(A, T["en" + u][:, :], T["inv" + u][:, 0:A], T.d1[:, 0:A], 2.0 * B, OP.min, OP.add, ["inv" + u, "d1"], ["en" + u])
+        scan(A, T["en" + u][:, :], T["inv" + u][:, 0:A], T["d1" + u][:, 0:A], 2.0 * B, OP.min, OP.add, ["inv" + u, "rx" + u, "ry" + u], ["en" + u])
         act(4, T.ou[:, s4], T["en" + u][:, 15:A:16], AF.Copy, ["en" + u], ["ou" + n], scale=256.0)
 
     def parents_out(r):
-        k = "ao%d" % (r // (R - 1))
+        k, s = "ao%d" % (r // (R - 1)), slice(8 * r, 8 * r + 8)
+        tc(8, T.oi[:, s], T.ou[:, s], ["ou0%d" % r, "ou1%d" % r], ["oi%d" % r])
+        ts(8, T.oj[:, s], T.oi[:, s], 255, None, OP.bitwise_and, None, ["oi%d" % r], ["oj%d" % r])
+        tc(8, T.ox[:, s], T.oj[:, s], ["oj%d" % r], ["ox%d" % r])
 
         def move(q):
             tr = []
@@ -350,24 +373,20 @@ def rank_program(g, core, T, topo):
                 en = topo.engines(core, d)
                 h, s = len(en) // 2, slice(8 * r + 4 * f, 8 * r + 4 * f + 4)
                 tr.append(RemoteDMATransfer(dst_ids=[DstId(rid=rid, pnc=pid)], dma_engine_mask=sum(1 << e for e in en[h * f:h * f + h]),
-                                            remote_sem=T.sem[k], src=T.ou[:, s], dst=T.on[:, s]))
+                                            remote_sem=T.sem[k], src=T.ox[:, s], dst=T.on[:, s]))
                 cnt["ls"] += h
                 cnt[k] = cnt.get(k, 0) + h
             q.remote_dma_fused(tr, local_sem=T.sem.ls)
-        call("G", move, ["ou0%d" % r, "ou1%d" % r, "of41%d" % r], ["on%d" % r], (), 0, REMOTE, k)
+        call("G", move, ["ox%d" % r, "of41%d" % r], ["on%d" % r], (), 0, LIST, k)
 
     def parents_in(k):
-        n, s = "%d" % k, slice(16 * k, 16 + 8 * k)
-        tc(16, T.oi[:, s], T.on[:, s], ["on%d" % (k + 1)], ["oi" + n])
-        ts(16, T.oj[:, s], T.oi[:, s], 255, None, OP.bitwise_and, None, ["oi" + n], ["oj" + n])
-        tc(16, T.ox[:, s], T.oj[:, s], ["oj" + n], ["ox" + n])
         for f in range(2):
             u, o = "%d" % f, slice(A * f, A * f + A)
             if k:
-                act(GATHER * A, T.of[:, o], T.ob[:, o].indirect(T.ox[:, 16 + 4 * f:20 + 4 * f]), AF.Copy, ["ox1", "ob" + u], ["of" + u])
+                act(GATHER * A, T.of[:, o], T.ob[:, o].indirect(T.on[:, 16 + 4 * f:20 + 4 * f]), AF.Copy, ["on2", "ob" + u], ["of" + u])
             else:
-                act(GATHER * A, T.oa[:, o], T.i4[:, 0:A].indirect(T.ox[:, 4 * f:4 + 4 * f]), AF.Copy, ["ox0", "i4"], ["oa" + u], scale=0.25)
-                act(GATHER * A, T.ob[:, o], T.oa[:, o].indirect(T.ox[:, 8 + 4 * f:12 + 4 * f]), AF.Identity, ["ox0", "oa" + u], ["ob" + u],
+                act(GATHER * A, T.oa[:, o], T.i4[:, 0:A].indirect(T.on[:, 4 * f:4 + 4 * f]), AF.Copy, ["on1", "i4"], ["oa" + u], scale=0.25)
+                act(GATHER * A, T.ob[:, o], T.oa[:, o].indirect(T.on[:, 8 + 4 * f:12 + 4 * f]), AF.Identity, ["on1", "oa" + u], ["ob" + u],
                     bias=float(A * ((rank - R + 2 * R * f) % N)))
 
     W = [slice(128 * b, 128 * b + 128) for b in range(4)]
@@ -409,18 +428,34 @@ def rank_program(g, core, T, topo):
 
     for r in range(R):
         at(r, "sides")
-        quant(128, T.sq[:, :], T.sp[:, :], T.bt[:, :], HALF[0] + HALF[1], ["sq"])
+        if r:
+            quant(128, T.sq[:, :], T.sp[:, :], T.bt[:, :], HALF[0] + HALF[1], ["sq"])
+        else:
+            quant(128, T.sq[:, :], T.sp[:, :], T.lr[:, :], ["lr0", "lr1"], ["sq"])
         for f in range(2):
             candidates(f, r)
             order(f, r)
+        lastw["sums"] = lastw["T"]
+        if r == R - 1:
+            at(r, "parents")
+            gate.update(S=lastw["sg0%d" % min(ALONE[0])])
+            parents_in(0)
+            gate.clear()
         for f in range(2):
             survive(f, r)
+        if r == 0:
+            at(r, "renew0")
+            halves(0, ["ry1"])
+            at(r, "parents")
         parents_out(r)
-        if r:
-            parents_in(r - 1)
+        gate.update(T=lastw["sums"], V=lastw["of41%d" % r])
         renew_left(r)
         renew_right(r)
+        gate.clear()
     at(R, "sides")
+    gate.update(S=lastw["rb3"])
+    parents_in(1)
+    gate.clear()
 
     quant(128, T.sq[:, :], T.sp[:, :], T.bt[:, :], HALF[0] + HALF[1], ["sq"])
     dma("Y", 512, T.ot[:, :], T.of[0:128:16, :], ["of0", "of1"], [], "do")

from concourse.bass import DstId, RemoteDMATransfer
from concourse.mybir import dt, AluOpType, ActivationFunctionType

N, C, A, R = 8, 320, 64, 3
BIG = 2.0 ** 90
B = 1536
TILES = [[19, 18, 17], [16, 15, 14, 13], [12, 11, 10, 9], [8, 7, 6, 5], [4, 3, 2, 1]]
WIDE = [C, 256, 192, 128, 128]
AT = [sum(WIDE[:j]) for j in range(6)]
ALONE = [range(19, 11, -1), range(19, 11, -1)]
SHARE, ADDING = 10, 2400
SCANS = [9, 6]
QUANT = [[0], [1, 2], [3, 4]]
WHERE = {c: (j, t) for j in range(5) for t, c in enumerate(TILES[j])}
BANKS = [[0, 1, 4, 6], [2, 3, 5, 7]]
FIXED = {"V": 25, "S": 45, "T": 10, "G": 170, "Y": 70}
GATHER, SCATTER, SIGNAL, LOCAL, LIST, REMOTE, WHOLE, HOLD = 1.5, 3.5, 230, 1400, 1500, 2000, 5000, 60

TURNS = ["sides", "cand0", "score0", "cand1", "score1", "rank0", "tail0", "rank1", "tail1", "renew0", "renew1", "unpack", "parents"]

SCRATCH = {}


def sbuf(kind, **names):
    for k, n in names.items():
        SCRATCH[k] = ("sbuf", [128, n], kind)


BF, F4, I4, U2, Q8, U1 = "bfloat16", "float32", "int32", "uint16", "float8_e4m3fn_x4", "uint8"
sbuf(I4, li=80, pki=16, qi=4, qj=4, oi=24, oj=24)
sbuf(U2, pk=16, off=320, ox=24, on=24)
sbuf(BF, xt=4 * C, lr=512, bt=512, vt=512, et=2048, a1=512, a2=128, aw=1024, zz=512, r16=C, mb=C, rs=C)
sbuf(Q8, vq=128, eq=512, aq=256, zc=128, wq=512, sq=128, st=256)
sbuf(U1, vs=128, es=512, ax=256, zp=128, wp=512, sp=128, ss=256)
sbuf(F4, yo=128, cf=8, yy=C, y4=A, i4=C, wj=256, kc=C, d4=A, ou=24, oa=128, ob=128, of=128)
SCRATCH["ps"] = ("psum", [128, 4096], F4)
for _f in "01":
    sbuf(BF, **{"xg" + _f: 4 * C, "zt" + _f: 4 * C, "ft" + _f: 512, "ut" + _f: 4 * AT[5], "jk" + _f: 20 * C, "sg" + _f: 12 * C})
    sbuf(F4, **{"mk" + _f: C, "sc" + _f: C, "rk" + _f: 20, "de" + _f: C, "d1" + _f: C, "dd" + _f: C, "vv" + _f: C, "inv" + _f: C, "gn" + _f: A, "en" + _f: A})
    sbuf(U2, **{"ro" + _f: 20, "of4" + _f: 16 * R})
    sbuf(Q8, **{"zq" + _f: C * R, "uq" + _f: AT[5], "fq" + _f: 128})
    sbuf(U1, **{"zs" + _f: C * R, "us" + _f: AT[5], "fs" + _f: 128})
sbuf(BF, zl=4 * C, pl=512, fh=256, yd=4 * C)
sbuf(F4, rb=256)
sbuf(U2, ln=16 * R)
sbuf(Q8, pc=128 * R, lc=256, yc=C * R)
sbuf(U1, pp=128 * R, lp=256, yp=C * R)
SEMAPHORES = ["sV", "sS", "sT", "sG", "ls", "dl", "d0", "d1", "dx", "dw", "dv", "dz", "du", "dg", "da1", "da2", "dy", "do", "ao0", "ao1"]
SEMAPHORES += [_k + "%d" % _r for _k in ("ar0", "ar1", "ay") for _r in range(R)]


def arrange(calls):
    after = [[] for _ in calls]
    for i, c in enumerate(calls):
        for d in c["deps"] | c["behind"]:
            after[d].append(i)
    left = [len(c["deps"] | c["behind"]) for c in calls]
    ready, free, order = [0.0] * len(calls), {e: 0.0 for e in FIXED}, []
    todo = {i for i in range(len(calls)) if not left[i]}
    while todo:
        first = min(todo, key=lambda i: (max(ready[i], free[calls[i]["e"]]), i))
        e = calls[first]["e"]
        now = max(ready[first], free[e])
        i = min([j for j in todo if calls[j]["e"] == e and ready[j] <= now + HOLD], key=lambda j: (calls[j]["turn"], j))
        todo.remove(i)
        order.append(i)
        start = max(now, ready[i])
        free[e] = start + calls[i]["busy"]
        for j in after[i]:
            ready[j] = max(ready[j], free[e] + calls[i]["late"] + SIGNAL if i in calls[j]["deps"] else start)
            left[j] -= 1
            if not left[j]:
                todo.add(j)
    return order


def rank_program(g, core, T, topo):
    rank = T.rank_of(core)
    if rank is None:
        return
    OP, AF = AluOpType, ActivationFunctionType
    Q = {"V": g.vector, "S": g.scalar, "T": g.tensor, "G": g, "Y": g.sync}
    calls, lastw, readers, bank, group, turn, moved, gate = [], {}, {}, {}, {}, [0], [0], {}

    def call(e, f, rd, wr, ps, busy, late=0.0, sem=None):
        i = len(calls)
        deps = {lastw[r] for r in list(rd) + list(wr) if r in lastw}
        for w in wr:
            deps |= set(readers.get(w, []))
        behind = set()
        for p in ps:
            for j in bank.get(p, []):
                if calls[j]["e"] != e:
                    deps.add(j)
                elif e == "T":
                    behind.add(j)
            bank[p] = [i] if e == "T" else bank.get(p, []) + [i]
        for j in list(deps):
            if calls[j]["sem"] and calls[j]["sem"] != sem:
                deps |= set(group[calls[j]["sem"]])
        if e == "Y" and "Y" in lastw:
            behind.add(lastw["Y"])
        if e in gate:
            behind.add(gate[e])
        lastw[e] = i
        for r in rd:
            readers.setdefault(r, []).append(i)
        for w in wr:
            lastw[w], readers[w] = i, []
        if sem:
            group.setdefault(sem, []).append(i)
        calls.append({"e": e, "f": f, "deps": deps, "behind": behind - deps, "busy": FIXED[e] + busy, "late": late, "sem": sem, "turn": turn[0]})

    def vec(n, f, rd, wr, ps):
        call("V", f, rd, wr, ps, max(64, n))

    def tt(n, o, a, b, how, rd, wr, ps=()):
        vec(n, lambda q: q.tensor_tensor(o, a, b, how), rd, wr, ps)

    def ts(n, o, a, s1, s2, o1, o2, rd, wr, ps=()):
        if o2 is None:
            vec(n, lambda q: q.tensor_scalar(o, a, s1, None, o1), rd, wr, ps)
        else:
            vec(n, lambda q: q.tensor_scalar(o, a, s1, s2, o1, o2), rd, wr, ps)

    def tc(n, o, a, rd, wr):
        vec(n, lambda q: q.tensor_copy(o, a), rd, wr, ())

    def fill(n, o, v, wr):
        vec(n, lambda q: q.memset(o, v), [], wr, ())

    def scan(n, o, a, b, first, o1, o2, rd, wr, ps=()):
        vec(n, lambda q: q.tensor_tensor_scan(o, a, b, first, o1, o2), rd, wr, ps)

    def quant(n, c, s, t, rd, wr):
        vec(1.06 * n + 14, lambda q: q.quantize_mx(c, s, t), rd, wr, ())

    def act(n, o, i, func, rd, wr, ps=(), **kw):
        call("S", lambda q: q.activation(o, i, func, **kw), rd, wr, ps, n + (24 if "accum_out" in kw else 0))

    def mm(b, n, w, ws, x, xs, rd, start=True, stop=True):
        call("T", lambda q: q.matmul_mx(T.ps[:, 512 * b:512 * b + n], w, ws, x, xs, start, stop), rd, [], [b], 0.6 * n, 30)

    def dma(e, n, out, in_, rd, wr, k):
        moved[0] = n + (0 if rd else moved[0])
        call(e, lambda q: q.dma_start(out, in_), rd, wr, (), 0, LOCAL + moved[0], k)

    def iota(n, o, pattern, base, mult, wr, **kw):
        call("G", lambda q: q.iota(o, pattern, base, mult, **kw), [], wr, (), 2 * n)

    def select(o, i, pattern, how, other, base, mult, rd, wr):
        call("G", lambda q: q.affine_select(o, i, pattern, how, other, base, mult), rd, wr, (), 1024)

    def at(r, name):
        turn[0] = len(TURNS) * (r + 1) + TURNS.index(name)

    def psum(b, lo, hi):
        return T.ps[:, 512 * b + lo:512 * b + hi]

    HALF = [["b%d%d" % (h, b) for b in range(4)] for h in range(2)]
    LI = ["li0", "li1", "li2", "li3"]
    cnt = {"ls": 0}

    for i, nm in enumerate(("la", "lx", "ra", "rx")):
        dma("S", 80, T.li[:, 20 * i:20 * i + 20], T[nm][:, :], [], [LI[i]], "dl")
    dma("Y", 512, T.lr[:, 0:256], T.l0[:, :], [], ["lr0"], "d0")
    dma("Y", 2560, T.xt[:, :], T.x[:, :], [], ["xt"], "dx")
    dma("Y", 512, T.lr[:, 256:512], T.r0[:, :], [], ["lr1"], "d1")

    big = {"allow_small_or_imprecise_dtypes": True}
    iota(1, T.qi[:, 3:4], [[1, 1]], 0, 1, ["qi"])
    iota(8, T.pki[:, 0:8], [[8, 8]], 64, 0, ["pki"])
    iota(8, T.pki[:, 8:16], [[8, 8]], 0, 0, ["pki2"])
    iota(C, T.r16[:, :], [[0, 20], [1, 16]], 0, 0, ["r16"], **big)
    iota(C, T.i4[:, :], [[4, C]], 0, 0, ["i4"], **big)
    iota(C, T.yy[:, :], [[0, 20], [-2 * B, 16]], 0, 0, ["yy"], **big)
    fill(256, T.zz[:, :], 0.0, ["zz"])
    at(0, "rank0")
    select(T.a1[:, :], T.zz[:, :], [[-16, 8], [0, 64]], OP.is_ge, 1.0, -16, 1, ["zz"], ["a1"])
    for h in range(2):
        select(T.aw[:, 512 * h:512 * h + 512], T.a1[:, :], [[-16, 8], [0, 64]], OP.is_ge, 0.0, 0, 1, ["a1"], ["aw%d" % h])
    select(T.a2[:, :], T.zz[:, 0:128], [[-16, 8], [0, 16]], OP.is_ge, -1.0, -16, 1, ["zz"], ["a2"])
    select(T.aw[:, 3:512:4], T.a2[:, :], [[-16, 8], [0, 16]], OP.is_ge, 0.0, 0, 1, ["a2"], ["aw0"])
    quant(256, T.aq[:, :], T.ax[:, :], T.aw[:, :], ["aw0", "aw1"], ["aq"])
    at(0, "tail0")
    iota(C, T.kc[:, :], [[16, 20], [0, 16]], 17 * B, 0, ["kc"], **big)
    iota(A, T.y4[:, :], [[0, 16], [-2 * B, 4]], 0, 0, ["y4"], **big)
    quant(128, T.zc[:, :], T.zp[:, :], T.zz[:, :], ["zz"], ["zc"])
    for f in range(2):
        u = "%d" % f
        for j in range(5):
            a = 4 * (AT[j] + 16 * TILES[j][-1])
            o, wr = T["ut" + u][:, a:4 * AT[j + 1]], ["u%d%d%d" % (f, j, t) for t in range(4)]
            at(0, "rank" + u)
            if f:
                dma("Y", 512, o, T.zz[:, 0:4 * AT[j + 1] - a], ["zz"], wr, "du")
            else:
                fill(2 * AT[j + 1] - a / 2, o, 0.0, wr)
    dma("Y", 2048, T.wq[:, :].bitcast(dt.uint8), T.wc[:, :], [], ["wq"], "dw")
    dma("Y", 512, T.wp[:, :], T.ws[:, :], [], ["wp"], "dw")
    dma("Y", 1024, T.vt[:, :], T.v[:, :], [], ["vt"], "dv")
    dma("Y", 512, T.pl[:, 256:512], T.zz[:, 0:256], ["zz"], ["pz"], "dz")
    dma("Y", 256, T.lc[:, 0:64].bitcast(dt.uint8), T.zc[:, 0:64].bitcast(dt.uint8), ["zc"], ["pad"], "dz")
    dma("Y", 64, T.lp[:, 0:64], T.zp[:, 0:64], ["zc"], ["pae"], "dz")
    for f in range(2):
        u = "%d" % f
        dma("Y", 512, T["ft" + u][:, 0:256], T.zz[:, 0:256], ["zz"], ["fz" + u], "dz")
        fill(1, T["jk" + u][:, C - 1:C], 0.0, ["rk%s0" % u])
    turn[0] = 0
    fill(160, T.rs[:, :], 0.0, ["rs"])
    fill(20, T.rs[:, 0:C:16], BIG, ["rs"])
    ts(1, T.qj[:, 0:1], T.qi[:, 3:4], 15, None, OP.bitwise_and, None, ["qi"], ["qj0"])
    ts(1, T.qj[:, 1:2], T.qi[:, 3:4], 2, 3, OP.logical_shift_right, OP.bitwise_and, ["qi"], ["qj1"])
    ts(1, T.qj[:, 2:3], T.qi[:, 3:4], 3, None, OP.bitwise_and, None, ["qi"], ["qj2"])
    tc(16, T.pk[:, :], T.pki[:, :], ["pki", "pki2"], ["pk"])
    tc(3, T.cf[:, 0:3], T.qj[:, 0:3], ["qj0", "qj1", "qj2"], ["cf0"])
    ts(2, T.cf[:, 3:5], T.qj[:, 0:2], 2.0 * B, None, OP.mult, None, ["qj0", "qj1"], ["cf3"])
    ts(2, T.cf[:, 5:7], T.qj[:, 0:2], -1.0 * B, -2.0 * B, OP.mult, OP.add, ["qj0", "qj1"], ["cf5"])
    ts(1, T.cf[:, 7:8], T.cf[:, 6:7], T.cf[:, 2:3], None, OP.add, None, ["cf0", "cf5"], ["cf7"])
    ts(1, T.cf[:, 5:6], T.cf[:, 5:6], T.cf[:, 0:1], None, OP.add, None, ["cf0", "cf5"], ["cf5"])
    ts(160, T.mb[:, :], T.r16[:, :], T.cf[:, 0:1], BIG, OP.not_equal, OP.mult, ["r16", "cf0"], ["mb"])
    at(0, "tail0")
    act(C, T.yy[:, :], T.yy[:, :], AF.Relu, ["cf3"], ["yy"], bias=T.cf[:, 3:4])
    for f in range(2):
        act(C, T["d1%d" % f][:, :], T.yy[:, :], AF.Identity, ["yy"], ["rx%d" % f, "ry%d" % f], bias=-1.0 * B)
    act(A, T.y4[:, :], T.y4[:, :], AF.Relu, ["cf3"], ["y4"], bias=T.cf[:, 4:5])
    act(A, T.d4[:, :], T.y4[:, :], AF.Identity, ["y4"], ["d4"], bias=-1.0 * B)
    iota(16, T.d4[:, 3:A:4], [[0, 16]], 5 * B, 0, ["d4"], **big)
    at(0, "score1")
    act(256, T.wj[:, :], T.i4[:, 0:256], AF.Copy, ["i4"], ["wj"], scale=2.0 ** -12)
    at(0, "renew0")
    for b in range(4):
        select(T.et[:, 512 * b:512 * b + 512], T.zz[:, :], [[1, 512]], OP.not_equal, 0.5, -b, -4, ["zz"], ["et%d" % b])
    quant(512, T.eq[:, :], T.es[:, :], T.et[:, :], ["et%d" % b for b in range(4)], ["eq"])
    at(0, "parents")
    quant(128, T.vq[:, :], T.vs[:, :], T.vt[:, :], ["vt"], ["vq"])

    turn[0] = 0
    for t in range(4):
        ts(80, T.off[:, 80 * t:80 * t + 80], T.li[:, :], 4.0, float(t), OP.mult, OP.add, LI, ["ot%d" % t])
    act(256, T.bt[:, 256:512], T.lr[:, 256:512], AF.Copy, ["lr1"], HALF[1], scale=0.5)
    for t in range(4):
        act(GATHER * C, T.zl[:, C * t:C * t + C], T.lr[:, 0:256].indirect(T.off[:, 80 * t:80 * t + 20]), AF.Copy, ["lr0", "ot%d" % t], ["zl%d" % t])

    def halves(f, rd):
        for t in range(4):
            act(GATHER * C, T["xg%d" % f][:, t:4 * C:4], T.xt[:, :].indirect(T.off[:, 80 * t + 40 * f + 20:80 * t + 40 * f + 40]), AF.Copy,
                ["xt", "ot%d" % t] + rd, ["xg%d%d" % (f, t)], scale=0.5)
    at(0, "cand1")
    halves(1, [])
    at(0, "score1")
    for f in range(2):
        act(GATHER * C, T["vv%d" % f][:, :], T.wj[:, :].indirect(T.off[:, 40 * f:40 * f + 20]), AF.Copy, ["wj", "ot0"], ["vv%d" % f])
    for f in range(2):
        call("G", lambda q, f=f: q.dma_start(T["vv%d" % f][:, :], T.i4[:, :], accum_op=OP.add), ["i4"], ["vv%d" % f], (), 400, 3000, "dg")

    def move(f, pairs, rd, k, late):
        d = T.cores[(rank + 1 - 2 * f) % N]
        rid, pid = topo.addr(d, core)
        m, ne = topo.mask(core, d), len(topo.engines(core, d))

        def writes(q):
            for o, i in pairs:
                q.remote_dma(o, i, T.sem[k], T.sem.ls, pid, rid, m)
                cnt["ls"] += ne
                cnt[k] = cnt.get(k, 0) + ne
        call("G", writes, rd, [k], (), FIXED["G"] * (len(pairs) - 1), late, k)

    def candidates(f, r):
        u = "%d" % f
        at(r, "cand" + u)
        k = SHARE if r and f else 0
        zt, xg, fam, ZU = T["zt" + u], T["xg" + u], T.bt[:, 256 * f:256 * f + 256], ["zu%d" % t for t in range(4)] if f else []
        for t in range(4):
            o, z = 80 * t + 40 * f, slice(64 * k + t, 4 * C, 4)
            if k:
                act(GATHER * 16 * k, zt[:, t:64 * k:4], fam.indirect(T.off[:, o:o + k]), AF.Copy, HALF[f] + ["ot%d" % t], [ZU[t]])
            if r or f:
                tt(GATHER * (C - 16 * k) + 30, zt[:, z], fam.indirect(T.off[:, o + k:o + 20]), xg[:, z], OP.add, HALF[f] + ["ot%d" % t, "xg%d%d" % (f, t)], ["zt%d%d" % (f, t)])
            else:
                tt(GATHER * C + 30, zt[:, z], T.xt[:, :].indirect(T.off[:, o + 20:o + 40]), T.zl[:, C * t:C * t + C], OP.add, ["xt", "zl%d" % t], ["zt0%d" % t])
        if k:
            call("G", lambda q: q.dma_start(zt[:, 0:64 * k], xg[:, 0:64 * k], accum_op=OP.add), ["xg1%d" % t for t in range(4)], ZU, (), 400, ADDING, "da%d" % r)
        s = slice(C * r, C * r + C)
        quant(C, T["zq" + u][:, s], T["zs" + u][:, s], zt[:, :], ["zt" + u + "%d" % t for t in range(4)] + ZU, ["zq%d%d" % (f, r)])
        if f:
            move(f, [(T.yc[:, s].bitcast(dt.uint8), T.zq1[:, s].bitcast(dt.uint8)), (T.yp[:, s], T.zs1[:, s])], ["zq1%d" % r], "ay%d" % r, WHOLE)

    def slot(f, c, a, b):
        j, t = WHERE[c]
        return T["ut%d" % f][:, 4 * (AT[j] + a) + t:4 * (AT[j] + b):4], ["u%d%d%d" % (f, j, t)]

    def order(f, r):
        u, (kv, ks, kd) = "%d" % f, BANKS[f][:3]
        at(r, "sides")
        s, k = slice(128 * f, 128 * f + 128), T.pk[:, 8 * f:8 * f + 8]
        tc(GATHER * 128, T.st[:, s].bitcast(dt.uint32), T.sq[:, 0:128].bitcast(dt.uint32).indirect(k), ["sq", "pk"], ["st" + u])
        act(GATHER * 128, T.ss[:, s], T.sp[:, 0:128].indirect(k), AF.Copy, ["sq", "pk"], ["ss" + u])
        at(r, "score" + u)
        for b in (kv, ks):
            mm(b, C, T.st[:, s], T.ss[:, s], T["zq" + u][:, C * r:C * r + C], T["zs" + u][:, C * r:C * r + C], ["st" + u, "ss" + u, "zq%d%d" % (f, r)])
        sc, sg, rk = T["sc" + u], T["sg" + u], T["rk" + u]
        cut = 0 if f else 16 * min(ALONE[f])
        for n, lo, hi in (("sc", cut, C), ("sd", 0, cut)):
            if hi > lo:
                tt(hi - lo, T["mk" + u][:, lo:hi], psum(kv, lo, hi), T.mb[:, lo:hi], OP.add, ["mb"], ["m" + n + u], [kv])
                scan(hi - lo, sc[:, lo:hi], T.rs[:, lo:hi], T["mk" + u][:, lo:hi], BIG, OP.add, OP.min, ["rs", "m" + n + u], [n + u])
        at(r, "rank" + u)
        for i, c in enumerate(ALONE[f]):
            act(16 * c, sg[:, C * i:C * i + 16 * c], psum(ks, 0, 16 * c), AF.Sign, ["sc" + u], ["sg%s%d" % (u, c)], [ks],
                bias=sc[:, 16 * c + 15:16 * c + 16], scale=-1.0)
        de, jk, a = T["de" + u], T["jk" + u], SCANS[f] + 1
        tt(C, T["ut" + u][:, 3:4 * C:4], psum(kv, 0, C), sc[:, :], OP.is_gt, ["sc" + u, "sd" + u], ["u%d03" % f], [kv])
        for c in range(19, 0, -1):
            w, sums = 16 * c, "rk%d%d" % (f, c)
            o, n = slot(f, c, 0, w)
            if c in ALONE[f]:
                i = C * ALONE[f].index(c)
                act(w, o, sg[:, i:i + w], AF.Relu, ["sg%s%d" % (u, c)], n + [sums], accum_out=rk[:, c:c + 1])
                continue
            ts(w, o, psum(kv, 0, w), sc[:, w + 15:w + 16], None, OP.is_lt, None, ["sc" + u, "sd" + u], n, [kv])
            if c >= a:
                act(w, jk[:, C * c:C * c + w], o, AF.Copy, n, ["jk%d%d" % (f, c), sums], accum_out=rk[:, c:c + 1])
        for c in range(a - 1, 0, -1):
            o, n = slot(f, c, 0, 16 * c)
            scan(8 * c, jk[:, C * c + C - 16 * c:C * c + C], o, T.zz[:, 0:16 * c], 0.0, OP.add, OP.add, n + ["zz"], ["rk%d%d" % (f, c)])
        scan(C, de[:, :], T.kc[:, :], T["ut" + u][:, 3:4 * C:4], 0.0, OP.max, OP.add, ["kc", "u%d03" % f], ["de" + u])
        tt(40, T["d1" + u][:, 15:16 * a:16], de[:, 15:16 * a:16], jk[:, C - 1:C * a:C], OP.subtract, ["rk%d%d" % (f, c) for c in range(a)] + ["de" + u], ["rx" + u])
        tt(40, T["d1" + u][:, 16 * a + 15:C:16], de[:, 16 * a + 15:C:16], rk[:, a:20], OP.subtract, ["rk%d%d" % (f, c) for c in range(a, 20)] + ["de" + u], ["ry" + u])
        for i, js in enumerate(QUANT):
            s = slice(AT[js[0]], AT[js[-1] + 1])
            quant(s.stop - s.start, T["uq" + u][:, s], T["us" + u][:, s], T["ut" + u][:, 4 * s.start:4 * s.stop],
                  ["u%d%d%d" % (f, j, t) for j in js for t in range(4)], ["uq%s%d" % (u, i)])
            for j in js:
                s = slice(AT[j], AT[j + 1])
                w = slice(128, 256) if j else slice(0, 128)
                mm(kd, WIDE[j], T.aq[:, w], T.ax[:, w], T["uq" + u][:, s], T["us" + u][:, s], ["aq", "uq%s%d" % (u, i)], j == 0, j == 4)

    def survive(f, r):
        u, b = "%d" % f, BANKS[f][2]
        n = "%d%d" % (f, r)
        at(r, "tail" + u)
        scan(C, T["dd" + u][:, :], psum(b, 0, C), T["d1" + u][:, :], 2.0 * B, OP.min, OP.add, ["rx" + u, "ry" + u], ["dd" + u], [b])
        ts(20, T["ro" + u][:, :], T["dd" + u][:, 15:C:16], T.cf[:, 5:6], None, OP.add, None, ["dd" + u, "cf5"], ["ro" + u])
        tc(SCATTER * C, T["inv" + u][:, :].indirect(T["ro" + u][:, 0:20]), T["vv" + u][:, :], ["ro" + u, "vv" + u], ["inv" + u])
        scan(A, T["gn" + u][:, :], T["inv" + u][:, 0:A], T.d4[:, :], 2.0 * B, OP.min, OP.add, ["inv" + u, "d4"], ["gn" + u])
        s = slice(16 * r, 16 * r + 16)
        ts(16, T["of4" + u][:, s], T["gn" + u][:, 3:A:4], T.cf[:, 7:8], None, OP.add, None, ["gn" + u, "cf7"], ["of4" + n])
        if f:
            move(f, [(T.ln[:, s], T.of41[:, s])], ["of4" + n], "ar" + n, LIST)
        else:
            act(GATHER * 256, T.pl[:, 0:256], T.zt0[:, :].indirect(T.of40[:, s]), AF.Copy, ["of4" + n] + ["zt0%d" % t for t in range(4)], ["pl"],
                scale=1.0 if r else 0.5)
            s, v = slice(64 * r + 64, 64 * r + 128), slice(128 * r, 128 * r + 64)
            quant(128, T.pc[:, 128 * r:128 * r + 128], T.pp[:, 128 * r:128 * r + 128], T.pl[:, :], ["pl", "pz"], ["pc" + n])
            move(f, [(T.lc[:, s].bitcast(dt.uint8), T.pc[:, v].bitcast(dt.uint8)), (T.lp[:, s], T.pp[:, v])], ["pc" + n], "ar" + n, REMOTE)
        at(r, "parents" if r < R - 1 else "tail1")
        s4 = slice(8 * r + 4 * f, 8 * r + 4 * f + 4)
        scan(A, T["en" + u][:, :], T["inv" + u][:, 0:A], T["d1" + u][:, 0:A], 2.0 * B, OP.min, OP.add, ["inv" + u, "rx" + u, "ry" + u], ["en" + u])
        act(4, T.ou[:, s4], T["en" + u][:, 15:A:16], AF.Copy, ["en" + u], ["ou" + n], scale=256.0)

    def parents_out(r):
        k, s = "ao%d" % (r // (R - 1)), slice(8 * r, 8 * r + 8)
        tc(8, T.oi[:, s], T.ou[:, s], ["ou0%d" % r, "ou1%d" % r], ["oi%d" % r])
        ts(8, T.oj[:, s], T.oi[:, s], 255, None, OP.bitwise_and, None, ["oi%d" % r], ["oj%d" % r])
        tc(8, T.ox[:, s], T.oj[:, s], ["oj%d" % r], ["ox%d" % r])

        def move(q):
            tr = []
            for f in range(2):
                d = T.cores[(rank + (R - r) * (1 - 2 * f)) % N]
                rid, pid = topo.addr(d, core)
                en = topo.engines(core, d)
                h, s = len(en) // 2, slice(8 * r + 4 * f, 8 * r + 4 * f + 4)
                tr.append(RemoteDMATransfer(dst_ids=[DstId(rid=rid, pnc=pid)], dma_engine_mask=sum(1 << e for e in en[h * f:h * f + h]),
                                            remote_sem=T.sem[k], src=T.ox[:, s], dst=T.on[:, s]))
                cnt["ls"] += h
                cnt[k] = cnt.get(k, 0) + h
            q.remote_dma_fused(tr, local_sem=T.sem.ls)
        call("G", move, ["ox%d" % r, "of41%d" % r], ["on%d" % r], (), 0, LIST, k)

    def parents_in(k):
        for f in range(2):
            u, o = "%d" % f, slice(A * f, A * f + A)
            if k:
                act(GATHER * A, T.of[:, o], T.ob[:, o].indirect(T.on[:, 16 + 4 * f:20 + 4 * f]), AF.Copy, ["on2", "ob" + u], ["of" + u])
            else:
                act(GATHER * A, T.oa[:, o], T.i4[:, 0:A].indirect(T.on[:, 4 * f:4 + 4 * f]), AF.Copy, ["on1", "i4"], ["oa" + u], scale=0.25)
                act(GATHER * A, T.ob[:, o], T.oa[:, o].indirect(T.on[:, 8 + 4 * f:12 + 4 * f]), AF.Identity, ["on1", "oa" + u], ["ob" + u],
                    bias=float(A * ((rank - R + 2 * R * f) % N)))

    W = [slice(128 * b, 128 * b + 128) for b in range(4)]

    def renew_left(r):
        last, x, K = r == R - 1, slice(64 * r, 64 * r + 128), BANKS[0]
        at(r, "renew0")
        FT = ["ft0%d" % b for b in range(4)]

        def unpack(b, start, stop):
            mm(K[b], 128, T.eq[:, W[b]], T.es[:, W[b]], T.lc[:, x], T.lp[:, x], ["ar0%d" % r, "eq", "pad", "pae"], start, stop)
        for b in range(4):
            unpack(b, True, True)
        for b in range(4):
            act(A, T.ft0[:, 256 + b:512:4], psum(K[b], 64, 128), AF.Copy, [], [FT[b]], [K[b]], scale=1.0 / 16 if last else 1.0 / 32)
        quant(128, T.fq0[:, :], T.fs0[:, :], T.ft0[:, :], FT + ["fz0"], ["fq0"])
        act(256, T.fh[:, :], T.ft0[:, 256:512], AF.Copy, FT, ["fh"], scale=32.0)
        for b in range(4):
            unpack(b, True, False)
            if last:
                unpack(b, False, False)
        for b in range(4):
            mm(K[b], 128, T.wq[:, W[b]], T.wp[:, W[b]], T.fq0[:, :], T.fs0[:, :], ["wq", "wp", "fq0"], False, True)
            tt(A, T.bt[:, b:256:4], psum(K[b], 64, 128), T.fh[:, b:256:4], OP.max, ["fh"], ["b0%d" % b], [K[b]])

    def renew_right(r):
        x, K = slice(C * r, C * r + C), [BANKS[1][b] for b in (3, 1, 0, 2)]
        at(r, "unpack")
        for b in range(4):
            mm(K[b], C, T.eq[:, W[b]], T.es[:, W[b]], T.yc[:, x], T.yp[:, x], ["ay%d" % r, "eq"])
            act(C, T.yd[:, b:4 * C:4], psum(K[b], 0, C), AF.Copy, [], ["yd%d" % b], [K[b]], scale=2.0 if r == R - 1 else 1.0)
        at(r, "renew1")
        act(GATHER * 256, T.ft1[:, 256:512], T.yd[:, :].indirect(T.ln[:, 16 * r:16 * r + 16]), AF.Copy, ["ar1%d" % r] + ["yd%d" % b for b in range(4)], ["ft1"])
        quant(128, T.fq1[:, :], T.fs1[:, :], T.ft1[:, :], ["ft1", "fz1"], ["fq1"])
        for b in range(4):
            mm(K[b], 128, T.wq[:, W[b]], T.wp[:, W[b]], T.fq1[:, :], T.fs1[:, :], ["wq", "wp", "fq1"])
            act(A, T.rb[:, A * b:A * b + A], psum(K[b], 64, 128), AF.Relu, [], ["rb%d" % b], [K[b]], scale=0.03125)
            tt(2 * A, T.bt[:, 256 + b:512:4], T.rb[:, A * b:A * b + A], T.ft1[:, 256 + b:512:4], OP.add, ["rb%d" % b, "ft1"], ["b1%d" % b])

    for r in range(R):
        at(r, "sides")
        if r:
            quant(128, T.sq[:, :], T.sp[:, :], T.bt[:, :], HALF[0] + HALF[1], ["sq"])
        else:
            quant(128, T.sq[:, :], T.sp[:, :], T.lr[:, :], ["lr0", "lr1"], ["sq"])
        for f in range(2):
            candidates(f, r)
            order(f, r)
        lastw["sums"] = lastw["T"]
        if r == R - 1:
            at(r, "parents")
            gate.update(S=lastw["sg0%d" % min(ALONE[0])])
            parents_in(0)
            gate.clear()
        for f in range(2):
            survive(f, r)
        if r == 0:
            at(r, "renew0")
            halves(0, ["ry1"])
            at(r, "parents")
        parents_out(r)
        gate.update(T=lastw["sums"], V=lastw["of41%d" % r])
        renew_left(r)
        renew_right(r)
        gate.clear()
    at(R, "sides")
    gate.update(S=lastw["rb3"])
    parents_in(1)
    gate.clear()

    quant(128, T.sq[:, :], T.sp[:, :], T.bt[:, :], HALF[0] + HALF[1], ["sq"])
    dma("Y", 512, T.ot[:, :], T.of[0:128:16, :], ["of0", "of1"], [], "do")
    dma("Y", 512, T.oc[:, :], T.sq[:, :].bitcast(dt.uint8), ["sq"], [], "do")
    mm(0, 128, T.vq[:, :], T.vs[:, :], T.sq[:, :], T.sp[:, :], ["vq", "sq"])
    act(128, T.yo[:, :], psum(0, 0, 128), AF.Copy, [], ["yo"], [0])
    dma("S", 512, T.y[:, :], T.yo[:, :], ["yo"], [], "dy")
    for k in range(4):
        dma("Y", 128, T.osc[4 * k:4 * k + 4, :], T.sp[32 * k:32 * k + 4, :], ["sq"], [], "do")

    seen, snap, token = {e: {} for e in Q}, {}, {}

    def wait(e, k, n):
        if seen[e].get(k, 0) >= n:
            return
        Q[e].wait_ge(T.sem[k], n)
        seen[e][k] = n
        for a, b in snap.get((k, n), {}).items():
            if seen[e].get(a, 0) < b:
                seen[e][a] = b

    for i in arrange(calls):
        c = calls[i]
        e, k, want = c["e"], c["sem"], {}
        for j in c["deps"]:
            a, n = token[j]
            want[a] = max(cnt[a] if calls[j]["sem"] else n, want.get(a, 0))
        for a in sorted(want):
            wait(e, a, want[a])
        done = c["f"](Q[e])
        if k is None or k[0] == "d":
            k, n = k or "s" + e, 16 if k else 1
            cnt[k] = cnt.get(k, 0) + n
            done.then_inc(T.sem[k], n)
        token[i] = (k, cnt[k])
        if k[0] != "a":
            snap[token[i]] = dict(seen[e])
    for k in sorted(cnt):
        wait("G", k, cnt[k])
